import numpy as np
import ml_dtypes


def mxq(x, axis, fmt="e4m3"):
    dtype, down = {"e4m3": (ml_dtypes.float8_e4m3fn, 7), "e5m2": (ml_dtypes.float8_e5m2, 14)}[fmt]
    v = np.moveaxis(np.asarray(x, np.float32).astype(ml_dtypes.bfloat16).astype(np.float64), axis, -1)
    blocks = v.reshape(v.shape[:-1] + (-1, 32))
    amax = np.abs(blocks).max(-1, keepdims=True)
    byte = np.maximum(np.where(amax > 0, np.frexp(amax)[1] - 1 + 127, 0) - down, 1)
    scale = np.exp2(byte - 127.0)
    codes = (blocks / scale).astype(np.float32).astype(dtype).astype(np.float64)
    return np.moveaxis((codes * scale).reshape(v.shape), -1, axis)


WIDE = False


def mx_kscale(k):
    if not WIDE:
        return np.ones(k)
    levels = np.array([24, -24, 12, -12, 0])
    if k % 512:
        return np.exp2(np.random.permutation(np.resize(levels, k // 32))).repeat(32)
    a = np.empty((k // 512, 16))
    for p in range(k // 512):
        a[p, :8] = np.random.permutation(np.resize(levels, 8))
        for g in range(8):
            far = levels[np.abs(levels - a[p, g]) >= 10]
            a[p, g + 8] = far[np.random.randint(len(far))]
    return np.exp2(a.ravel()).repeat(32)


def f64(x):
    return np.asarray(x).astype(np.float64)


def striped(idx):
    return np.tile(idx.reshape(-1, 16).T, (8, 1)).astype(np.uint16)


def unstriped(offs):
    return offs[:16].T.reshape(-1).astype(np.int64)


E2M1 = np.array([0.0, 0.5, 1.0, 1.5, 2.0, 3.0, 4.0, 6.0, -0.0, -0.5, -1.0, -1.5, -2.0, -3.0, -4.0, -6.0])


def pack_weight(w, fmt):
    k, n = w.shape
    w = f64(np.asarray(w, np.float32).astype(ml_dtypes.bfloat16)).reshape(k // 32, 32, n)
    amax = np.abs(w).max(1)
    if fmt == "e4m3":
        byte = np.frexp(amax)[1] - 1 + 127 - 7
    else:
        mant, ex = np.frexp(amax / 6.0)
        byte = np.where(mant > 0.5, ex, ex - 1) + 127
    byte = np.clip(np.where(amax > 0, byte, 1), 1, 254)
    scaled = (w * np.exp2(127.0 - byte)[:, None, :]).reshape(k, n).astype(np.float32)
    by_word = np.ascontiguousarray(scaled.reshape(k // 512, 128, 4, n).transpose(0, 1, 3, 2))
    if fmt == "e4m3":
        words = by_word.astype(ml_dtypes.float8_e4m3fn).view(np.uint8)
    else:
        c = by_word.astype(ml_dtypes.float4_e2m1fn).view(np.uint8) & 0xF
        words = (c[..., 0::2] | (c[..., 1::2] << 4)).reshape(k // 512, 128, 2 * n)
    return np.ascontiguousarray(words), np.ascontiguousarray(byte.astype(np.uint8).reshape(k // 512, 16, n))


def unpack_weight(words, scales, fmt):
    g, _, n = scales.shape
    words = np.ascontiguousarray(words).reshape(g, 128, n, -1)
    if fmt == "e4m3":
        vals = words.view(ml_dtypes.float8_e4m3fn).astype(np.float64)
    else:
        nib = np.empty((g, 128, n, 4), np.uint8)
        nib[..., 0::2] = words & 0xF
        nib[..., 1::2] = words >> 4
        vals = E2M1[nib]
    vals = vals * np.repeat(np.exp2(scales.astype(np.float64) - 127.0), 8, axis=1)[..., None]
    return vals.transpose(0, 1, 3, 2).reshape(g * 512, n)


def pack_table4(v):
    words, scales = pack_weight(v, "e2m1")
    g, t = words.shape[0] // 2, v.shape[1]
    return np.ascontiguousarray(words.reshape(g, 2, 128, t, 2).transpose(0, 2, 3, 1, 4).reshape(g, 128, t, 4)), scales


def unpack_table4(words, scales):
    g, _, t, _ = words.shape
    return unpack_weight(words.reshape(g, 128, t, 2, 2).transpose(0, 3, 1, 2, 4).reshape(2 * g, 128, 2 * t), scales, "e2m1")


K, R, N, T, J = 1024, 1024, 512, 2048, 1024


def setup_inputs():
    n = np.random.standard_normal
    s = mx_kscale(K)[:, None]
    u = mx_kscale(R)[:, None]
    wd = n((R, N)) / np.sqrt(R) / u
    wd4 = pack_weight(wd, "e2m1")
    wdrest = wd - unpack_weight(*wd4, "e2m1")
    p_tab = pack_table4(n((K, T)) * s)
    p_ws = pack_weight(n((K, R)) / np.sqrt(2 * K) / s, "e4m3")
    p_wd8 = pack_weight(wdrest, "e4m3")
    return {
        "tab_words": p_tab[0],
        "tab_scales": p_tab[1],
        "ws_words": p_ws[0],
        "ws_scales": p_ws[1],
        "wt": (n((K, R)) / np.sqrt(2 * K) / s).astype(np.float32),
        "sm": (np.random.uniform(0.5, 2.0, R) * u[:, 0]).astype(np.float32),
        "wd4_words": wd4[0],
        "wd4_scales": wd4[1],
        "wd8_words": p_wd8[0],
        "wd8_scales": p_wd8[1],
        "b": (0.3 * n(N)).astype(np.float32),
        "wgo": np.tile(np.random.uniform(0.5, 2.0, J), (128, 1)).astype(np.float32),
        "offs": striped(np.random.permutation(T)[:J]),
        "offs2": striped(np.random.permutation(T)[:J]),
    }


def reference(tab_words, tab_scales, ws_words, ws_scales, wt, sm, wd4_words, wd4_scales, wd8_words, wd8_scales, b, wgo, offs, offs2):
    idx = unstriped(offs)
    idx2 = unstriped(offs2)
    tab_ = unpack_table4(tab_words, tab_scales)[:, idx]
    tabb_ = unpack_table4(tab_words, tab_scales)[:, idx2]
    ws_ = unpack_weight(ws_words, ws_scales, "e4m3")
    wt_ = mxq(f64(wt), 0, "e4m3")
    a = ws_.T @ tab_ + wt_.T @ tabb_
    h = f64(sm)[:, None] * np.tanh(a)
    h_ = mxq(h, 0, "e4m3")
    wd4_ = unpack_weight(wd4_words, wd4_scales, "e2m1")
    wd8_ = unpack_weight(wd8_words, wd8_scales, "e4m3")
    y = wd4_.T @ h_ + wd8_.T @ h_
    out = np.zeros((N, T))
    out[:, idx2] = f64(wgo)[0] * (y + f64(b)[:, None])
    return out

@@ -1,0 +1,316 @@
+from contextlib import ExitStack
+
+import concourse.mybir as mybir
+
+K, R, N, T, J = 1024, 1024, 512, 2048, 1024
+FLOPS = 2 * (2 * K * R * J + 2 * R * N * J)
+
+F32 = mybir.dt.float32
+BF16 = mybir.dt.bfloat16
+I32 = mybir.dt.int32
+U32 = mybir.dt.uint32
+U16 = mybir.dt.uint16
+U8 = mybir.dt.uint8
+FP8X4 = mybir.dt.float8_e4m3fn_x4
+FP4X4 = mybir.dt.float4_e2m1fn_x4
+ACT = mybir.ActivationFunctionType
+MULT = mybir.AluOpType.mult
+
+P = 128
+CH = 256
+NCH = J // CH
+HALF = 512
+LOW = 24
+ON_VECTOR = {(0, 0, 0), (0, 0, 1), (0, 1, 0), (0, 1, 1), (1, 0, 0), (2, 0, 0), (3, 0, 0)}
+ON_GPSIMD = set()
+RUNS = ((0, 256), (256, 512), (512, 1024))
+HOLD_ON = (None, (24576, 26624), (28672, 30720))
+HELD = (3, 3, 3)
+
+
+def tile_list_msg_tanh_res_bias_kernel(
+    tc, tab_words, tab_scales, ws_words, ws_scales, wt, sm, wd4_words, wd4_scales, wd8_words, wd8_scales, b, wgo, offs, offs2, out
+):
+    nc = tc.nc
+    with ExitStack() as ctx:
+        keep = ctx.enter_context(tc.tile_pool(name="keep", bufs=1))
+        ring = ctx.enter_context(tc.tile_pool(name="ring", bufs=2))
+        placed = ctx.enter_context(tc.tile_pool(name="placed", bufs=1))
+        ps1 = ctx.enter_context(tc.psum_pool(name="ps1", bufs=6))
+        ps2 = ctx.enter_context(tc.psum_pool(name="ps2", bufs=2))
+
+        lists = [keep.tile([P, J // 16], U16, name="offs_a"), keep.tile([P, J // 16], U16, name="offs_b")]
+        tab_w = keep.tile([P, T], I32, name="tab_w", align_bytes=64)
+        tab_s = keep.tile([P, T], U8, name="tab_s", align_bytes=64)
+        ws_s_raw = keep.tile([P, 2, R], U8, name="ws_s_raw", align_bytes=64)
+        wd4_s = keep.tile([P, 2, N], U8, name="wd4_s", align_bytes=64)
+        wd8_s = keep.tile([P, 2, N], U8, name="wd8_s", align_bytes=64)
+        tab_plane = [keep.tile([P, J], U8, name="tab_plane%d" % i, align_bytes=64) for i in range(4)]
+        windows = [keep.tile([P, T], F32, name="window%d" % c, align_bytes=64) for c in range(2)]
+        warm = keep.tile([P, 1], F32, name="warm")
+        warm2 = keep.tile([P, 1], F32, name="warm2")
+
+        for q in range(4):
+            nc.vector.memset(tab_s[32 * q : 32 * q + LOW, :].bitcast(I32), 0)
+        nc.gpsimd.memset(ws_s_raw[:].rearrange("p a r -> p (a r)").bitcast(I32), 0)
+        nc.gpsimd.memset(warm[:], 0.0)
+        nc.scalar.activation(out=warm2[:], in_=warm[:], func=ACT.Tanh)
+        nc.gpsimd.memset(wd4_s[:].rearrange("p a r -> p (a r)").bitcast(I32), 0)
+        nc.gpsimd.memset(wd8_s[:].rearrange("p a r -> p (a r)").bitcast(I32), 0)
+        for plane in tab_plane:
+            nc.gpsimd.memset(plane[96:128, :].bitcast(I32), 0)
+
+        def load_rows(dst, src):
+            for q in range(4):
+                nc.sync.dma_start(out=dst[32 * q + LOW : 32 * q + 32, :].bitcast(I32), in_=src[:, 4 * q : 4 * q + 4, :].bitcast(I32))
+
+        def lower(dst, src, a):
+            nc.gpsimd.dma_start(out=dst[0:100, :].bitcast(I32), in_=src[LOW + 4 * a : LOW + 4 * a + 100, :].bitcast(I32))
+
+        wt_raw = {}
+        ws_raw = {}
+
+        def load_wt(a, blk):
+            raw = keep.tile([P, 4, HALF], F32, name="wt_raw%d%d" % (a, blk))
+            nc.sync.dma_start(out=raw[:], in_=wt[512 * a : 512 * (a + 1), HALF * blk : HALF * (blk + 1)].rearrange("(p i) r -> p i r", i=4))
+            wt_raw[a, blk] = raw
+
+        def load_ws(blk):
+            raw = keep.tile([P, 2, HALF], I32, name="ws_raw%d" % blk)
+            src = ws_words.rearrange("a p r i -> p a (r i)")[:, :, 4 * HALF * blk : 4 * HALF * (blk + 1)]
+            nc.sync.dma_start(out=raw[:], in_=src.bitcast(I32))
+            ws_raw[blk] = raw
+
+        nc.sync.dma_start(lists[0][:], offs)
+        load_rows(tab_s, tab_scales)
+        nc.sync.dma_start(lists[1][:], offs2)
+        nc.sync.dma_start(out=tab_w[:], in_=tab_words[0].rearrange("p t d -> p (t d)").bitcast(I32))
+        load_wt(0, 0)
+        for q in range(4):
+            nc.sync.dma_start(
+                out=ws_s_raw[32 * q : 32 * q + 4, :, :].bitcast(I32),
+                in_=ws_scales[:, 4 * q : 4 * q + 4, :].rearrange("a q r -> q a r").bitcast(I32),
+            )
+        load_wt(1, 0)
+        load_ws(0)
+        load_wt(0, 1)
+        load_wt(1, 1)
+        load_ws(1)
+        sm_t = keep.tile([P, 2, 4], F32, name="sm_t")
+        b_t = keep.tile([P, 4], F32, name="b_t")
+        wd8_w = keep.tile([P, 2, N], I32, name="wd8_w", align_bytes=64)
+        wd4_w = keep.tile([P, 2, 2 * N], U8, name="wd4_w", align_bytes=64)
+        wgo_t = keep.tile([P, J], F32, name="wgo_t")
+        nc.sync.dma_start(out=sm_t[:], in_=sm.rearrange("(g p t) -> p g t", g=2, t=4))
+        nc.sync.dma_start(out=wd8_w[:], in_=wd8_words.rearrange("a p n i -> p a (n i)").bitcast(I32))
+        nc.sync.dma_start(out=wd4_w[:].bitcast(I32), in_=wd4_words.rearrange("a p n -> p a n").bitcast(I32))
+        with nc.allow_non_contiguous_dma(reason="one bias value to a partition"):
+            nc.sync.dma_start(out=b_t[:], in_=b.rearrange("(c p) -> p c", p=P))
+        nc.sync.dma_start(out=wgo_t[:], in_=wgo)
+
+        for i in (1, 0):
+            g = keep.tile([P, J], U8, name="picked_s%d" % i, align_bytes=64)
+            nc.vector.tensor_copy(g[:], tab_s[:].indirect(lists[i][:]))
+            for a in range(2):
+                lower(tab_plane[2 * i + a], g, a)
+        ws_s = keep.tile([P, 2, R], U8, name="ws_s", align_bytes=64)
+        nc.vector.tensor_copy(
+            out=ws_s[:].rearrange("p a (g t mq mm) -> p (a g) mq t mm", g=2, t=4, mm=16),
+            in_=ws_s_raw[:].rearrange("p a (g mq mm t) -> p (a g) mq t mm", g=2, t=4, mm=16),
+        )
+        for dst, src in ((wd8_s, wd8_scales), (wd4_s, wd4_scales)):
+            for q in range(4):
+                nc.gpsimd.dma_start(
+                    out=dst[32 * q : 32 * q + 4, :, :].bitcast(I32),
+                    in_=src[:, 4 * q : 4 * q + 4, :].rearrange("a q n -> q a n").bitcast(I32),
+                )
+        for c in range(len(windows)):
+            nc.gpsimd.memset(windows[c][:], 0.0)
+
+        parted = {}
+
+        def gather_words(run):
+            lo, hi = RUNS[run]
+            gs = []
+            for i in range(2):
+                if run == 0:
+                    g = keep.tile([P, hi - lo], U32, name="picked_w%d" % i)
+                else:
+                    g = placed.tile([P, hi - lo], U32, name="picked_w%d%d" % (run, i), align_bytes=64, offset=HOLD_ON[run][i])
+                nc.vector.tensor_copy(g[:], tab_w[:].bitcast(U32).indirect(lists[i][:, lo // 16 : hi // 16]))
+                gs.append(g)
+            for i in range(2):
+                pt = keep.tile([P, 2, 2 * (hi - lo)], U8, name="parted%d%d" % (i, run), align_bytes=64)
+                nc.vector.tensor_copy(out=pt[:].bitcast(U16), in_=gs[i][:].bitcast(U16).rearrange("p (n d) -> p d n", d=2))
+                for tok in range(lo, hi, P):
+                    parted[i, tok] = (pt, tok - lo)
+
+        wt_c = {}
+        wt_s = {}
+        ws_c = {}
+
+        def prepare_wt(a, blk):
+            grouped = placed.tile([P, 4, P, 4], BF16, name="wt_bf%d%d" % (a, blk), align_bytes=64, offset=24576 + 4096 * (2 * blk + a))
+            dst = grouped[:].rearrange("p t m i -> p m i t")
+            src = wt_raw[a, blk][:].rearrange("p i (m t) -> p m i t", t=4)
+            cut = 128 if (a, blk) == (1, 1) else P
+            nc.scalar.copy(out=dst[:, 0:cut], in_=src[:, 0:cut])
+            if cut < P:
+                nc.vector.tensor_copy(out=dst[:, cut:P], in_=src[:, cut:P])
+            codes = keep.tile([P, HALF], U32, name="wt_c%d%d" % (a, blk), align_bytes=64)
+            scales = keep.tile([P, HALF], U8, name="wt_s%d%d" % (a, blk), align_bytes=64)
+            nc.vector.quantize_mx(out=codes[:].bitcast(FP8X4), scales=scales[:], in_=grouped[:].rearrange("p t m i -> p (t m i)"))
+            wt_c[a, blk] = codes
+            wt_s[a, blk] = scales
+
+        def prepare_ws(blk):
+            perm = keep.tile([P, 2, HALF], I32, name="ws_c%d" % blk, align_bytes=64)
+            nc.vector.tensor_copy(
+                out=perm[:].rearrange("p a (t mq mm) -> p a mq t mm", t=4, mm=4),
+                in_=ws_raw[blk][:].rearrange("p a (mq mm t) -> p a mq t mm", t=4, mm=4),
+            )
+            ws_c[blk] = perm
+
+        h_c = {}
+        h_s = {}
+
+        sums = {}
+
+        def sums1(ch, blk):
+            for s in range(2):
+                tok = ch * CH + s * P
+                acc = ps1.tile([P, 4, P], F32, name="acc1", tag="acc1")
+                sums[ch, blk, s] = acc
+                passes = [(i, a, t) for i in (1, 0) for a in range(2) for t in range(4)]
+                for n, (i, a, t) in enumerate(passes):
+                    cols = slice(P * t, P * (t + 1))
+                    if i == 1:
+                        wc, wsc = wt_c[a, blk][:, cols], wt_s[a, blk][:, cols]
+                    else:
+                        wc, wsc = ws_c[blk][:, a, cols], ws_s[:, a, HALF * blk + P * t : HALF * blk + P * (t + 1)]
+                    pt, loc = parted[i, tok]
+                    nc.tensor.matmul_mx(
+                        out=acc[:, t, :],
+                        lhsT=wc.bitcast(FP8X4),
+                        lhsT_scale=wsc,
+                        rhs=pt[:, a, 2 * loc : 2 * (loc + P)].bitcast(FP4X4),
+                        rhs_scale=tab_plane[2 * i + a][:, tok : tok + P],
+                        start=(n == 0),
+                        stop=(n == len(passes) - 1),
+                    )
+
+        def stage1(ch, blk):
+            if (ch, blk, 0) not in sums:
+                sums1(ch, blk)
+            th = ring.tile([P, 2, 4 * P], F32, name="th", tag="th", bufs=3)
+            if ch == 0:
+                hb = placed.tile([P, CH, 4], BF16, name="hb0%d" % blk, align_bytes=64, offset=8192 * blk)
+            else:
+                hb = ring.tile([P, CH, 4], BF16, name="hb", tag="hb", bufs=3, align_bytes=64)
+            on_s = [s for s in range(2) if (ch, blk, s) not in ON_VECTOR and (ch, blk, s) not in ON_GPSIMD]
+            for s in range(2):
+                acc = sums[ch, blk, s]
+                if s in on_s:
+                    nc.scalar.activation(out=th[:, s, :], in_=acc[:].rearrange("p t n -> p (t n)"), func=ACT.Tanh)
+                else:
+                    nc.scalar.activation(
+                        out=th[:, s, :].rearrange("p (n t) -> p n t", t=4),
+                        in_=acc[:].rearrange("p t n -> p n t"),
+                        func=ACT.Tanh,
+                    )
+                    engine = nc.vector if (ch, blk, s) in ON_VECTOR else nc.gpsimd
+                    engine.tensor_tensor(
+                        out=hb[:, P * s : P * (s + 1), :],
+                        in0=th[:, s, :].rearrange("p (n t) -> p n t", t=4),
+                        in1=sm_t[:, blk, :].unsqueeze(1).to_broadcast([P, P, 4]),
+                        op=MULT,
+                    )
+            if on_s:
+                s0, s1 = on_s[0], on_s[-1] + 1
+                if blk == 1 and ch > 0:
+                    hp = placed.tile([P, 4, CH], BF16, name="hp%d1" % ch, align_bytes=64, offset=16384 + 2048 * (ch - 1))
+                else:
+                    hp = ring.tile([P, 4, CH], BF16, name="hp", tag="hp")
+                for t in range(4):
+                    nc.scalar.activation(
+                        out=hp[:, t, P * s0 : P * s1].rearrange("p (s n) -> p s n", n=P),
+                        in_=th[:, s0:s1, P * t : P * (t + 1)],
+                        func=ACT.Copy,
+                        scale=sm_t[:, blk, t : t + 1],
+                    )
+                nc.scalar.copy(
+                    out=hb[:, P * s0 : P * s1, :].rearrange("p (c i) t -> p c t i", i=4),
+                    in_=hp[:, :, P * s0 : P * s1].rearrange("p t (c i) -> p c t i", i=4),
+                )
+            codes = keep.tile([P, CH], U32, name="h_c%d%d" % (ch, blk), align_bytes=64)
+            scales = keep.tile([P, CH], U8, name="h_s%d%d" % (ch, blk), align_bytes=64)
+            nc.vector.quantize_mx(out=codes[:].bitcast(FP8X4), scales=scales[:], in_=hb[:].rearrange("p n t -> p (n t)"))
+            h_c[ch, blk] = codes
+            h_s[ch, blk] = scales
+
+        def stage2(ch):
+            accs = []
+            for c in range(4):
+                acc = ps2.tile([P, CH], F32, name="acc2", tag="acc2")
+                accs.append(acc)
+                for a in (1, 0):
+                    nc.tensor.matmul_mx(
+                        out=acc[:],
+                        lhsT=wd8_w[:, a, P * c : P * (c + 1)].bitcast(FP8X4),
+                        lhsT_scale=wd8_s[:, a, P * c : P * (c + 1)],
+                        rhs=h_c[ch, a][:].bitcast(FP8X4),
+                        rhs_scale=h_s[ch, a][:],
+                        start=(a == 1),
+                        stop=False,
+                    )
+                    for s in range(CH // P):
+                        cols = slice(P * s, P * (s + 1))
+                        nc.tensor.matmul_mx(
+                            out=acc[:, cols],
+                            lhsT=wd4_w[:, a, 2 * P * c : 2 * P * (c + 1)].bitcast(FP4X4),
+                            lhsT_scale=wd4_s[:, a, P * c : P * (c + 1)],
+                            rhs=h_c[ch, a][:, cols].bitcast(FP8X4),
+                            rhs_scale=h_s[ch, a][:, cols],
+                            start=False,
+                            stop=(a == 0 and s == CH // P - 1),
+                        )
+            return accs
+
+        def emit(ch, c, acc):
+            if ch < NCH - 1 and c == HELD[ch]:
+                y = placed.tile([P, CH], F32, name="y%d3" % ch, align_bytes=64, offset=16384 + 2048 * ch)
+            else:
+                y = ring.tile([P, CH], F32, name="y", tag="y", bufs=6)
+            nc.scalar.activation(out=y[:], in_=acc[:], func=ACT.Identity, bias=b_t[:, c : c + 1])
+            nc.vector.tensor_tensor(
+                windows[c][:].indirect(lists[1][:, 16 * ch : 16 * (ch + 1)]), y[:], wgo_t[:, CH * ch : CH * (ch + 1)], MULT
+            )
+            if ch == NCH - 1:
+                nc.sync.dma_start(out=out[P * c : P * (c + 1), :], in_=windows[c][:])
+
+        gather_words(0)
+        prepare_wt(0, 0)
+        prepare_wt(1, 0)
+        prepare_ws(0)
+        gather_words(1)
+        prepare_wt(0, 1)
+        prepare_wt(1, 1)
+        prepare_ws(1)
+        stage1(0, 0)
+        sums1(1, 0)
+        stage1(0, 1)
+        gather_words(2)
+        for c in range(len(windows), 4):
+            w = placed.tile([P, T], F32, name="window%d" % c, align_bytes=64, offset=8192 * (c - 2))
+            nc.gpsimd.memset(w[:], 0.0)
+            windows.append(w)
+        for ch in range(NCH):
+            accs = stage2(ch)
+            held = HELD[ch] if ch < NCH - 1 else 4
+            for c in range(held):
+                emit(ch, c, accs[c])
+            if ch + 1 < NCH:
+                stage1(ch + 1, 0)
+                stage1(ch + 1, 1)
+            for c in range(held, 4):
+                emit(ch, c, accs[c])

@@ -21,7 +21,7 @@ CH = 256
 NCH = J // CH
 HALF = 512
 LOW = 24
-ON_VECTOR = {(0, 0, 0), (0, 0, 1), (0, 1, 0), (0, 1, 1), (1, 0, 0), (2, 0, 0), (3, 0, 0)}
+ON_VECTOR = {(0, 0, 0), (0, 0, 1), (0, 1, 0), (0, 1, 1), (2, 0, 0), (3, 0, 0)}
 ON_GPSIMD = set()
 RUNS = ((0, 256), (256, 512), (512, 1024))
 HOLD_ON = (None, (24576, 26624), (28672, 30720))
@@ -43,29 +43,29 @@ def tile_list_msg_tanh_res_bias_kernel(
         tab_w = keep.tile([P, T], I32, name="tab_w", align_bytes=64)
         tab_s = keep.tile([P, T], U8, name="tab_s", align_bytes=64)
         ws_s_raw = keep.tile([P, 2, R], U8, name="ws_s_raw", align_bytes=64)
-        wd4_s = keep.tile([P, 2, N], U8, name="wd4_s", align_bytes=64)
-        wd8_s = keep.tile([P, 2, N], U8, name="wd8_s", align_bytes=64)
-        tab_plane = [keep.tile([P, J], U8, name="tab_plane%d" % i, align_bytes=64) for i in range(4)]
-        windows = [keep.tile([P, T], F32, name="window%d" % c, align_bytes=64) for c in range(2)]
+        wd_s = keep.tile([P, 4 * N], U8, name="wd_s", align_bytes=64)
+        wd8_s = wd_s[:, 0 : 2 * N].rearrange("p (a n) -> p a n", a=2)
+        wd4_s = wd_s[:, 2 * N : 4 * N].rearrange("p (a n) -> p a n", a=2)
+        planes = keep.tile([P, 4 * J], U8, name="tab_plane", align_bytes=64)
+        tab_plane = [planes[:, J * i : J * (i + 1)] for i in range(4)]
+        windows = [keep.tile([P, T], F32, name="window%d" % c, align_bytes=64) for c in range(3)]
         warm = keep.tile([P, 1], F32, name="warm")
         warm2 = keep.tile([P, 1], F32, name="warm2")
 
         for q in range(4):
             nc.vector.memset(tab_s[32 * q : 32 * q + LOW, :].bitcast(I32), 0)
-        nc.gpsimd.memset(ws_s_raw[:].rearrange("p a r -> p (a r)").bitcast(I32), 0)
-        nc.gpsimd.memset(warm[:], 0.0)
+        nc.vector.memset(ws_s_raw[:].rearrange("p a r -> p (a r)").bitcast(I32), 0)
+        nc.vector.memset(warm[:], 0.0)
         nc.scalar.activation(out=warm2[:], in_=warm[:], func=ACT.Tanh)
-        nc.gpsimd.memset(wd4_s[:].rearrange("p a r -> p (a r)").bitcast(I32), 0)
-        nc.gpsimd.memset(wd8_s[:].rearrange("p a r -> p (a r)").bitcast(I32), 0)
-        for plane in tab_plane:
-            nc.gpsimd.memset(plane[96:128, :].bitcast(I32), 0)
+        nc.vector.memset(wd_s[:].bitcast(I32), 0)
+        nc.vector.memset(planes[96:128, :].bitcast(I32), 0)
 
         def load_rows(dst, src):
             for q in range(4):
                 nc.sync.dma_start(out=dst[32 * q + LOW : 32 * q + 32, :].bitcast(I32), in_=src[:, 4 * q : 4 * q + 4, :].bitcast(I32))
 
         def lower(dst, src, a):
-            nc.gpsimd.dma_start(out=dst[0:100, :].bitcast(I32), in_=src[LOW + 4 * a : LOW + 4 * a + 100, :].bitcast(I32))
+            nc.sync.dma_start(out=dst[0:100, :].bitcast(I32), in_=src[LOW + 4 * a : LOW + 4 * a + 100, :].bitcast(I32))
 
         wt_raw = {}
         ws_raw = {}
@@ -93,6 +93,11 @@ def tile_list_msg_tanh_res_bias_kernel(
             )
         load_wt(1, 0)
         load_ws(0)
+        for i in (1, 0):
+            g = keep.tile([P, J], U8, name="picked_s%d" % i, align_bytes=64)
+            nc.vector.tensor_copy(g[:], tab_s[:].indirect(lists[i][:]))
+            for a in range(2):
+                lower(tab_plane[2 * i + a], g, a)
         load_wt(0, 1)
         load_wt(1, 1)
         load_ws(1)
@@ -104,28 +109,23 @@ def tile_list_msg_tanh_res_bias_kernel(
         nc.sync.dma_start(out=sm_t[:], in_=sm.rearrange("(g p t) -> p g t", g=2, t=4))
         nc.sync.dma_start(out=wd8_w[:], in_=wd8_words.rearrange("a p n i -> p a (n i)").bitcast(I32))
         nc.sync.dma_start(out=wd4_w[:].bitcast(I32), in_=wd4_words.rearrange("a p n -> p a n").bitcast(I32))
+        nc.sync.dma_start(out=wgo_t[:], in_=wgo)
+        for dst, src in ((wd8_s, wd8_scales), (wd4_s, wd4_scales)):
+            for q in range(4):
+                nc.sync.dma_start(
+                    out=dst[32 * q : 32 * q + 4, :, :].bitcast(I32),
+                    in_=src[:, 4 * q : 4 * q + 4, :].rearrange("a q n -> q a n").bitcast(I32),
+                )
         with nc.allow_non_contiguous_dma(reason="one bias value to a partition"):
             nc.sync.dma_start(out=b_t[:], in_=b.rearrange("(c p) -> p c", p=P))
-        nc.sync.dma_start(out=wgo_t[:], in_=wgo)
 
-        for i in (1, 0):
-            g = keep.tile([P, J], U8, name="picked_s%d" % i, align_bytes=64)
-            nc.vector.tensor_copy(g[:], tab_s[:].indirect(lists[i][:]))
-            for a in range(2):
-                lower(tab_plane[2 * i + a], g, a)
         ws_s = keep.tile([P, 2, R], U8, name="ws_s", align_bytes=64)
         nc.vector.tensor_copy(
             out=ws_s[:].rearrange("p a (g t mq mm) -> p (a g) mq t mm", g=2, t=4, mm=16),
             in_=ws_s_raw[:].rearrange("p a (g mq mm t) -> p (a g) mq t mm", g=2, t=4, mm=16),
         )
-        for dst, src in ((wd8_s, wd8_scales), (wd4_s, wd4_scales)):
-            for q in range(4):
-                nc.gpsimd.dma_start(
-                    out=dst[32 * q : 32 * q + 4, :, :].bitcast(I32),
-                    in_=src[:, 4 * q : 4 * q + 4, :].rearrange("a q n -> q a n").bitcast(I32),
-                )
         for c in range(len(windows)):
-            nc.gpsimd.memset(windows[c][:], 0.0)
+            nc.vector.memset(windows[c][:], 0.0)
 
         parted = {}
 
@@ -151,8 +151,8 @@ def tile_list_msg_tanh_res_bias_kernel(
 
         def prepare_wt(a, blk):
             grouped = placed.tile([P, 4, P, 4], BF16, name="wt_bf%d%d" % (a, blk), align_bytes=64, offset=24576 + 4096 * (2 * blk + a))
-            dst = grouped[:].rearrange("p t m i -> p m i t")
-            src = wt_raw[a, blk][:].rearrange("p i (m t) -> p m i t", t=4)
+            dst = grouped[:].rearrange("p t m i -> p m t i")
+            src = wt_raw[a, blk][:].rearrange("p i (m t) -> p m t i", t=4)
             cut = 128 if (a, blk) == (1, 1) else P
             nc.scalar.copy(out=dst[:, 0:cut], in_=src[:, 0:cut])
             if cut < P:
@@ -239,8 +239,8 @@ def tile_list_msg_tanh_res_bias_kernel(
                         scale=sm_t[:, blk, t : t + 1],
                     )
                 nc.scalar.copy(
-                    out=hb[:, P * s0 : P * s1, :].rearrange("p (c i) t -> p c t i", i=4),
-                    in_=hp[:, :, P * s0 : P * s1].rearrange("p t (c i) -> p c t i", i=4),
+                    out=hb[:, P * s0 : P * s1, :],
+                    in_=hp[:, :, P * s0 : P * s1].rearrange("p t n -> p n t"),
                 )
             codes = keep.tile([P, CH], U32, name="h_c%d%d" % (ch, blk), align_bytes=64)
             scales = keep.tile([P, CH], U8, name="h_s%d%d" % (ch, blk), align_bytes=64)
@@ -302,7 +302,7 @@ def tile_list_msg_tanh_res_bias_kernel(
         gather_words(2)
         for c in range(len(windows), 4):
             w = placed.tile([P, T], F32, name="window%d" % c, align_bytes=64, offset=8192 * (c - 2))
-            nc.gpsimd.memset(w[:], 0.0)
+            nc.vector.memset(w[:], 0.0)
             windows.append(w)
         for ch in range(NCH):
             accs = stage2(ch)

@@ -17,15 +17,29 @@ ACT = mybir.ActivationFunctionType
 MULT = mybir.AluOpType.mult
 
 P = 128
-CH = 256
-NCH = J // CH
-HALF = 512
-LOW = 24
-ON_VECTOR = {(0, 0, 0), (0, 0, 1), (0, 1, 0), (0, 1, 1), (2, 0, 0), (3, 0, 0)}
-ON_GPSIMD = set()
-RUNS = ((0, 256), (256, 512), (512, 1024))
-HOLD_ON = (None, (24576, 26624), (28672, 30720))
-HELD = (3, 3, 3)
+PACK = 4
+PASS = P * PACK
+QUADS = 4
+CHUNK = 256
+CHUNKS = J // CHUNK
+GROUPS = CHUNK // P
+TILES = N // P
+SOURCE, TARGET = 0, 1
+
+ROW0 = 24
+PLANE_ROWS = 100
+PAD = 4
+
+ON_VECTOR = {(0, half, group) for half in range(2) for group in range(GROUPS)} | {(CHUNKS - 1, 0, 0)}
+
+KEPT_BACK = (1, 2, 2)
+
+SLOT = 4096
+AT_WT_BF16 = 0
+AT_SCALED = 4 * SLOT
+AT_FIRST_H = 8 * SLOT
+AT_LAST_WT = 10 * SLOT
+LATE_GATHERS = {2: AT_WT_BF16 + SLOT, 3: AT_FIRST_H}
 
 
 def tile_list_msg_tanh_res_bias_kernel(
@@ -36,281 +50,284 @@ def tile_list_msg_tanh_res_bias_kernel(
         keep = ctx.enter_context(tc.tile_pool(name="keep", bufs=1))
         ring = ctx.enter_context(tc.tile_pool(name="ring", bufs=2))
         placed = ctx.enter_context(tc.tile_pool(name="placed", bufs=1))
-        ps1 = ctx.enter_context(tc.psum_pool(name="ps1", bufs=6))
-        ps2 = ctx.enter_context(tc.psum_pool(name="ps2", bufs=2))
+        psum_a = ctx.enter_context(tc.psum_pool(name="psum_a", bufs=6))
+        psum_y = ctx.enter_context(tc.psum_pool(name="psum_y", bufs=2))
 
-        lists = [keep.tile([P, J // 16], U16, name="offs_a"), keep.tile([P, J // 16], U16, name="offs_b")]
+        lists = [keep.tile([P, J // 16], U16, name="list_source"), keep.tile([P, J // 16], U16, name="list_target")]
         tab_w = keep.tile([P, T], I32, name="tab_w", align_bytes=64)
-        tab_s = keep.tile([P, T], U8, name="tab_s", align_bytes=64)
-        ws_s_raw = keep.tile([P, 2, R], U8, name="ws_s_raw", align_bytes=64)
-        wd_s = keep.tile([P, 4 * N], U8, name="wd_s", align_bytes=64)
-        wd8_s = wd_s[:, 0 : 2 * N].rearrange("p (a n) -> p a n", a=2)
-        wd4_s = wd_s[:, 2 * N : 4 * N].rearrange("p (a n) -> p a n", a=2)
-        planes = keep.tile([P, 4 * J], U8, name="tab_plane", align_bytes=64)
-        tab_plane = [planes[:, J * i : J * (i + 1)] for i in range(4)]
-        windows = [keep.tile([P, T], F32, name="window%d" % c, align_bytes=64) for c in range(3)]
-        warm = keep.tile([P, 1], F32, name="warm")
-        warm2 = keep.tile([P, 1], F32, name="warm2")
+        tab_s = keep.tile([P, T + PAD], U8, name="tab_s", align_bytes=64)
+        ws_s_tile = keep.tile([P, 2 * R + PAD], U8, name="ws_s_tile", align_bytes=64)
+        ws_s_loaded = ws_s_tile[:, 0 : 2 * R].rearrange("p (a r) -> p a r", a=2)
+        wd_s_tile = keep.tile([P, 4 * N + PAD], U8, name="wd_s_tile", align_bytes=64)
+        wd8_s = wd_s_tile[:, 0 : 2 * N].rearrange("p (a n) -> p a n", a=2)
+        wd4_s = wd_s_tile[:, 2 * N : 4 * N].rearrange("p (a n) -> p a n", a=2)
+        v_s_tile = keep.tile([P, 4 * J], U8, name="v_s_tile", align_bytes=64)
+        v_s = {(lst, a): v_s_tile[:, J * (2 * lst + a) : J * (2 * lst + a + 1)] for lst in range(2) for a in range(2)}
+        windows = [keep.tile([P, T], F32, name="window%d" % c, align_bytes=64) for c in range(TILES)]
 
-        for q in range(4):
-            nc.vector.memset(tab_s[32 * q : 32 * q + LOW, :].bitcast(I32), 0)
-        nc.vector.memset(ws_s_raw[:].rearrange("p a r -> p (a r)").bitcast(I32), 0)
-        nc.vector.memset(warm[:], 0.0)
-        nc.scalar.activation(out=warm2[:], in_=warm[:], func=ACT.Tanh)
-        nc.vector.memset(wd_s[:].bitcast(I32), 0)
-        nc.vector.memset(planes[96:128, :].bitcast(I32), 0)
+        nc.vector.memset(ws_s_tile[:].bitcast(I32), 0)
+        for quad in range(QUADS):
+            nc.vector.memset(tab_s[32 * quad : 32 * quad + ROW0, :].bitcast(I32), 0)
+        nc.vector.memset(wd_s_tile[:].bitcast(I32), 0)
+        nc.gpsimd.memset(v_s_tile[96:P, :].bitcast(I32), 0)
+        for window in windows:
+            nc.gpsimd.memset(window[:].bitcast(I32), 0)
 
-        def load_rows(dst, src):
-            for q in range(4):
-                nc.sync.dma_start(out=dst[32 * q + LOW : 32 * q + 32, :].bitcast(I32), in_=src[:, 4 * q : 4 * q + 4, :].bitcast(I32))
+        wt_loaded = {}
+        ws_loaded = {}
 
-        def lower(dst, src, a):
-            nc.sync.dma_start(out=dst[0:100, :].bitcast(I32), in_=src[LOW + 4 * a : LOW + 4 * a + 100, :].bitcast(I32))
+        def load_wt(a, half):
+            if (a, half) == (1, 1):
+                loaded = placed.tile([P, PACK, PASS], F32, name="wt_loaded11", align_bytes=64, offset=AT_LAST_WT)
+            else:
+                loaded = keep.tile([P, PACK, PASS], F32, name="wt_loaded%d%d" % (a, half))
+            rows = wt[PASS * a : PASS * (a + 1), PASS * half : PASS * (half + 1)]
+            nc.sync.dma_start(out=loaded[:], in_=rows.rearrange("(p i) r -> p i r", i=PACK))
+            wt_loaded[a, half] = loaded
 
-        wt_raw = {}
-        ws_raw = {}
+        def load_ws(half):
+            loaded = keep.tile([P, 2, PASS], I32, name="ws_loaded%d" % half)
+            words = ws_words.rearrange("a p r i -> p a (r i)")[:, :, PACK * PASS * half : PACK * PASS * (half + 1)]
+            nc.sync.dma_start(out=loaded[:], in_=words.bitcast(I32))
+            ws_loaded[half] = loaded
 
-        def load_wt(a, blk):
-            raw = keep.tile([P, 4, HALF], F32, name="wt_raw%d%d" % (a, blk))
-            nc.sync.dma_start(out=raw[:], in_=wt[512 * a : 512 * (a + 1), HALF * blk : HALF * (blk + 1)].rearrange("(p i) r -> p i r", i=4))
-            wt_raw[a, blk] = raw
+        def load_planes(planes, scales):
+            for quad in range(QUADS):
+                nc.sync.dma_start(
+                    out=planes[32 * quad : 32 * quad + 4, :, :].bitcast(I32),
+                    in_=scales[:, 4 * quad : 4 * quad + 4, :].rearrange("a q n -> q a n").bitcast(I32),
+                )
 
-        def load_ws(blk):
-            raw = keep.tile([P, 2, HALF], I32, name="ws_raw%d" % blk)
-            src = ws_words.rearrange("a p r i -> p a (r i)")[:, :, 4 * HALF * blk : 4 * HALF * (blk + 1)]
-            nc.sync.dma_start(out=raw[:], in_=src.bitcast(I32))
-            ws_raw[blk] = raw
+        def gather_scales():
+            for lst in (TARGET, SOURCE):
+                picked_s = keep.tile([P, J], U8, name="picked_s%d" % lst, align_bytes=64)
+                nc.vector.tensor_copy(picked_s[:], tab_s[:, 0:T].indirect(lists[lst][:]))
+                for a in range(2):
+                    first = ROW0 + 4 * a
+                    nc.sync.dma_start(
+                        out=v_s[lst, a][0:PLANE_ROWS, :].bitcast(I32), in_=picked_s[first : first + PLANE_ROWS, :].bitcast(I32)
+                    )
 
-        nc.sync.dma_start(lists[0][:], offs)
-        load_rows(tab_s, tab_scales)
-        nc.sync.dma_start(lists[1][:], offs2)
+        nc.sync.dma_start(lists[TARGET][:], offs2)
+        for quad in range(QUADS):
+            nc.sync.dma_start(
+                out=tab_s[32 * quad + ROW0 : 32 * quad + 32, 0:T].bitcast(I32),
+                in_=tab_scales[:, 4 * quad : 4 * quad + 4, :].bitcast(I32),
+            )
+        nc.sync.dma_start(lists[SOURCE][:], offs)
         nc.sync.dma_start(out=tab_w[:], in_=tab_words[0].rearrange("p t d -> p (t d)").bitcast(I32))
         load_wt(0, 0)
-        for q in range(4):
-            nc.sync.dma_start(
-                out=ws_s_raw[32 * q : 32 * q + 4, :, :].bitcast(I32),
-                in_=ws_scales[:, 4 * q : 4 * q + 4, :].rearrange("a q r -> q a r").bitcast(I32),
-            )
+        load_planes(ws_s_loaded, ws_scales)
         load_wt(1, 0)
         load_ws(0)
-        for i in (1, 0):
-            g = keep.tile([P, J], U8, name="picked_s%d" % i, align_bytes=64)
-            nc.vector.tensor_copy(g[:], tab_s[:].indirect(lists[i][:]))
-            for a in range(2):
-                lower(tab_plane[2 * i + a], g, a)
+        gather_scales()
         load_wt(0, 1)
         load_wt(1, 1)
         load_ws(1)
-        sm_t = keep.tile([P, 2, 4], F32, name="sm_t")
-        b_t = keep.tile([P, 4], F32, name="b_t")
+        sm_t = keep.tile([P, 2, PACK], F32, name="sm_t")
+        b_t = keep.tile([P, TILES], F32, name="b_t")
         wd8_w = keep.tile([P, 2, N], I32, name="wd8_w", align_bytes=64)
         wd4_w = keep.tile([P, 2, 2 * N], U8, name="wd4_w", align_bytes=64)
         wgo_t = keep.tile([P, J], F32, name="wgo_t")
-        nc.sync.dma_start(out=sm_t[:], in_=sm.rearrange("(g p t) -> p g t", g=2, t=4))
+        nc.sync.dma_start(out=sm_t[:], in_=sm.rearrange("(g p t) -> p g t", g=2, t=PACK))
         nc.sync.dma_start(out=wd8_w[:], in_=wd8_words.rearrange("a p n i -> p a (n i)").bitcast(I32))
         nc.sync.dma_start(out=wd4_w[:].bitcast(I32), in_=wd4_words.rearrange("a p n -> p a n").bitcast(I32))
         nc.sync.dma_start(out=wgo_t[:], in_=wgo)
-        for dst, src in ((wd8_s, wd8_scales), (wd4_s, wd4_scales)):
-            for q in range(4):
-                nc.sync.dma_start(
-                    out=dst[32 * q : 32 * q + 4, :, :].bitcast(I32),
-                    in_=src[:, 4 * q : 4 * q + 4, :].rearrange("a q n -> q a n").bitcast(I32),
-                )
+        load_planes(wd8_s, wd8_scales)
+        load_planes(wd4_s, wd4_scales)
         with nc.allow_non_contiguous_dma(reason="one bias value to a partition"):
             nc.sync.dma_start(out=b_t[:], in_=b.rearrange("(c p) -> p c", p=P))
 
-        ws_s = keep.tile([P, 2, R], U8, name="ws_s", align_bytes=64)
-        nc.vector.tensor_copy(
-            out=ws_s[:].rearrange("p a (g t mq mm) -> p (a g) mq t mm", g=2, t=4, mm=16),
-            in_=ws_s_raw[:].rearrange("p a (g mq mm t) -> p (a g) mq t mm", g=2, t=4, mm=16),
-        )
-        for c in range(len(windows)):
-            nc.vector.memset(windows[c][:], 0.0)
+        picked_w = {}
+        v_w = {}
 
-        parted = {}
+        def entries(lst, chunk):
+            return lists[lst][:, chunk * CHUNK // 16 : (chunk + 1) * CHUNK // 16]
 
-        def gather_words(run):
-            lo, hi = RUNS[run]
-            gs = []
-            for i in range(2):
-                if run == 0:
-                    g = keep.tile([P, hi - lo], U32, name="picked_w%d" % i)
+        def gather_words(chunk):
+            for lst in (TARGET, SOURCE):
+                name = "picked_w%d%d" % (chunk, lst)
+                if chunk in LATE_GATHERS:
+                    picked = placed.tile([P, CHUNK], U32, name=name, align_bytes=64, offset=LATE_GATHERS[chunk] + 4 * CHUNK * lst)
                 else:
-                    g = placed.tile([P, hi - lo], U32, name="picked_w%d%d" % (run, i), align_bytes=64, offset=HOLD_ON[run][i])
-                nc.vector.tensor_copy(g[:], tab_w[:].bitcast(U32).indirect(lists[i][:, lo // 16 : hi // 16]))
-                gs.append(g)
-            for i in range(2):
-                pt = keep.tile([P, 2, 2 * (hi - lo)], U8, name="parted%d%d" % (i, run), align_bytes=64)
-                nc.vector.tensor_copy(out=pt[:].bitcast(U16), in_=gs[i][:].bitcast(U16).rearrange("p (n d) -> p d n", d=2))
-                for tok in range(lo, hi, P):
-                    parted[i, tok] = (pt, tok - lo)
+                    picked = keep.tile([P, CHUNK], U32, name=name)
+                nc.vector.tensor_copy(picked[:], tab_w[:].bitcast(U32).indirect(entries(lst, chunk)))
+                picked_w[lst, chunk] = picked
 
-        wt_c = {}
+        def part_words(chunk):
+            for lst in (TARGET, SOURCE):
+                parted = keep.tile([P, 2, 2 * CHUNK], U8, name="v_w%d%d" % (lst, chunk), align_bytes=64)
+                nc.vector.tensor_copy(
+                    out=parted[:].bitcast(U16), in_=picked_w[lst, chunk][:].bitcast(U16).rearrange("p (n d) -> p d n", d=2)
+                )
+                v_w[lst, chunk] = parted
+
+        wt_w = {}
         wt_s = {}
-        ws_c = {}
+        ws_w = {}
+        ws_s = keep.tile([P, 2, R], U8, name="ws_s", align_bytes=64)
 
-        def prepare_wt(a, blk):
-            grouped = placed.tile([P, 4, P, 4], BF16, name="wt_bf%d%d" % (a, blk), align_bytes=64, offset=24576 + 4096 * (2 * blk + a))
-            dst = grouped[:].rearrange("p t m i -> p m t i")
-            src = wt_raw[a, blk][:].rearrange("p i (m t) -> p m t i", t=4)
-            cut = 128 if (a, blk) == (1, 1) else P
-            nc.scalar.copy(out=dst[:, 0:cut], in_=src[:, 0:cut])
-            if cut < P:
-                nc.vector.tensor_copy(out=dst[:, cut:P], in_=src[:, cut:P])
-            codes = keep.tile([P, HALF], U32, name="wt_c%d%d" % (a, blk), align_bytes=64)
-            scales = keep.tile([P, HALF], U8, name="wt_s%d%d" % (a, blk), align_bytes=64)
-            nc.vector.quantize_mx(out=codes[:].bitcast(FP8X4), scales=scales[:], in_=grouped[:].rearrange("p t m i -> p (t m i)"))
-            wt_c[a, blk] = codes
-            wt_s[a, blk] = scales
-
-        def prepare_ws(blk):
-            perm = keep.tile([P, 2, HALF], I32, name="ws_c%d" % blk, align_bytes=64)
+        def reorder_ws_scales():
             nc.vector.tensor_copy(
-                out=perm[:].rearrange("p a (t mq mm) -> p a mq t mm", t=4, mm=4),
-                in_=ws_raw[blk][:].rearrange("p a (mq mm t) -> p a mq t mm", t=4, mm=4),
+                out=ws_s[:].rearrange("p a (g t mq mm) -> p (a g) mq t mm", g=2, t=PACK, mm=16),
+                in_=ws_s_loaded.rearrange("p a (g mq mm t) -> p (a g) mq t mm", g=2, t=PACK, mm=16),
             )
-            ws_c[blk] = perm
 
-        h_c = {}
+        def reorder_ws_words(half):
+            words = keep.tile([P, 2, PASS], I32, name="ws_w%d" % half, align_bytes=64)
+            nc.vector.tensor_copy(
+                out=words[:].rearrange("p a (t mq mm) -> p a mq t mm", t=PACK, mm=4),
+                in_=ws_loaded[half][:].rearrange("p a (mq mm t) -> p a mq t mm", t=PACK, mm=4),
+            )
+            ws_w[half] = words
+
+        def quantize_wt(a, half):
+            rounded = placed.tile(
+                [P, PACK, P, PACK], BF16, name="wt_bf16_%d%d" % (a, half), align_bytes=64, offset=AT_WT_BF16 + SLOT * (2 * half + a)
+            )
+            nc.scalar.copy(
+                out=rounded[:].rearrange("p t m i -> p m t i"),
+                in_=wt_loaded[a, half][:].rearrange("p i (m t) -> p m t i", t=PACK),
+            )
+            words = keep.tile([P, PASS], U32, name="wt_w%d%d" % (a, half), align_bytes=64)
+            plane = keep.tile([P, PASS], U8, name="wt_s%d%d" % (a, half), align_bytes=64)
+            nc.vector.quantize_mx(out=words[:].bitcast(FP8X4), scales=plane[:], in_=rounded[:].rearrange("p t m i -> p (t m i)"))
+            wt_w[a, half] = words
+            wt_s[a, half] = plane
+
+        h_w = {}
         h_s = {}
-
         sums = {}
 
-        def sums1(ch, blk):
-            for s in range(2):
-                tok = ch * CH + s * P
-                acc = ps1.tile([P, 4, P], F32, name="acc1", tag="acc1")
-                sums[ch, blk, s] = acc
-                passes = [(i, a, t) for i in (1, 0) for a in range(2) for t in range(4)]
-                for n, (i, a, t) in enumerate(passes):
-                    cols = slice(P * t, P * (t + 1))
-                    if i == 1:
-                        wc, wsc = wt_c[a, blk][:, cols], wt_s[a, blk][:, cols]
-                    else:
-                        wc, wsc = ws_c[blk][:, a, cols], ws_s[:, a, HALF * blk + P * t : HALF * blk + P * (t + 1)]
-                    pt, loc = parted[i, tok]
-                    nc.tensor.matmul_mx(
-                        out=acc[:, t, :],
-                        lhsT=wc.bitcast(FP8X4),
-                        lhsT_scale=wsc,
-                        rhs=pt[:, a, 2 * loc : 2 * (loc + P)].bitcast(FP4X4),
-                        rhs_scale=tab_plane[2 * i + a][:, tok : tok + P],
-                        start=(n == 0),
-                        stop=(n == len(passes) - 1),
-                    )
-
-        def stage1(ch, blk):
-            if (ch, blk, 0) not in sums:
-                sums1(ch, blk)
-            th = ring.tile([P, 2, 4 * P], F32, name="th", tag="th", bufs=3)
-            if ch == 0:
-                hb = placed.tile([P, CH, 4], BF16, name="hb0%d" % blk, align_bytes=64, offset=8192 * blk)
-            else:
-                hb = ring.tile([P, CH, 4], BF16, name="hb", tag="hb", bufs=3, align_bytes=64)
-            on_s = [s for s in range(2) if (ch, blk, s) not in ON_VECTOR and (ch, blk, s) not in ON_GPSIMD]
-            for s in range(2):
-                acc = sums[ch, blk, s]
-                if s in on_s:
-                    nc.scalar.activation(out=th[:, s, :], in_=acc[:].rearrange("p t n -> p (t n)"), func=ACT.Tanh)
+        def first_product(chunk, half, group):
+            bank = psum_a.tile([P, PACK * P], F32, name="bank_a", tag="bank_a")
+            sums[chunk, half, group] = bank
+            edge = chunk * CHUNK + group * P
+            passes = [(lst, a, t) for lst in (TARGET, SOURCE) for a in range(2) for t in range(PACK)]
+            for n, (lst, a, t) in enumerate(passes):
+                cols = slice(P * t, P * (t + 1))
+                if lst == TARGET:
+                    words, plane = wt_w[a, half][:, cols], wt_s[a, half][:, cols]
                 else:
-                    nc.scalar.activation(
-                        out=th[:, s, :].rearrange("p (n t) -> p n t", t=4),
-                        in_=acc[:].rearrange("p t n -> p n t"),
-                        func=ACT.Tanh,
+                    words, plane = ws_w[half][:, a, cols], ws_s[:, a, PASS * half + P * t : PASS * half + P * (t + 1)]
+                nc.tensor.matmul_mx(
+                    out=bank[:, cols],
+                    lhsT=words.bitcast(FP8X4),
+                    lhsT_scale=plane,
+                    rhs=v_w[lst, chunk][:, a, 2 * P * group : 2 * P * (group + 1)].bitcast(FP4X4),
+                    rhs_scale=v_s[lst, a][:, edge : edge + P],
+                    start=(n == 0),
+                    stop=(n == len(passes) - 1),
+                )
+
+        def make_h(chunk, half):
+            if (chunk, half) == (0, 0):
+                tanh = placed.tile([P, GROUPS, PACK * P], F32, name="tanh00", align_bytes=64, offset=AT_LAST_WT)
+            else:
+                tanh = ring.tile([P, GROUPS, PACK * P], F32, name="tanh", tag="tanh", bufs=3)
+            if (chunk, half) == (0, 1):
+                h = placed.tile([P, CHUNK, PACK], BF16, name="h01", align_bytes=64, offset=AT_FIRST_H)
+            else:
+                h = ring.tile([P, CHUNK, PACK], BF16, name="h", tag="h", bufs=3, align_bytes=64)
+            on_scalar = [group for group in range(GROUPS) if (chunk, half, group) not in ON_VECTOR]
+            if on_scalar:
+                if half == 1:
+                    scaled = placed.tile(
+                        [P, PACK, CHUNK], BF16, name="scaled%d1" % chunk, align_bytes=64, offset=AT_SCALED + SLOT * (chunk - 1)
                     )
-                    engine = nc.vector if (ch, blk, s) in ON_VECTOR else nc.gpsimd
-                    engine.tensor_tensor(
-                        out=hb[:, P * s : P * (s + 1), :],
-                        in0=th[:, s, :].rearrange("p (n t) -> p n t", t=4),
-                        in1=sm_t[:, blk, :].unsqueeze(1).to_broadcast([P, P, 4]),
+                else:
+                    scaled = ring.tile([P, PACK, CHUNK], BF16, name="scaled", tag="scaled")
+            for group in range(GROUPS):
+                if (chunk, half, group) not in sums:
+                    first_product(chunk, half, group)
+                bank = sums[chunk, half, group]
+                if group in on_scalar:
+                    nc.scalar.activation(out=tanh[:, group, :], in_=bank[:], func=ACT.Tanh)
+                else:
+                    side_by_side = tanh[:, group, :].rearrange("p (n t) -> p n t", t=PACK)
+                    nc.scalar.activation(out=side_by_side, in_=bank[:].rearrange("p (t n) -> p n t", t=PACK), func=ACT.Tanh)
+                    nc.vector.tensor_tensor(
+                        out=h[:, P * group : P * (group + 1), :],
+                        in0=side_by_side,
+                        in1=sm_t[:, half, :].unsqueeze(1).to_broadcast([P, P, PACK]),
                         op=MULT,
                     )
-            if on_s:
-                s0, s1 = on_s[0], on_s[-1] + 1
-                if blk == 1 and ch > 0:
-                    hp = placed.tile([P, 4, CH], BF16, name="hp%d1" % ch, align_bytes=64, offset=16384 + 2048 * (ch - 1))
-                else:
-                    hp = ring.tile([P, 4, CH], BF16, name="hp", tag="hp")
-                for t in range(4):
+            if on_scalar:
+                edges = slice(P * on_scalar[0], P * (on_scalar[-1] + 1))
+                for t in range(PACK):
                     nc.scalar.activation(
-                        out=hp[:, t, P * s0 : P * s1].rearrange("p (s n) -> p s n", n=P),
-                        in_=th[:, s0:s1, P * t : P * (t + 1)],
+                        out=scaled[:, t, edges].rearrange("p (g n) -> p g n", n=P),
+                        in_=tanh[:, on_scalar[0] : on_scalar[-1] + 1, P * t : P * (t + 1)],
                         func=ACT.Copy,
-                        scale=sm_t[:, blk, t : t + 1],
+                        scale=sm_t[:, half, t : t + 1],
                     )
-                nc.scalar.copy(
-                    out=hb[:, P * s0 : P * s1, :],
-                    in_=hp[:, :, P * s0 : P * s1].rearrange("p t n -> p n t"),
+                nc.scalar.copy(out=h[:, edges, :], in_=scaled[:, :, edges].rearrange("p t n -> p n t"))
+            words = keep.tile([P, CHUNK], U32, name="h_w%d%d" % (chunk, half), align_bytes=64)
+            plane = keep.tile([P, CHUNK], U8, name="h_s%d%d" % (chunk, half), align_bytes=64)
+            nc.vector.quantize_mx(out=words[:].bitcast(FP8X4), scales=plane[:], in_=h[:].rearrange("p n t -> p (n t)"))
+            h_w[chunk, half] = words
+            h_s[chunk, half] = plane
+
+        def send(chunk, c):
+            bank = psum_y.tile([P, CHUNK], F32, name="bank_y", tag="bank_y")
+            rows = slice(P * c, P * (c + 1))
+            for half in (1, 0):
+                nc.tensor.matmul_mx(
+                    out=bank[:],
+                    lhsT=wd8_w[:, half, rows].bitcast(FP8X4),
+                    lhsT_scale=wd8_s[:, half, rows],
+                    rhs=h_w[chunk, half][:].bitcast(FP8X4),
+                    rhs_scale=h_s[chunk, half][:],
+                    start=(half == 1),
+                    stop=False,
                 )
-            codes = keep.tile([P, CH], U32, name="h_c%d%d" % (ch, blk), align_bytes=64)
-            scales = keep.tile([P, CH], U8, name="h_s%d%d" % (ch, blk), align_bytes=64)
-            nc.vector.quantize_mx(out=codes[:].bitcast(FP8X4), scales=scales[:], in_=hb[:].rearrange("p n t -> p (n t)"))
-            h_c[ch, blk] = codes
-            h_s[ch, blk] = scales
-
-        def stage2(ch):
-            accs = []
-            for c in range(4):
-                acc = ps2.tile([P, CH], F32, name="acc2", tag="acc2")
-                accs.append(acc)
-                for a in (1, 0):
+                for group in range(GROUPS):
+                    cols = slice(P * group, P * (group + 1))
                     nc.tensor.matmul_mx(
-                        out=acc[:],
-                        lhsT=wd8_w[:, a, P * c : P * (c + 1)].bitcast(FP8X4),
-                        lhsT_scale=wd8_s[:, a, P * c : P * (c + 1)],
-                        rhs=h_c[ch, a][:].bitcast(FP8X4),
-                        rhs_scale=h_s[ch, a][:],
-                        start=(a == 1),
-                        stop=False,
+                        out=bank[:, cols],
+                        lhsT=wd4_w[:, half, 2 * P * c : 2 * P * (c + 1)].bitcast(FP4X4),
+                        lhsT_scale=wd4_s[:, half, rows],
+                        rhs=h_w[chunk, half][:, cols].bitcast(FP8X4),
+                        rhs_scale=h_s[chunk, half][:, cols],
+                        start=False,
+                        stop=(half == 0 and group == GROUPS - 1),
                     )
-                    for s in range(CH // P):
-                        cols = slice(P * s, P * (s + 1))
-                        nc.tensor.matmul_mx(
-                            out=acc[:, cols],
-                            lhsT=wd4_w[:, a, 2 * P * c : 2 * P * (c + 1)].bitcast(FP4X4),
-                            lhsT_scale=wd4_s[:, a, P * c : P * (c + 1)],
-                            rhs=h_c[ch, a][:, cols].bitcast(FP8X4),
-                            rhs_scale=h_s[ch, a][:, cols],
-                            start=False,
-                            stop=(a == 0 and s == CH // P - 1),
-                        )
-            return accs
-
-        def emit(ch, c, acc):
-            if ch < NCH - 1 and c == HELD[ch]:
-                y = placed.tile([P, CH], F32, name="y%d3" % ch, align_bytes=64, offset=16384 + 2048 * ch)
+            if chunk < CHUNKS - 1 and c == KEPT_BACK[chunk]:
+                y = placed.tile([P, CHUNK], F32, name="y_kept%d" % chunk, align_bytes=64, offset=AT_SCALED + SLOT * chunk)
             else:
-                y = ring.tile([P, CH], F32, name="y", tag="y", bufs=6)
-            nc.scalar.activation(out=y[:], in_=acc[:], func=ACT.Identity, bias=b_t[:, c : c + 1])
+                y = ring.tile([P, CHUNK], F32, name="y", tag="y", bufs=6)
+            nc.scalar.activation(out=y[:], in_=bank[:], func=ACT.Identity, bias=b_t[:, c : c + 1])
             nc.vector.tensor_tensor(
-                windows[c][:].indirect(lists[1][:, 16 * ch : 16 * (ch + 1)]), y[:], wgo_t[:, CH * ch : CH * (ch + 1)], MULT
+                windows[c][:].indirect(entries(TARGET, chunk)), y[:], wgo_t[:, CHUNK * chunk : CHUNK * (chunk + 1)], MULT
             )
-            if ch == NCH - 1:
-                nc.sync.dma_start(out=out[P * c : P * (c + 1), :], in_=windows[c][:])
+            if chunk == CHUNKS - 1:
+                nc.sync.dma_start(out=out[rows, :], in_=windows[c][:])
 
         gather_words(0)
-        prepare_wt(0, 0)
-        prepare_wt(1, 0)
-        prepare_ws(0)
         gather_words(1)
-        prepare_wt(0, 1)
-        prepare_wt(1, 1)
-        prepare_ws(1)
-        stage1(0, 0)
-        sums1(1, 0)
-        stage1(0, 1)
-        gather_words(2)
-        for c in range(len(windows), 4):
-            w = placed.tile([P, T], F32, name="window%d" % c, align_bytes=64, offset=8192 * (c - 2))
-            nc.vector.memset(w[:], 0.0)
-            windows.append(w)
-        for ch in range(NCH):
-            accs = stage2(ch)
-            held = HELD[ch] if ch < NCH - 1 else 4
-            for c in range(held):
-                emit(ch, c, accs[c])
-            if ch + 1 < NCH:
-                stage1(ch + 1, 0)
-                stage1(ch + 1, 1)
-            for c in range(held, 4):
-                emit(ch, c, accs[c])
+        part_words(0)
+        quantize_wt(0, 0)
+        quantize_wt(1, 0)
+        reorder_ws_scales()
+        reorder_ws_words(0)
+        part_words(1)
+        quantize_wt(0, 1)
+        quantize_wt(1, 1)
+        reorder_ws_words(1)
+        make_h(0, 0)
+        for group in range(GROUPS):
+            first_product(1, 0, group)
+        make_h(0, 1)
+        for chunk in LATE_GATHERS:
+            gather_words(chunk)
+            part_words(chunk)
+
+        for chunk in range(CHUNKS - 1):
+            for c in range(KEPT_BACK[chunk]):
+                send(chunk, c)
+            make_h(chunk + 1, 0)
+            make_h(chunk + 1, 1)
+            for c in range(KEPT_BACK[chunk], TILES):
+                send(chunk, c)
+        for c in range(TILES):
+            send(CHUNKS - 1, c)

@@ -28,6 +28,7 @@ SOURCE, TARGET = 0, 1
 
 ROW0 = 24
 PLANE_ROWS = 100
+EARLY = 2 * CHUNK
 PAD = 4
 
 ON_VECTOR = {(0, half, group) for half in range(2) for group in range(GROUPS)} | {(CHUNKS - 1, 0, 0)}
@@ -38,8 +39,12 @@ SLOT = 4096
 AT_WT_BF16 = 0
 AT_SCALED = 4 * SLOT
 AT_FIRST_H = 8 * SLOT
-AT_LAST_WT = 10 * SLOT
+AT_WT_F32 = 10 * SLOT
 LATE_GATHERS = {2: AT_WT_BF16 + SLOT, 3: AT_FIRST_H}
+
+
+def at_wt(a, half):
+    return AT_WT_F32 + 2 * SLOT * (3 - 2 * half - a)
 
 
 def tile_list_msg_tanh_res_bias_kernel(
@@ -63,7 +68,7 @@ def tile_list_msg_tanh_res_bias_kernel(
         wd4_s = wd_s_tile[:, 2 * N : 4 * N].rearrange("p (a n) -> p a n", a=2)
         v_s_tile = keep.tile([P, 4 * J], U8, name="v_s_tile", align_bytes=64)
         v_s = {(lst, a): v_s_tile[:, J * (2 * lst + a) : J * (2 * lst + a + 1)] for lst in range(2) for a in range(2)}
-        windows = [keep.tile([P, T], F32, name="window%d" % c, align_bytes=64) for c in range(TILES)]
+        windows = [keep.tile([P, T], F32, name="window%d" % c, align_bytes=64) for c in range(2)]
 
         nc.vector.memset(ws_s_tile[:].bitcast(I32), 0)
         for quad in range(QUADS):
@@ -77,10 +82,7 @@ def tile_list_msg_tanh_res_bias_kernel(
         ws_loaded = {}
 
         def load_wt(a, half):
-            if (a, half) == (1, 1):
-                loaded = placed.tile([P, PACK, PASS], F32, name="wt_loaded11", align_bytes=64, offset=AT_LAST_WT)
-            else:
-                loaded = keep.tile([P, PACK, PASS], F32, name="wt_loaded%d%d" % (a, half))
+            loaded = placed.tile([P, PACK, PASS], F32, name="wt_loaded%d%d" % (a, half), align_bytes=64, offset=at_wt(a, half))
             rows = wt[PASS * a : PASS * (a + 1), PASS * half : PASS * (half + 1)]
             nc.sync.dma_start(out=loaded[:], in_=rows.rearrange("(p i) r -> p i r", i=PACK))
             wt_loaded[a, half] = loaded
@@ -98,14 +100,20 @@ def tile_list_msg_tanh_res_bias_kernel(
                     in_=scales[:, 4 * quad : 4 * quad + 4, :].rearrange("a q n -> q a n").bitcast(I32),
                 )
 
+        picked_s = {}
+
         def gather_scales():
             for lst in (TARGET, SOURCE):
-                picked_s = keep.tile([P, J], U8, name="picked_s%d" % lst, align_bytes=64)
-                nc.vector.tensor_copy(picked_s[:], tab_s[:, 0:T].indirect(lists[lst][:]))
+                picked_s[lst] = keep.tile([P, J], U8, name="picked_s%d" % lst, align_bytes=64)
+                nc.vector.tensor_copy(picked_s[lst][:], tab_s[:, 0:T].indirect(lists[lst][:]))
+
+        def lower_planes(lo, hi):
+            for lst in (TARGET, SOURCE):
                 for a in range(2):
                     first = ROW0 + 4 * a
                     nc.sync.dma_start(
-                        out=v_s[lst, a][0:PLANE_ROWS, :].bitcast(I32), in_=picked_s[first : first + PLANE_ROWS, :].bitcast(I32)
+                        out=v_s[lst, a][0:PLANE_ROWS, lo:hi].bitcast(I32),
+                        in_=picked_s[lst][first : first + PLANE_ROWS, lo:hi].bitcast(I32),
                     )
 
         nc.sync.dma_start(lists[TARGET][:], offs2)
@@ -115,28 +123,31 @@ def tile_list_msg_tanh_res_bias_kernel(
                 in_=tab_scales[:, 4 * quad : 4 * quad + 4, :].bitcast(I32),
             )
         nc.sync.dma_start(lists[SOURCE][:], offs)
+        sm_t = keep.tile([P, 2, PACK], F32, name="sm_t")
+        b_t = keep.tile([P, TILES], F32, name="b_t")
+        wd8_w = keep.tile([P, 2, N], I32, name="wd8_w", align_bytes=64)
+        wd4_w = keep.tile([P, 2, 2 * N], U8, name="wd4_w", align_bytes=64)
+        wgo_t = keep.tile([P, J], F32, name="wgo_t")
         nc.sync.dma_start(out=tab_w[:], in_=tab_words[0].rearrange("p t d -> p (t d)").bitcast(I32))
         load_wt(0, 0)
         load_planes(ws_s_loaded, ws_scales)
         load_wt(1, 0)
         load_ws(0)
         gather_scales()
+        lower_planes(0, EARLY)
         load_wt(0, 1)
         load_wt(1, 1)
         load_ws(1)
-        sm_t = keep.tile([P, 2, PACK], F32, name="sm_t")
-        b_t = keep.tile([P, TILES], F32, name="b_t")
-        wd8_w = keep.tile([P, 2, N], I32, name="wd8_w", align_bytes=64)
-        wd4_w = keep.tile([P, 2, 2 * N], U8, name="wd4_w", align_bytes=64)
-        wgo_t = keep.tile([P, J], F32, name="wgo_t")
         nc.sync.dma_start(out=sm_t[:], in_=sm.rearrange("(g p t) -> p g t", g=2, t=PACK))
         nc.sync.dma_start(out=wd8_w[:], in_=wd8_words.rearrange("a p n i -> p a (n i)").bitcast(I32))
         nc.sync.dma_start(out=wd4_w[:].bitcast(I32), in_=wd4_words.rearrange("a p n -> p a n").bitcast(I32))
-        nc.sync.dma_start(out=wgo_t[:], in_=wgo)
         load_planes(wd8_s, wd8_scales)
         load_planes(wd4_s, wd4_scales)
         with nc.allow_non_contiguous_dma(reason="one bias value to a partition"):
             nc.sync.dma_start(out=b_t[:], in_=b.rearrange("(c p) -> p c", p=P))
+        nc.sync.dma_start(out=wgo_t[:, 0:CHUNK], in_=wgo[:, 0:CHUNK])
+        lower_planes(EARLY, J)
+        nc.sync.dma_start(out=wgo_t[:, CHUNK:J], in_=wgo[:, CHUNK:J])
 
         picked_w = {}
         v_w = {}
@@ -222,7 +233,7 @@ def tile_list_msg_tanh_res_bias_kernel(
 
         def make_h(chunk, half):
             if (chunk, half) == (0, 0):
-                tanh = placed.tile([P, GROUPS, PACK * P], F32, name="tanh00", align_bytes=64, offset=AT_LAST_WT)
+                tanh = placed.tile([P, GROUPS, PACK * P], F32, name="tanh00", align_bytes=64, offset=at_wt(1, 1))
             else:
                 tanh = ring.tile([P, GROUPS, PACK * P], F32, name="tanh", tag="tanh", bufs=3)
             if (chunk, half) == (0, 1):
@@ -314,6 +325,10 @@ def tile_list_msg_tanh_res_bias_kernel(
         quantize_wt(0, 1)
         quantize_wt(1, 1)
         reorder_ws_words(1)
+        for a, half in ((1, 0), (0, 1)):
+            window = placed.tile([P, T], F32, name="window%d" % len(windows), align_bytes=64, offset=at_wt(a, half))
+            nc.vector.memset(window[:].bitcast(I32), 0)
+            windows.append(window)
         make_h(0, 0)
         for group in range(GROUPS):
             first_product(1, 0, group)

@@ -26,25 +26,17 @@ GROUPS = CHUNK // P
 TILES = N // P
 SOURCE, TARGET = 0, 1
 
-ROW0 = 24
-PLANE_ROWS = 100
-EARLY = 2 * CHUNK
-PAD = 4
+UNITS = [(0, 0), (1, 0), (0, 1), (1, 1), (2, 0), (2, 1), (3, 0), (3, 1)]
 
-ON_VECTOR = {(0, half, group) for half in range(2) for group in range(GROUPS)} | {(CHUNKS - 1, 0, 0)}
+ON_VECTOR = {(0, 0), (0, 1), (1, 0)}
 
-KEPT_BACK = (1, 2, 2)
-
-SLOT = 4096
-AT_WT_BF16 = 0
-AT_SCALED = 4 * SLOT
-AT_FIRST_H = 8 * SLOT
-AT_WT_F32 = 10 * SLOT
-LATE_GATHERS = {2: AT_WT_BF16 + SLOT, 3: AT_FIRST_H}
-
-
-def at_wt(a, half):
-    return AT_WT_F32 + 2 * SLOT * (3 - 2 * half - a)
+SLOT = 4 * PACK * CHUNK
+KB = 1024
+AT_ROUNDED = SLOT * len(UNITS)
+AT_FIRST_H = AT_ROUNDED + 4 * KB
+LATE_GATHERS = {2: AT_ROUNDED, 3: AT_FIRST_H}
+BANK = 2048
+BANKS_A = 6
 
 
 def tile_list_msg_tanh_res_bias_kernel(
@@ -55,37 +47,34 @@ def tile_list_msg_tanh_res_bias_kernel(
         keep = ctx.enter_context(tc.tile_pool(name="keep", bufs=1))
         ring = ctx.enter_context(tc.tile_pool(name="ring", bufs=2))
         placed = ctx.enter_context(tc.tile_pool(name="placed", bufs=1))
-        psum_a = ctx.enter_context(tc.psum_pool(name="psum_a", bufs=6))
-        psum_y = ctx.enter_context(tc.psum_pool(name="psum_y", bufs=2))
+        psum = ctx.enter_context(tc.psum_pool(name="psum", bufs=1))
 
         lists = [keep.tile([P, J // 16], U16, name="list_source"), keep.tile([P, J // 16], U16, name="list_target")]
         tab_w = keep.tile([P, T], I32, name="tab_w", align_bytes=64)
-        tab_s = keep.tile([P, T + PAD], U8, name="tab_s", align_bytes=64)
-        ws_s_tile = keep.tile([P, 2 * R + PAD], U8, name="ws_s_tile", align_bytes=64)
-        ws_s_loaded = ws_s_tile[:, 0 : 2 * R].rearrange("p (a r) -> p a r", a=2)
-        wd_s_tile = keep.tile([P, 4 * N + PAD], U8, name="wd_s_tile", align_bytes=64)
-        wd8_s = wd_s_tile[:, 0 : 2 * N].rearrange("p (a n) -> p a n", a=2)
-        wd4_s = wd_s_tile[:, 2 * N : 4 * N].rearrange("p (a n) -> p a n", a=2)
-        v_s_tile = keep.tile([P, 4 * J], U8, name="v_s_tile", align_bytes=64)
-        v_s = {(lst, a): v_s_tile[:, J * (2 * lst + a) : J * (2 * lst + a + 1)] for lst in range(2) for a in range(2)}
-        windows = [keep.tile([P, T], F32, name="window%d" % c, align_bytes=64) for c in range(2)]
+        tab_s = keep.tile([P, T], U8, name="tab_s", align_bytes=64)
+        ws_s_loaded = keep.tile([P, 2, R], U8, name="ws_s_loaded", align_bytes=64)
+        wd_s = keep.tile([P, 2, 2, N], U8, name="wd_s", align_bytes=64)
+        wd8_s, wd4_s = wd_s[:, 0, :, :], wd_s[:, 1, :, :]
+        picked_s = keep.tile([P, 2, J], U8, name="picked_s", align_bytes=64)
+        lowered_s = keep.tile([P, 2, J], U8, name="lowered_s", align_bytes=64)
+        windows = [keep.tile([P, T], F32, name="window%d" % c, align_bytes=64) for c in range(TILES)]
 
-        nc.vector.memset(ws_s_tile[:].bitcast(I32), 0)
-        for quad in range(QUADS):
-            nc.vector.memset(tab_s[32 * quad : 32 * quad + ROW0, :].bitcast(I32), 0)
-        nc.vector.memset(wd_s_tile[:].bitcast(I32), 0)
-        nc.gpsimd.memset(v_s_tile[96:P, :].bitcast(I32), 0)
-        for window in windows:
-            nc.gpsimd.memset(window[:].bitcast(I32), 0)
+        nc.vector.memset(tab_s[:].bitcast(I32), 0)
+        nc.vector.memset(ws_s_loaded[:].rearrange("p a r -> p (a r)").bitcast(I32), 0)
+        nc.vector.memset(lowered_s[:].rearrange("p l j -> p (l j)").bitcast(I32), 0)
+        nc.vector.memset(wd_s[:].rearrange("p w a n -> p (w a n)").bitcast(I32), 0)
+        for window in windows[:3]:
+            nc.vector.memset(window[:].bitcast(I32), 0)
 
         wt_loaded = {}
         ws_loaded = {}
 
-        def load_wt(a, half):
-            loaded = placed.tile([P, PACK, PASS], F32, name="wt_loaded%d%d" % (a, half), align_bytes=64, offset=at_wt(a, half))
-            rows = wt[PASS * a : PASS * (a + 1), PASS * half : PASS * (half + 1)]
+        def load_wt(a, half, lo=0, hi=PASS):
+            name = "wt_loaded%d%d_%d" % (a, half, lo)
+            loaded = keep.tile([P, PACK, hi - lo], F32, name=name, align_bytes=64)
+            rows = wt[PASS * a : PASS * (a + 1), PASS * half + lo : PASS * half + hi]
             nc.sync.dma_start(out=loaded[:], in_=rows.rearrange("(p i) r -> p i r", i=PACK))
-            wt_loaded[a, half] = loaded
+            wt_loaded.setdefault((a, half), []).append((lo, hi, loaded))
 
         def load_ws(half):
             loaded = keep.tile([P, 2, PASS], I32, name="ws_loaded%d" % half)
@@ -100,76 +89,67 @@ def tile_list_msg_tanh_res_bias_kernel(
                     in_=scales[:, 4 * quad : 4 * quad + 4, :].rearrange("a q n -> q a n").bitcast(I32),
                 )
 
-        picked_s = {}
-
-        def gather_scales():
-            for lst in (TARGET, SOURCE):
-                picked_s[lst] = keep.tile([P, J], U8, name="picked_s%d" % lst, align_bytes=64)
-                nc.vector.tensor_copy(picked_s[lst][:], tab_s[:, 0:T].indirect(lists[lst][:]))
-
-        def lower_planes(lo, hi):
-            for lst in (TARGET, SOURCE):
-                for a in range(2):
-                    first = ROW0 + 4 * a
-                    nc.sync.dma_start(
-                        out=v_s[lst, a][0:PLANE_ROWS, lo:hi].bitcast(I32),
-                        in_=picked_s[lst][first : first + PLANE_ROWS, lo:hi].bitcast(I32),
-                    )
-
-        nc.sync.dma_start(lists[TARGET][:], offs2)
-        for quad in range(QUADS):
-            nc.sync.dma_start(
-                out=tab_s[32 * quad + ROW0 : 32 * quad + 32, 0:T].bitcast(I32),
-                in_=tab_scales[:, 4 * quad : 4 * quad + 4, :].bitcast(I32),
-            )
-        nc.sync.dma_start(lists[SOURCE][:], offs)
         sm_t = keep.tile([P, 2, PACK], F32, name="sm_t")
         b_t = keep.tile([P, TILES], F32, name="b_t")
-        wd8_w = keep.tile([P, 2, N], I32, name="wd8_w", align_bytes=64)
+        wd8_w = keep.tile([P, 2, PACK * N], U8, name="wd8_w", align_bytes=64)
         wd4_w = keep.tile([P, 2, 2 * N], U8, name="wd4_w", align_bytes=64)
-        wgo_t = keep.tile([P, J], F32, name="wgo_t")
-        nc.sync.dma_start(out=tab_w[:], in_=tab_words[0].rearrange("p t d -> p (t d)").bitcast(I32))
+        wgo_first = keep.tile([P, CHUNK], F32, name="wgo_first")
+        wgo_rest = keep.tile([P, J - CHUNK], F32, name="wgo_rest")
+
+        nc.sync.dma_start(lists[TARGET][:], offs2)
+        nc.sync.dma_start(lists[SOURCE][:], offs)
+        for quad in range(QUADS):
+            nc.sync.dma_start(
+                out=tab_s[32 * quad : 32 * quad + 8, :].bitcast(I32),
+                in_=tab_scales[:, 4 * quad : 4 * quad + 4, :].bitcast(I32),
+            )
         load_wt(0, 0)
-        load_planes(ws_s_loaded, ws_scales)
+        for lst in (TARGET, SOURCE):
+            nc.vector.tensor_copy(picked_s[:, lst, :], tab_s[:].indirect(lists[lst][:]))
+        for window in windows[3:]:
+            nc.vector.memset(window[:].bitcast(I32), 0)
         load_wt(1, 0)
-        load_ws(0)
-        gather_scales()
-        lower_planes(0, EARLY)
+        nc.sync.dma_start(out=tab_w[:], in_=tab_words[0].rearrange("p t d -> p (t d)").bitcast(I32))
         load_wt(0, 1)
-        load_wt(1, 1)
+        load_planes(ws_s_loaded, ws_scales)
+        load_ws(0)
+        for quad in range(QUADS):
+            nc.sync.dma_start(
+                out=lowered_s[32 * quad : 32 * quad + 4, :, :].bitcast(I32),
+                in_=picked_s[32 * quad + 4 : 32 * quad + 8, :, :].bitcast(I32),
+            )
+        load_wt(1, 1, 0, PASS // 2)
+        load_wt(1, 1, PASS // 2, PASS)
         load_ws(1)
         nc.sync.dma_start(out=sm_t[:], in_=sm.rearrange("(g p t) -> p g t", g=2, t=PACK))
-        nc.sync.dma_start(out=wd8_w[:], in_=wd8_words.rearrange("a p n i -> p a (n i)").bitcast(I32))
-        nc.sync.dma_start(out=wd4_w[:].bitcast(I32), in_=wd4_words.rearrange("a p n -> p a n").bitcast(I32))
+        nc.sync.dma_start(out=wd8_w[:].bitcast(I32), in_=wd8_words.rearrange("a p n i -> p a (n i)").bitcast(I32))
         load_planes(wd8_s, wd8_scales)
+        nc.sync.dma_start(out=wd4_w[:].bitcast(I32), in_=wd4_words.rearrange("a p n -> p a n").bitcast(I32))
         load_planes(wd4_s, wd4_scales)
         with nc.allow_non_contiguous_dma(reason="one bias value to a partition"):
             nc.sync.dma_start(out=b_t[:], in_=b.rearrange("(c p) -> p c", p=P))
-        nc.sync.dma_start(out=wgo_t[:, 0:CHUNK], in_=wgo[:, 0:CHUNK])
-        lower_planes(EARLY, J)
-        nc.sync.dma_start(out=wgo_t[:, CHUNK:J], in_=wgo[:, CHUNK:J])
+        nc.sync.dma_start(out=wgo_first[:], in_=wgo[:, 0:CHUNK])
+        nc.sync.dma_start(out=wgo_rest[:], in_=wgo[:, CHUNK:J])
+        v_s = [picked_s, lowered_s]
 
-        picked_w = {}
         v_w = {}
 
-        def entries(lst, chunk):
-            return lists[lst][:, chunk * CHUNK // 16 : (chunk + 1) * CHUNK // 16]
+        def entries(lst, first, count=1):
+            return lists[lst][:, first * CHUNK // 16 : (first + count) * CHUNK // 16]
 
-        def gather_words(chunk):
+        def fetch_words(chunk):
+            picked = {}
             for lst in (TARGET, SOURCE):
                 name = "picked_w%d%d" % (chunk, lst)
                 if chunk in LATE_GATHERS:
-                    picked = placed.tile([P, CHUNK], U32, name=name, align_bytes=64, offset=LATE_GATHERS[chunk] + 4 * CHUNK * lst)
+                    picked[lst] = placed.tile([P, CHUNK], U32, name=name, align_bytes=64, offset=LATE_GATHERS[chunk] + 4 * CHUNK * lst)
                 else:
-                    picked = keep.tile([P, CHUNK], U32, name=name)
-                nc.vector.tensor_copy(picked[:], tab_w[:].bitcast(U32).indirect(entries(lst, chunk)))
-                picked_w[lst, chunk] = picked
-
-        def part_words(chunk):
+                    picked[lst] = keep.tile([P, CHUNK], U32, name=name)
+                nc.vector.tensor_copy(picked[lst][:], tab_w[:].bitcast(U32).indirect(entries(lst, chunk)))
             for lst in (TARGET, SOURCE):
                 parted = keep.tile([P, 2, 2 * CHUNK], U8, name="v_w%d%d" % (lst, chunk), align_bytes=64)
                 nc.vector.tensor_copy(
-                    out=parted[:].bitcast(U16), in_=picked_w[lst, chunk][:].bitcast(U16).rearrange("p (n d) -> p d n", d=2)
+                    out=parted[:].bitcast(U16), in_=picked[lst][:].bitcast(U16).rearrange("p (n d) -> p d n", d=2)
                 )
                 v_w[lst, chunk] = parted
 
@@ -181,7 +161,7 @@ def tile_list_msg_tanh_res_bias_kernel(
         def reorder_ws_scales():
             nc.vector.tensor_copy(
                 out=ws_s[:].rearrange("p a (g t mq mm) -> p (a g) mq t mm", g=2, t=PACK, mm=16),
-                in_=ws_s_loaded.rearrange("p a (g mq mm t) -> p (a g) mq t mm", g=2, t=PACK, mm=16),
+                in_=ws_s_loaded[:].rearrange("p a (g mq mm t) -> p (a g) mq t mm", g=2, t=PACK, mm=16),
             )
 
         def reorder_ws_words(half):
@@ -193,13 +173,15 @@ def tile_list_msg_tanh_res_bias_kernel(
             ws_w[half] = words
 
         def quantize_wt(a, half):
-            rounded = placed.tile(
-                [P, PACK, P, PACK], BF16, name="wt_bf16_%d%d" % (a, half), align_bytes=64, offset=AT_WT_BF16 + SLOT * (2 * half + a)
-            )
-            nc.scalar.copy(
-                out=rounded[:].rearrange("p t m i -> p m t i"),
-                in_=wt_loaded[a, half][:].rearrange("p i (m t) -> p m t i", t=PACK),
-            )
+            if (a, half) == (0, 1):
+                rounded = placed.tile([P, PACK, P, PACK], BF16, name="wt_bf16_01", align_bytes=64, offset=AT_ROUNDED)
+            else:
+                rounded = keep.tile([P, PACK, P, PACK], BF16, name="wt_bf16_%d%d" % (a, half), align_bytes=64)
+            for lo, hi, loaded in wt_loaded[a, half]:
+                nc.scalar.copy(
+                    out=rounded[:, :, lo // PACK : hi // PACK, :].rearrange("p t m i -> p m t i"),
+                    in_=loaded[:].rearrange("p i (m t) -> p m t i", t=PACK),
+                )
             words = keep.tile([P, PASS], U32, name="wt_w%d%d" % (a, half), align_bytes=64)
             plane = keep.tile([P, PASS], U8, name="wt_s%d%d" % (a, half), align_bytes=64)
             nc.vector.quantize_mx(out=words[:].bitcast(FP8X4), scales=plane[:], in_=rounded[:].rearrange("p t m i -> p (t m i)"))
@@ -208,53 +190,47 @@ def tile_list_msg_tanh_res_bias_kernel(
 
         h_w = {}
         h_s = {}
-        sums = {}
 
         def first_product(chunk, half, group):
-            bank = psum_a.tile([P, PACK * P], F32, name="bank_a", tag="bank_a")
-            sums[chunk, half, group] = bank
-            edge = chunk * CHUNK + group * P
-            passes = [(lst, a, t) for lst in (TARGET, SOURCE) for a in range(2) for t in range(PACK)]
+            turn = GROUPS * UNITS.index((chunk, half)) + group
+            bank = psum.tile([P, PACK * P], F32, name="a%d%d%d" % (chunk, half, group), offset=BANK * (turn % BANKS_A))
+            if (chunk, half) in ON_VECTOR:
+                first, width, outputs = group * P, P, range(PACK)
+            else:
+                first, width, outputs = 0, CHUNK, range(2 * group, 2 * group + 2)
+            edge = chunk * CHUNK + first
+            passes = [(lst, a, t) for lst, a in (((TARGET, 0), (TARGET, 1), (SOURCE, 0), (SOURCE, 1)), ((TARGET, 0), (SOURCE, 0), (SOURCE, 1), (TARGET, 1)))[half] for t in outputs]
             for n, (lst, a, t) in enumerate(passes):
                 cols = slice(P * t, P * (t + 1))
+                at = width * (t - outputs[0])
                 if lst == TARGET:
                     words, plane = wt_w[a, half][:, cols], wt_s[a, half][:, cols]
                 else:
                     words, plane = ws_w[half][:, a, cols], ws_s[:, a, PASS * half + P * t : PASS * half + P * (t + 1)]
                 nc.tensor.matmul_mx(
-                    out=bank[:, cols],
+                    out=bank[:, at : at + width],
                     lhsT=words.bitcast(FP8X4),
                     lhsT_scale=plane,
-                    rhs=v_w[lst, chunk][:, a, 2 * P * group : 2 * P * (group + 1)].bitcast(FP4X4),
-                    rhs_scale=v_s[lst, a][:, edge : edge + P],
+                    rhs=v_w[lst, chunk][:, a, 2 * first : 2 * (first + width)].bitcast(FP4X4),
+                    rhs_scale=v_s[a][:, lst, edge : edge + width],
                     start=(n == 0),
                     stop=(n == len(passes) - 1),
                 )
+            return bank
 
         def make_h(chunk, half):
-            if (chunk, half) == (0, 0):
-                tanh = placed.tile([P, GROUPS, PACK * P], F32, name="tanh00", align_bytes=64, offset=at_wt(1, 1))
+            slot = SLOT * UNITS.index((chunk, half))
+            if (chunk, half) in ON_VECTOR:
+                tanh = placed.tile([P, GROUPS, PACK * P], F32, name="tanh%d%d" % (chunk, half), align_bytes=64, offset=slot)
             else:
                 tanh = ring.tile([P, GROUPS, PACK * P], F32, name="tanh", tag="tanh", bufs=3)
             if (chunk, half) == (0, 1):
                 h = placed.tile([P, CHUNK, PACK], BF16, name="h01", align_bytes=64, offset=AT_FIRST_H)
             else:
                 h = ring.tile([P, CHUNK, PACK], BF16, name="h", tag="h", bufs=3, align_bytes=64)
-            on_scalar = [group for group in range(GROUPS) if (chunk, half, group) not in ON_VECTOR]
-            if on_scalar:
-                if half == 1:
-                    scaled = placed.tile(
-                        [P, PACK, CHUNK], BF16, name="scaled%d1" % chunk, align_bytes=64, offset=AT_SCALED + SLOT * (chunk - 1)
-                    )
-                else:
-                    scaled = ring.tile([P, PACK, CHUNK], BF16, name="scaled", tag="scaled")
             for group in range(GROUPS):
-                if (chunk, half, group) not in sums:
-                    first_product(chunk, half, group)
-                bank = sums[chunk, half, group]
-                if group in on_scalar:
-                    nc.scalar.activation(out=tanh[:, group, :], in_=bank[:], func=ACT.Tanh)
-                else:
+                bank = first_product(chunk, half, group)
+                if (chunk, half) in ON_VECTOR:
                     side_by_side = tanh[:, group, :].rearrange("p (n t) -> p n t", t=PACK)
                     nc.scalar.activation(out=side_by_side, in_=bank[:].rearrange("p (t n) -> p n t", t=PACK), func=ACT.Tanh)
                     nc.vector.tensor_tensor(
@@ -263,86 +239,83 @@ def tile_list_msg_tanh_res_bias_kernel(
                         in1=sm_t[:, half, :].unsqueeze(1).to_broadcast([P, P, PACK]),
                         op=MULT,
                     )
-            if on_scalar:
-                edges = slice(P * on_scalar[0], P * (on_scalar[-1] + 1))
+                else:
+                    nc.scalar.activation(out=tanh[:, group, :], in_=bank[:], func=ACT.Tanh)
+            if (chunk, half) not in ON_VECTOR:
+                scaled = placed.tile(
+                    [P, PACK, CHUNK], BF16, name="scaled%d%d" % (chunk, half), align_bytes=64, offset=slot
+                )
                 for t in range(PACK):
                     nc.scalar.activation(
-                        out=scaled[:, t, edges].rearrange("p (g n) -> p g n", n=P),
-                        in_=tanh[:, on_scalar[0] : on_scalar[-1] + 1, P * t : P * (t + 1)],
+                        out=scaled[:, t, :],
+                        in_=tanh[:, t // 2, CHUNK * (t % 2) : CHUNK * (t % 2 + 1)],
                         func=ACT.Copy,
                         scale=sm_t[:, half, t : t + 1],
                     )
-                nc.scalar.copy(out=h[:, edges, :], in_=scaled[:, :, edges].rearrange("p t n -> p n t"))
+                nc.scalar.copy(out=h[:], in_=scaled[:].rearrange("p t n -> p n t"))
             words = keep.tile([P, CHUNK], U32, name="h_w%d%d" % (chunk, half), align_bytes=64)
             plane = keep.tile([P, CHUNK], U8, name="h_s%d%d" % (chunk, half), align_bytes=64)
             nc.vector.quantize_mx(out=words[:].bitcast(FP8X4), scales=plane[:], in_=h[:].rearrange("p n t -> p (n t)"))
             h_w[chunk, half] = words
             h_s[chunk, half] = plane
 
-        def send(chunk, c):
-            bank = psum_y.tile([P, CHUNK], F32, name="bank_y", tag="bank_y")
+        def send(chunks, c, at_bank, at_y=None):
+            width = CHUNK * len(chunks)
+            name = "%d%d" % (chunks[0], c)
+            bank = psum.tile([P, width], F32, name="b" + name, offset=BANK * at_bank)
             rows = slice(P * c, P * (c + 1))
-            for half in (1, 0):
-                nc.tensor.matmul_mx(
-                    out=bank[:],
-                    lhsT=wd8_w[:, half, rows].bitcast(FP8X4),
-                    lhsT_scale=wd8_s[:, half, rows],
-                    rhs=h_w[chunk, half][:].bitcast(FP8X4),
-                    rhs_scale=h_s[chunk, half][:],
-                    start=(half == 1),
-                    stop=False,
-                )
-                for group in range(GROUPS):
-                    cols = slice(P * group, P * (group + 1))
-                    nc.tensor.matmul_mx(
-                        out=bank[:, cols],
-                        lhsT=wd4_w[:, half, 2 * P * c : 2 * P * (c + 1)].bitcast(FP4X4),
-                        lhsT_scale=wd4_s[:, half, rows],
-                        rhs=h_w[chunk, half][:, cols].bitcast(FP8X4),
-                        rhs_scale=h_s[chunk, half][:, cols],
-                        start=False,
-                        stop=(half == 0 and group == GROUPS - 1),
-                    )
-            if chunk < CHUNKS - 1 and c == KEPT_BACK[chunk]:
-                y = placed.tile([P, CHUNK], F32, name="y_kept%d" % chunk, align_bytes=64, offset=AT_SCALED + SLOT * chunk)
+            for n, chunk in enumerate(chunks):
+                for half in (1, 0):
+                    for wd_w, wd_plane, fmt in ((wd8_w[:, half, PACK * P * c : PACK * P * (c + 1)], wd8_s, FP8X4), (wd4_w[:, half, 2 * P * c : 2 * P * (c + 1)], wd4_s, FP4X4)):
+                        nc.tensor.matmul_mx(
+                            out=bank[:, CHUNK * n : CHUNK * (n + 1)],
+                            lhsT=wd_w.bitcast(fmt),
+                            lhsT_scale=wd_plane[:, half, rows],
+                            rhs=h_w[chunk, half][:].bitcast(FP8X4),
+                            rhs_scale=h_s[chunk, half][:],
+                            start=(half == 1 and fmt is FP8X4),
+                            stop=(half == 0 and fmt is FP4X4),
+                        )
+            if at_y is None:
+                y = keep.tile([P, width], F32, name="y" + name)
             else:
-                y = ring.tile([P, CHUNK], F32, name="y", tag="y", bufs=6)
+                y = placed.tile([P, width], F32, name="y" + name, align_bytes=64, offset=at_y)
             nc.scalar.activation(out=y[:], in_=bank[:], func=ACT.Identity, bias=b_t[:, c : c + 1])
             nc.vector.tensor_tensor(
-                windows[c][:].indirect(entries(TARGET, chunk)), y[:], wgo_t[:, CHUNK * chunk : CHUNK * (chunk + 1)], MULT
+                windows[c][:].indirect(entries(TARGET, chunks[0], len(chunks))),
+                y[:],
+                wgo_first[:] if chunks[0] == 0 else wgo_rest[:, CHUNK * (chunks[0] - 1) : CHUNK * (chunks[0] - 1) + width],
+                MULT,
             )
-            if chunk == CHUNKS - 1:
+            if chunks[-1] == CHUNKS - 1:
                 nc.sync.dma_start(out=out[rows, :], in_=windows[c][:])
 
-        gather_words(0)
-        gather_words(1)
-        part_words(0)
+        fetch_words(0)
         quantize_wt(0, 0)
         quantize_wt(1, 0)
         reorder_ws_scales()
         reorder_ws_words(0)
-        part_words(1)
+        fetch_words(1)
         quantize_wt(0, 1)
         quantize_wt(1, 1)
         reorder_ws_words(1)
-        for a, half in ((1, 0), (0, 1)):
-            window = placed.tile([P, T], F32, name="window%d" % len(windows), align_bytes=64, offset=at_wt(a, half))
-            nc.vector.memset(window[:].bitcast(I32), 0)
-            windows.append(window)
         make_h(0, 0)
-        for group in range(GROUPS):
-            first_product(1, 0, group)
         make_h(0, 1)
-        for chunk in LATE_GATHERS:
-            gather_words(chunk)
-            part_words(chunk)
+        make_h(1, 0)
+        fetch_words(2)
+        fetch_words(3)
 
-        for chunk in range(CHUNKS - 1):
-            for c in range(KEPT_BACK[chunk]):
-                send(chunk, c)
-            make_h(chunk + 1, 0)
+        last = CHUNKS - 1
+        for chunk in range(last):
+            at = [SLOT * UNITS.index((chunk + 1, half)) for half in range(2)]
+            if chunk > 0:
+                make_h(chunk + 1, 0)
+            send([chunk], 0, BANKS_A, at[0])
+            send([chunk], 1, BANKS_A + 1, at[0] + 4 * CHUNK)
             make_h(chunk + 1, 1)
-            for c in range(KEPT_BACK[chunk], TILES):
-                send(chunk, c)
-        for c in range(TILES):
-            send(CHUNKS - 1, c)
+            send([chunk], 2, BANKS_A, at[1])
+            if chunk + 1 < last:
+                send([chunk], 3, BANKS_A + 1, at[1] + 4 * CHUNK)
+        for c in range(TILES - 1):
+            send([last], c, BANKS_A + (c + 1) % 2)
+        send([last - 1, last], TILES - 1, (GROUPS * len(UNITS) - 1) % BANKS_A)

@@ -35,6 +35,7 @@ KB = 1024
 AT_ROUNDED = SLOT * len(UNITS)
 AT_FIRST_H = AT_ROUNDED + 4 * KB
 LATE_GATHERS = {2: AT_ROUNDED, 3: AT_FIRST_H}
+PAD = 4
 BANK = 2048
 BANKS_A = 6
 
@@ -51,20 +52,23 @@ def tile_list_msg_tanh_res_bias_kernel(
 
         lists = [keep.tile([P, J // 16], U16, name="list_source"), keep.tile([P, J // 16], U16, name="list_target")]
         tab_w = keep.tile([P, T], I32, name="tab_w", align_bytes=64)
-        tab_s = keep.tile([P, T], U8, name="tab_s", align_bytes=64)
-        ws_s_loaded = keep.tile([P, 2, R], U8, name="ws_s_loaded", align_bytes=64)
-        wd_s = keep.tile([P, 2, 2, N], U8, name="wd_s", align_bytes=64)
+        tab_s = keep.tile([P, T + PAD], U8, name="tab_s", align_bytes=64)
+        ws_s_tile = keep.tile([P, 2 * R + PAD], U8, name="ws_s_tile", align_bytes=64)
+        ws_s_loaded = ws_s_tile[:, 0 : 2 * R].rearrange("p (a r) -> p a r", a=2)
+        wd_s_tile = keep.tile([P, 4 * N + PAD], U8, name="wd_s_tile", align_bytes=64)
+        wd_s = wd_s_tile[:, 0 : 4 * N].rearrange("p (w a n) -> p w a n", w=2, a=2)
         wd8_s, wd4_s = wd_s[:, 0, :, :], wd_s[:, 1, :, :]
         picked_s = keep.tile([P, 2, J], U8, name="picked_s", align_bytes=64)
-        lowered_s = keep.tile([P, 2, J], U8, name="lowered_s", align_bytes=64)
+        lowered_tile = keep.tile([P, 2 * J + PAD], U8, name="lowered_tile", align_bytes=64)
+        lowered_s = lowered_tile[:, 0 : 2 * J].rearrange("p (l j) -> p l j", l=2)
         windows = [keep.tile([P, T], F32, name="window%d" % c, align_bytes=64) for c in range(TILES)]
 
         nc.vector.memset(tab_s[:].bitcast(I32), 0)
-        nc.vector.memset(ws_s_loaded[:].rearrange("p a r -> p (a r)").bitcast(I32), 0)
-        nc.vector.memset(lowered_s[:].rearrange("p l j -> p (l j)").bitcast(I32), 0)
-        nc.vector.memset(wd_s[:].rearrange("p w a n -> p (w a n)").bitcast(I32), 0)
-        for window in windows[:3]:
-            nc.vector.memset(window[:].bitcast(I32), 0)
+        nc.vector.memset(ws_s_tile[:].bitcast(I32), 0)
+        nc.vector.memset(lowered_tile[:].bitcast(I32), 0)
+        nc.vector.memset(wd_s_tile[:].bitcast(I32), 0)
+        for window in windows:
+            nc.gpsimd.memset(window[:].bitcast(I32), 0)
 
         wt_loaded = {}
         ws_loaded = {}
@@ -100,17 +104,14 @@ def tile_list_msg_tanh_res_bias_kernel(
         nc.sync.dma_start(lists[SOURCE][:], offs)
         for quad in range(QUADS):
             nc.sync.dma_start(
-                out=tab_s[32 * quad : 32 * quad + 8, :].bitcast(I32),
+                out=tab_s[32 * quad : 32 * quad + 8, 0:T].bitcast(I32),
                 in_=tab_scales[:, 4 * quad : 4 * quad + 4, :].bitcast(I32),
             )
         load_wt(0, 0)
         for lst in (TARGET, SOURCE):
-            nc.vector.tensor_copy(picked_s[:, lst, :], tab_s[:].indirect(lists[lst][:]))
-        for window in windows[3:]:
-            nc.vector.memset(window[:].bitcast(I32), 0)
-        load_wt(1, 0)
+            nc.vector.tensor_copy(picked_s[:, lst, :], tab_s[:, 0:T].indirect(lists[lst][:]))
         nc.sync.dma_start(out=tab_w[:], in_=tab_words[0].rearrange("p t d -> p (t d)").bitcast(I32))
-        load_wt(0, 1)
+        load_wt(1, 0)
         load_planes(ws_s_loaded, ws_scales)
         load_ws(0)
         for quad in range(QUADS):
@@ -118,6 +119,7 @@ def tile_list_msg_tanh_res_bias_kernel(
                 out=lowered_s[32 * quad : 32 * quad + 4, :, :].bitcast(I32),
                 in_=picked_s[32 * quad + 4 : 32 * quad + 8, :, :].bitcast(I32),
             )
+        load_wt(0, 1)
         load_wt(1, 1, 0, PASS // 2)
         load_wt(1, 1, PASS // 2, PASS)
         load_ws(1)
@@ -161,7 +163,7 @@ def tile_list_msg_tanh_res_bias_kernel(
         def reorder_ws_scales():
             nc.vector.tensor_copy(
                 out=ws_s[:].rearrange("p a (g t mq mm) -> p (a g) mq t mm", g=2, t=PACK, mm=16),
-                in_=ws_s_loaded[:].rearrange("p a (g mq mm t) -> p (a g) mq t mm", g=2, t=PACK, mm=16),
+                in_=ws_s_loaded.rearrange("p a (g mq mm t) -> p (a g) mq t mm", g=2, t=PACK, mm=16),
             )
 
         def reorder_ws_words(half):
@@ -173,12 +175,13 @@ def tile_list_msg_tanh_res_bias_kernel(
             ws_w[half] = words
 
         def quantize_wt(a, half):
-            if (a, half) == (0, 1):
-                rounded = placed.tile([P, PACK, P, PACK], BF16, name="wt_bf16_01", align_bytes=64, offset=AT_ROUNDED)
+            if (a, half) == (1, 0):
+                rounded = placed.tile([P, PACK, P, PACK], BF16, name="wt_bf16_10", align_bytes=64, offset=AT_ROUNDED)
             else:
                 rounded = keep.tile([P, PACK, P, PACK], BF16, name="wt_bf16_%d%d" % (a, half), align_bytes=64)
             for lo, hi, loaded in wt_loaded[a, half]:
-                nc.scalar.copy(
+                round_copy = nc.vector.tensor_copy if (a, half) in ((0, 1), (1, 1)) else nc.scalar.copy
+                round_copy(
                     out=rounded[:, :, lo // PACK : hi // PACK, :].rearrange("p t m i -> p m t i"),
                     in_=loaded[:].rearrange("p i (m t) -> p m t i", t=PACK),
                 )
@@ -292,17 +295,17 @@ def tile_list_msg_tanh_res_bias_kernel(
 
         fetch_words(0)
         quantize_wt(0, 0)
-        quantize_wt(1, 0)
+        fetch_words(1)
         reorder_ws_scales()
         reorder_ws_words(0)
-        fetch_words(1)
+        quantize_wt(1, 0)
+        fetch_words(2)
         quantize_wt(0, 1)
         quantize_wt(1, 1)
         reorder_ws_words(1)
         make_h(0, 0)
         make_h(0, 1)
         make_h(1, 0)
-        fetch_words(2)
         fetch_words(3)
 
         last = CHUNKS - 1

@@ -27,17 +27,17 @@ TILES = N // P
 SOURCE, TARGET = 0, 1
 
 UNITS = [(0, 0), (1, 0), (0, 1), (1, 1), (2, 0), (2, 1), (3, 0), (3, 1)]
+ON_VECTOR = {(1, 0), (0, 1)}
+PASSES = (((TARGET, 0), (TARGET, 1), (SOURCE, 0), (SOURCE, 1)), ((TARGET, 0), (SOURCE, 0), (SOURCE, 1), (TARGET, 1)))
+PAD = 4
+BANK = 2048
+BANKS = 8
 
-ON_VECTOR = {(0, 0), (0, 1), (1, 0)}
-
-SLOT = 4 * PACK * CHUNK
 KB = 1024
+SLOT = 4 * KB
 AT_ROUNDED = SLOT * len(UNITS)
 AT_FIRST_H = AT_ROUNDED + 4 * KB
 LATE_GATHERS = {2: AT_ROUNDED, 3: AT_FIRST_H}
-PAD = 4
-BANK = 2048
-BANKS_A = 6
 
 
 def tile_list_msg_tanh_res_bias_kernel(
@@ -46,7 +46,7 @@ def tile_list_msg_tanh_res_bias_kernel(
     nc = tc.nc
     with ExitStack() as ctx:
         keep = ctx.enter_context(tc.tile_pool(name="keep", bufs=1))
-        ring = ctx.enter_context(tc.tile_pool(name="ring", bufs=2))
+        ring = ctx.enter_context(tc.tile_pool(name="ring", bufs=3))
         placed = ctx.enter_context(tc.tile_pool(name="placed", bufs=1))
         psum = ctx.enter_context(tc.psum_pool(name="psum", bufs=1))
 
@@ -56,17 +56,22 @@ def tile_list_msg_tanh_res_bias_kernel(
         ws_s_tile = keep.tile([P, 2 * R + PAD], U8, name="ws_s_tile", align_bytes=64)
         ws_s_loaded = ws_s_tile[:, 0 : 2 * R].rearrange("p (a r) -> p a r", a=2)
         wd_s_tile = keep.tile([P, 4 * N + PAD], U8, name="wd_s_tile", align_bytes=64)
-        wd_s = wd_s_tile[:, 0 : 4 * N].rearrange("p (w a n) -> p w a n", w=2, a=2)
-        wd8_s, wd4_s = wd_s[:, 0, :, :], wd_s[:, 1, :, :]
+        wd8_s = wd_s_tile[:, 0 : 2 * N].rearrange("p (a n) -> p a n", a=2)
+        wd4_s = wd_s_tile[:, 2 * N : 4 * N].rearrange("p (a n) -> p a n", a=2)
         picked_s = keep.tile([P, 2, J], U8, name="picked_s", align_bytes=64)
         lowered_tile = keep.tile([P, 2 * J + PAD], U8, name="lowered_tile", align_bytes=64)
         lowered_s = lowered_tile[:, 0 : 2 * J].rearrange("p (l j) -> p l j", l=2)
+        v_s = [picked_s, lowered_s]
         windows = [keep.tile([P, T], F32, name="window%d" % c, align_bytes=64) for c in range(TILES)]
+        sm_t = keep.tile([P, 2, PACK], F32, name="sm_t")
+        b_t = keep.tile([P, TILES], F32, name="b_t")
+        wd8_w = keep.tile([P, 2, PACK * N], U8, name="wd8_w", align_bytes=64)
+        wd4_w = keep.tile([P, 2, 2 * N], U8, name="wd4_w", align_bytes=64)
+        wgo_first = keep.tile([P, CHUNK], F32, name="wgo_first")
+        wgo_rest = keep.tile([P, J - CHUNK], F32, name="wgo_rest")
 
-        nc.vector.memset(tab_s[:].bitcast(I32), 0)
-        nc.vector.memset(ws_s_tile[:].bitcast(I32), 0)
-        nc.vector.memset(lowered_tile[:].bitcast(I32), 0)
-        nc.vector.memset(wd_s_tile[:].bitcast(I32), 0)
+        for planes in (tab_s, ws_s_tile, lowered_tile, wd_s_tile):
+            nc.vector.memset(planes[:].bitcast(I32), 0)
         for window in windows:
             nc.gpsimd.memset(window[:].bitcast(I32), 0)
 
@@ -74,8 +79,7 @@ def tile_list_msg_tanh_res_bias_kernel(
         ws_loaded = {}
 
         def load_wt(a, half, lo=0, hi=PASS):
-            name = "wt_loaded%d%d_%d" % (a, half, lo)
-            loaded = keep.tile([P, PACK, hi - lo], F32, name=name, align_bytes=64)
+            loaded = keep.tile([P, PACK, hi - lo], F32, name="wt_loaded%d%d_%d" % (a, half, lo), align_bytes=64)
             rows = wt[PASS * a : PASS * (a + 1), PASS * half + lo : PASS * half + hi]
             nc.sync.dma_start(out=loaded[:], in_=rows.rearrange("(p i) r -> p i r", i=PACK))
             wt_loaded.setdefault((a, half), []).append((lo, hi, loaded))
@@ -93,20 +97,13 @@ def tile_list_msg_tanh_res_bias_kernel(
                     in_=scales[:, 4 * quad : 4 * quad + 4, :].rearrange("a q n -> q a n").bitcast(I32),
                 )
 
-        sm_t = keep.tile([P, 2, PACK], F32, name="sm_t")
-        b_t = keep.tile([P, TILES], F32, name="b_t")
-        wd8_w = keep.tile([P, 2, PACK * N], U8, name="wd8_w", align_bytes=64)
-        wd4_w = keep.tile([P, 2, 2 * N], U8, name="wd4_w", align_bytes=64)
-        wgo_first = keep.tile([P, CHUNK], F32, name="wgo_first")
-        wgo_rest = keep.tile([P, J - CHUNK], F32, name="wgo_rest")
-
         nc.sync.dma_start(lists[TARGET][:], offs2)
         nc.sync.dma_start(lists[SOURCE][:], offs)
         for quad in range(QUADS):
             nc.sync.dma_start(
-                out=tab_s[32 * quad : 32 * quad + 8, 0:T].bitcast(I32),
-                in_=tab_scales[:, 4 * quad : 4 * quad + 4, :].bitcast(I32),
+                out=tab_s[32 * quad : 32 * quad + 4, 0:T].bitcast(I32), in_=tab_scales[0, 4 * quad : 4 * quad + 4, :].bitcast(I32)
             )
+        nc.sync.dma_start(out=tab_s[4:P:8, 0:T].bitcast(I32), in_=tab_scales[1].bitcast(I32))
         load_wt(0, 0)
         for lst in (TARGET, SOURCE):
             nc.vector.tensor_copy(picked_s[:, lst, :], tab_s[:, 0:T].indirect(lists[lst][:]))
@@ -114,16 +111,15 @@ def tile_list_msg_tanh_res_bias_kernel(
         load_wt(1, 0)
         load_planes(ws_s_loaded, ws_scales)
         load_ws(0)
-        for quad in range(QUADS):
-            nc.sync.dma_start(
-                out=lowered_s[32 * quad : 32 * quad + 4, :, :].bitcast(I32),
-                in_=picked_s[32 * quad + 4 : 32 * quad + 8, :, :].bitcast(I32),
-            )
         load_wt(0, 1)
+        for row in range(4):
+            nc.sync.dma_start(
+                out=lowered_s[row:P:32, :, :].bitcast(I32), in_=picked_s[8 * row + 4 : P : 32, :, :].bitcast(I32)
+            )
+        nc.sync.dma_start(out=sm_t[:], in_=sm.rearrange("(g p t) -> p g t", g=2, t=PACK))
         load_wt(1, 1, 0, PASS // 2)
         load_wt(1, 1, PASS // 2, PASS)
         load_ws(1)
-        nc.sync.dma_start(out=sm_t[:], in_=sm.rearrange("(g p t) -> p g t", g=2, t=PACK))
         nc.sync.dma_start(out=wd8_w[:].bitcast(I32), in_=wd8_words.rearrange("a p n i -> p a (n i)").bitcast(I32))
         load_planes(wd8_s, wd8_scales)
         nc.sync.dma_start(out=wd4_w[:].bitcast(I32), in_=wd4_words.rearrange("a p n -> p a n").bitcast(I32))
@@ -132,7 +128,6 @@ def tile_list_msg_tanh_res_bias_kernel(
             nc.sync.dma_start(out=b_t[:], in_=b.rearrange("(c p) -> p c", p=P))
         nc.sync.dma_start(out=wgo_first[:], in_=wgo[:, 0:CHUNK])
         nc.sync.dma_start(out=wgo_rest[:], in_=wgo[:, CHUNK:J])
-        v_s = [picked_s, lowered_s]
 
         v_w = {}
 
@@ -144,12 +139,12 @@ def tile_list_msg_tanh_res_bias_kernel(
             for lst in (TARGET, SOURCE):
                 name = "picked_w%d%d" % (chunk, lst)
                 if chunk in LATE_GATHERS:
-                    picked[lst] = placed.tile([P, CHUNK], U32, name=name, align_bytes=64, offset=LATE_GATHERS[chunk] + 4 * CHUNK * lst)
+                    picked[lst] = placed.tile([P, CHUNK], U32, name=name, align_bytes=64, offset=LATE_GATHERS[chunk] + KB * lst)
                 else:
                     picked[lst] = keep.tile([P, CHUNK], U32, name=name)
                 nc.vector.tensor_copy(picked[lst][:], tab_w[:].bitcast(U32).indirect(entries(lst, chunk)))
             for lst in (TARGET, SOURCE):
-                parted = keep.tile([P, 2, 2 * CHUNK], U8, name="v_w%d%d" % (lst, chunk), align_bytes=64)
+                parted = keep.tile([P, 2, 2 * CHUNK], U8, name="v_w%d%d" % (chunk, lst), align_bytes=64)
                 nc.vector.tensor_copy(
                     out=parted[:].bitcast(U16), in_=picked[lst][:].bitcast(U16).rearrange("p (n d) -> p d n", d=2)
                 )
@@ -175,12 +170,13 @@ def tile_list_msg_tanh_res_bias_kernel(
             ws_w[half] = words
 
         def quantize_wt(a, half):
+            name = "wt_bf16_%d%d" % (a, half)
             if (a, half) == (1, 0):
-                rounded = placed.tile([P, PACK, P, PACK], BF16, name="wt_bf16_10", align_bytes=64, offset=AT_ROUNDED)
+                rounded = placed.tile([P, PACK, P, PACK], BF16, name=name, align_bytes=64, offset=AT_ROUNDED)
             else:
-                rounded = keep.tile([P, PACK, P, PACK], BF16, name="wt_bf16_%d%d" % (a, half), align_bytes=64)
+                rounded = keep.tile([P, PACK, P, PACK], BF16, name=name, align_bytes=64)
             for lo, hi, loaded in wt_loaded[a, half]:
-                round_copy = nc.vector.tensor_copy if (a, half) in ((0, 1), (1, 1)) else nc.scalar.copy
+                round_copy = nc.vector.tensor_copy if (a, half) == (1, 1) else nc.scalar.copy
                 round_copy(
                     out=rounded[:, :, lo // PACK : hi // PACK, :].rearrange("p t m i -> p m t i"),
                     in_=loaded[:].rearrange("p i (m t) -> p m t i", t=PACK),
@@ -191,107 +187,128 @@ def tile_list_msg_tanh_res_bias_kernel(
             wt_w[a, half] = words
             wt_s[a, half] = plane
 
+        sums = {}
+        tanh = {}
         h_w = {}
         h_s = {}
 
-        def first_product(chunk, half, group):
-            turn = GROUPS * UNITS.index((chunk, half)) + group
-            bank = psum.tile([P, PACK * P], F32, name="a%d%d%d" % (chunk, half, group), offset=BANK * (turn % BANKS_A))
-            if (chunk, half) in ON_VECTOR:
-                first, width, outputs = group * P, P, range(PACK)
-            else:
-                first, width, outputs = 0, CHUNK, range(2 * group, 2 * group + 2)
-            edge = chunk * CHUNK + first
-            passes = [(lst, a, t) for lst, a in (((TARGET, 0), (TARGET, 1), (SOURCE, 0), (SOURCE, 1)), ((TARGET, 0), (SOURCE, 0), (SOURCE, 1), (TARGET, 1)))[half] for t in outputs]
-            for n, (lst, a, t) in enumerate(passes):
-                cols = slice(P * t, P * (t + 1))
-                at = width * (t - outputs[0])
-                if lst == TARGET:
-                    words, plane = wt_w[a, half][:, cols], wt_s[a, half][:, cols]
-                else:
-                    words, plane = ws_w[half][:, a, cols], ws_s[:, a, PASS * half + P * t : PASS * half + P * (t + 1)]
-                nc.tensor.matmul_mx(
-                    out=bank[:, at : at + width],
-                    lhsT=words.bitcast(FP8X4),
-                    lhsT_scale=plane,
-                    rhs=v_w[lst, chunk][:, a, 2 * first : 2 * (first + width)].bitcast(FP4X4),
-                    rhs_scale=v_s[a][:, lst, edge : edge + width],
-                    start=(n == 0),
-                    stop=(n == len(passes) - 1),
-                )
-            return bank
+        def bank_of(unit, part):
+            return BANK * ((2 * UNITS.index(unit) + part) % BANKS)
 
-        def make_h(chunk, half):
-            slot = SLOT * UNITS.index((chunk, half))
-            if (chunk, half) in ON_VECTOR:
-                tanh = placed.tile([P, GROUPS, PACK * P], F32, name="tanh%d%d" % (chunk, half), align_bytes=64, offset=slot)
+        def first_product(unit):
+            chunk, half = unit
+            for part in range(2):
+                bank = psum.tile([P, PASS], F32, name="a%d%d%d" % (chunk, half, part), offset=bank_of(unit, part))
+                sums[unit, part] = bank
+                if unit in ON_VECTOR:
+                    first, width, outputs = part * P, P, range(PACK)
+                else:
+                    first, width, outputs = 0, CHUNK, range(2 * part, 2 * part + 2)
+                edge = chunk * CHUNK + first
+                passes = [(lst, a, t) for lst, a in PASSES[half] for t in outputs]
+                for n, (lst, a, t) in enumerate(passes):
+                    cols = slice(P * t, P * (t + 1))
+                    if lst == TARGET:
+                        words, plane = wt_w[a, half][:, cols], wt_s[a, half][:, cols]
+                    else:
+                        words, plane = ws_w[half][:, a, cols], ws_s[:, a, PASS * half + P * t : PASS * half + P * (t + 1)]
+                    at = width * (t - outputs[0])
+                    nc.tensor.matmul_mx(
+                        out=bank[:, at : at + width],
+                        lhsT=words.bitcast(FP8X4),
+                        lhsT_scale=plane,
+                        rhs=v_w[lst, chunk][:, a, 2 * first : 2 * (first + width)].bitcast(FP4X4),
+                        rhs_scale=v_s[a][:, lst, edge : edge + width],
+                        start=(n == 0),
+                        stop=(n == len(passes) - 1),
+                    )
+
+        def make_tanh(unit):
+            if unit in ON_VECTOR:
+                values = placed.tile([P, 2, PASS], F32, name="tanh%d%d" % unit, align_bytes=64, offset=SLOT * UNITS.index(unit))
             else:
-                tanh = ring.tile([P, GROUPS, PACK * P], F32, name="tanh", tag="tanh", bufs=3)
-            if (chunk, half) == (0, 1):
+                values = ring.tile([P, 2, PASS], F32, name="tanh", tag="tanh")
+            for part in range(2):
+                bank = sums[unit, part]
+                if unit in ON_VECTOR:
+                    nc.scalar.activation(
+                        out=values[:, part, :].rearrange("p (n t) -> p n t", t=PACK),
+                        in_=bank[:].rearrange("p (t n) -> p n t", t=PACK),
+                        func=ACT.Tanh,
+                    )
+                else:
+                    nc.scalar.activation(out=values[:, part, :], in_=bank[:], func=ACT.Tanh)
+            tanh[unit] = values
+
+        def make_h(unit):
+            chunk, half = unit
+            if unit == (0, 1):
                 h = placed.tile([P, CHUNK, PACK], BF16, name="h01", align_bytes=64, offset=AT_FIRST_H)
             else:
-                h = ring.tile([P, CHUNK, PACK], BF16, name="h", tag="h", bufs=3, align_bytes=64)
-            for group in range(GROUPS):
-                bank = first_product(chunk, half, group)
-                if (chunk, half) in ON_VECTOR:
-                    side_by_side = tanh[:, group, :].rearrange("p (n t) -> p n t", t=PACK)
-                    nc.scalar.activation(out=side_by_side, in_=bank[:].rearrange("p (t n) -> p n t", t=PACK), func=ACT.Tanh)
+                h = ring.tile([P, CHUNK, PACK], BF16, name="h", tag="h", align_bytes=64)
+            if unit in ON_VECTOR:
+                for part in range(2):
                     nc.vector.tensor_tensor(
-                        out=h[:, P * group : P * (group + 1), :],
-                        in0=side_by_side,
+                        out=h[:, P * part : P * (part + 1), :],
+                        in0=tanh[unit][:, part, :].rearrange("p (n t) -> p n t", t=PACK),
                         in1=sm_t[:, half, :].unsqueeze(1).to_broadcast([P, P, PACK]),
                         op=MULT,
                     )
-                else:
-                    nc.scalar.activation(out=tanh[:, group, :], in_=bank[:], func=ACT.Tanh)
-            if (chunk, half) not in ON_VECTOR:
-                scaled = placed.tile(
-                    [P, PACK, CHUNK], BF16, name="scaled%d%d" % (chunk, half), align_bytes=64, offset=slot
-                )
+            else:
+                scaled = placed.tile([P, PACK, CHUNK], BF16, name="scaled%d%d" % unit, align_bytes=64, offset=SLOT * UNITS.index(unit))
                 for t in range(PACK):
                     nc.scalar.activation(
                         out=scaled[:, t, :],
-                        in_=tanh[:, t // 2, CHUNK * (t % 2) : CHUNK * (t % 2 + 1)],
+                        in_=tanh[unit][:, t // 2, CHUNK * (t % 2) : CHUNK * (t % 2 + 1)],
                         func=ACT.Copy,
                         scale=sm_t[:, half, t : t + 1],
                     )
-                nc.scalar.copy(out=h[:], in_=scaled[:].rearrange("p t n -> p n t"))
-            words = keep.tile([P, CHUNK], U32, name="h_w%d%d" % (chunk, half), align_bytes=64)
-            plane = keep.tile([P, CHUNK], U8, name="h_s%d%d" % (chunk, half), align_bytes=64)
+                nc.scalar.copy(
+                    out=h[:].rearrange("p (c i) t -> p c t i", i=4), in_=scaled[:].rearrange("p t (c i) -> p c t i", i=4)
+                )
+            words = keep.tile([P, CHUNK], U32, name="h_w%d%d" % unit, align_bytes=64)
+            plane = keep.tile([P, CHUNK], U8, name="h_s%d%d" % unit, align_bytes=64)
             nc.vector.quantize_mx(out=words[:].bitcast(FP8X4), scales=plane[:], in_=h[:].rearrange("p n t -> p (n t)"))
-            h_w[chunk, half] = words
-            h_s[chunk, half] = plane
+            h_w[unit] = words
+            h_s[unit] = plane
 
-        def send(chunks, c, at_bank, at_y=None):
-            width = CHUNK * len(chunks)
-            name = "%d%d" % (chunks[0], c)
-            bank = psum.tile([P, width], F32, name="b" + name, offset=BANK * at_bank)
+        def second_product(bank, chunk, c):
             rows = slice(P * c, P * (c + 1))
-            for n, chunk in enumerate(chunks):
-                for half in (1, 0):
-                    for wd_w, wd_plane, fmt in ((wd8_w[:, half, PACK * P * c : PACK * P * (c + 1)], wd8_s, FP8X4), (wd4_w[:, half, 2 * P * c : 2 * P * (c + 1)], wd4_s, FP4X4)):
-                        nc.tensor.matmul_mx(
-                            out=bank[:, CHUNK * n : CHUNK * (n + 1)],
-                            lhsT=wd_w.bitcast(fmt),
-                            lhsT_scale=wd_plane[:, half, rows],
-                            rhs=h_w[chunk, half][:].bitcast(FP8X4),
-                            rhs_scale=h_s[chunk, half][:],
-                            start=(half == 1 and fmt is FP8X4),
-                            stop=(half == 0 and fmt is FP4X4),
-                        )
+            for half in (1, 0):
+                for words, plane, fmt in (
+                    (wd8_w[:, half, PACK * P * c : PACK * P * (c + 1)], wd8_s, FP8X4),
+                    (wd4_w[:, half, 2 * P * c : 2 * P * (c + 1)], wd4_s, FP4X4),
+                ):
+                    nc.tensor.matmul_mx(
+                        out=bank,
+                        lhsT=words.bitcast(fmt),
+                        lhsT_scale=plane[:, half, rows],
+                        rhs=h_w[chunk, half][:].bitcast(FP8X4),
+                        rhs_scale=h_s[chunk, half][:],
+                        start=(half == 1 and fmt is FP8X4),
+                        stop=(half == 0 and fmt is FP4X4),
+                    )
+
+        def send(result, chunk, c, at_y):
+            width = result.shape[1]
+            name = "y%d%d" % (chunk, c)
             if at_y is None:
-                y = keep.tile([P, width], F32, name="y" + name)
+                y = keep.tile([P, width], F32, name=name)
             else:
-                y = placed.tile([P, width], F32, name="y" + name, align_bytes=64, offset=at_y)
-            nc.scalar.activation(out=y[:], in_=bank[:], func=ACT.Identity, bias=b_t[:, c : c + 1])
-            nc.vector.tensor_tensor(
-                windows[c][:].indirect(entries(TARGET, chunks[0], len(chunks))),
-                y[:],
-                wgo_first[:] if chunks[0] == 0 else wgo_rest[:, CHUNK * (chunks[0] - 1) : CHUNK * (chunks[0] - 1) + width],
-                MULT,
-            )
-            if chunks[-1] == CHUNKS - 1:
-                nc.sync.dma_start(out=out[rows, :], in_=windows[c][:])
+                y = placed.tile([P, width], F32, name=name, align_bytes=64, offset=at_y)
+            nc.scalar.activation(out=y[:], in_=result, func=ACT.Identity, bias=b_t[:, c : c + 1])
+            weight = wgo_first[:] if chunk == 0 else wgo_rest[:, CHUNK * (chunk - 1) : CHUNK * (chunk - 1) + width]
+            nc.vector.tensor_tensor(windows[c][:].indirect(entries(TARGET, chunk, width // CHUNK)), y[:], weight, MULT)
+            if CHUNK * chunk + width == J:
+                nc.sync.dma_start(out=out[P * c : P * (c + 1), :], in_=windows[c][:])
+
+        def send_tiles(chunk, tiles, at_bank, behind=None):
+            bank = psum.tile([P, CHUNK * len(tiles)], F32, name="b%d%d" % (chunk, tiles[0]), offset=at_bank)
+            for n, c in enumerate(tiles):
+                second_product(bank[:, CHUNK * n : CHUNK * (n + 1)], chunk, c)
+            for n, c in enumerate(tiles):
+                at_y = None if behind is None else SLOT * UNITS.index(behind) + KB * n
+                send(bank[:, CHUNK * n : CHUNK * (n + 1)], chunk, c, at_y)
 
         fetch_words(0)
         quantize_wt(0, 0)
@@ -303,22 +320,32 @@ def tile_list_msg_tanh_res_bias_kernel(
         quantize_wt(0, 1)
         quantize_wt(1, 1)
         reorder_ws_words(1)
-        make_h(0, 0)
-        make_h(0, 1)
-        make_h(1, 0)
+        first_product((0, 0))
+        make_tanh((0, 0))
+        make_h((0, 0))
+        first_product((0, 1))
+        make_tanh((0, 1))
+        make_h((0, 1))
+        first_product((1, 0))
+        make_tanh((1, 0))
+        make_h((1, 0))
         fetch_words(3)
 
         last = CHUNKS - 1
         for chunk in range(last):
-            at = [SLOT * UNITS.index((chunk + 1, half)) for half in range(2)]
-            if chunk > 0:
-                make_h(chunk + 1, 0)
-            send([chunk], 0, BANKS_A, at[0])
-            send([chunk], 1, BANKS_A + 1, at[0] + 4 * CHUNK)
-            make_h(chunk + 1, 1)
-            send([chunk], 2, BANKS_A, at[1])
+            first_product((chunk + 1, 1))
+            send_tiles(chunk, (0, 1), bank_of((chunk + 1, 0), 1), (chunk + 1, 0))
+            make_tanh((chunk + 1, 1))
+            make_h((chunk + 1, 1))
             if chunk + 1 < last:
-                send([chunk], 3, BANKS_A + 1, at[1] + 4 * CHUNK)
+                first_product((chunk + 2, 0))
+                send_tiles(chunk, (2, 3), bank_of((chunk + 1, 1), 1), (chunk + 1, 1))
+                make_tanh((chunk + 2, 0))
+                make_h((chunk + 2, 0))
+        send_tiles(last - 1, (2,), bank_of((last, 1), 1), (last, 1))
         for c in range(TILES - 1):
-            send([last], c, BANKS_A + (c + 1) % 2)
-        send([last - 1, last], TILES - 1, (GROUPS * len(UNITS) - 1) % BANKS_A)
+            send_tiles(last, (c,), BANK * c)
+        bank = psum.tile([P, 2 * CHUNK], F32, name="b_last", offset=bank_of((last, 1), 0))
+        for n, chunk in enumerate((last - 1, last)):
+            second_product(bank[:, CHUNK * n : CHUNK * (n + 1)], chunk, TILES - 1)
+        send(bank[:], last - 1, TILES - 1, None)

@@ -35,9 +35,8 @@ BANKS = 8
 
 KB = 1024
 SLOT = 4 * KB
-AT_ROUNDED = SLOT * len(UNITS)
-AT_FIRST_H = AT_ROUNDED + 4 * KB
-LATE_GATHERS = {2: AT_ROUNDED, 3: AT_FIRST_H}
+AT_WS = SLOT * len(UNITS)
+LATE_GATHERS = {2: AT_WS, 3: AT_WS + 4 * KB}
 
 
 def tile_list_msg_tanh_res_bias_kernel(
@@ -70,8 +69,9 @@ def tile_list_msg_tanh_res_bias_kernel(
         wgo_first = keep.tile([P, CHUNK], F32, name="wgo_first")
         wgo_rest = keep.tile([P, J - CHUNK], F32, name="wgo_rest")
 
-        for planes in (tab_s, ws_s_tile, lowered_tile, wd_s_tile):
-            nc.vector.memset(planes[:].bitcast(I32), 0)
+        nc.gpsimd.memset(tab_s[:, 0 : T // 2].bitcast(I32), 0)
+        for planes in (tab_s[:, T // 2 :], ws_s_tile[:], lowered_tile[:], wd_s_tile[:]):
+            nc.vector.memset(planes.bitcast(I32), 0)
         for window in windows:
             nc.gpsimd.memset(window[:].bitcast(I32), 0)
 
@@ -85,7 +85,7 @@ def tile_list_msg_tanh_res_bias_kernel(
             wt_loaded.setdefault((a, half), []).append((lo, hi, loaded))
 
         def load_ws(half):
-            loaded = keep.tile([P, 2, PASS], I32, name="ws_loaded%d" % half)
+            loaded = placed.tile([P, 2, PASS], I32, name="ws_loaded%d" % half, align_bytes=64, offset=AT_WS + 4 * KB * half)
             words = ws_words.rearrange("a p r i -> p a (r i)")[:, :, PACK * PASS * half : PACK * PASS * (half + 1)]
             nc.sync.dma_start(out=loaded[:], in_=words.bitcast(I32))
             ws_loaded[half] = loaded
@@ -134,21 +134,22 @@ def tile_list_msg_tanh_res_bias_kernel(
         def entries(lst, first, count=1):
             return lists[lst][:, first * CHUNK // 16 : (first + count) * CHUNK // 16]
 
-        def fetch_words(chunk):
+        def fetch_words(chunk, count=1):
             picked = {}
             for lst in (TARGET, SOURCE):
                 name = "picked_w%d%d" % (chunk, lst)
                 if chunk in LATE_GATHERS:
                     picked[lst] = placed.tile([P, CHUNK], U32, name=name, align_bytes=64, offset=LATE_GATHERS[chunk] + KB * lst)
                 else:
-                    picked[lst] = keep.tile([P, CHUNK], U32, name=name)
-                nc.vector.tensor_copy(picked[lst][:], tab_w[:].bitcast(U32).indirect(entries(lst, chunk)))
+                    picked[lst] = keep.tile([P, count * CHUNK], U32, name=name)
+                nc.vector.tensor_copy(picked[lst][:], tab_w[:].bitcast(U32).indirect(entries(lst, chunk, count)))
             for lst in (TARGET, SOURCE):
-                parted = keep.tile([P, 2, 2 * CHUNK], U8, name="v_w%d%d" % (chunk, lst), align_bytes=64)
+                parted = keep.tile([P, 2, 2 * count * CHUNK], U8, name="v_w%d%d" % (chunk, lst), align_bytes=64)
                 nc.vector.tensor_copy(
                     out=parted[:].bitcast(U16), in_=picked[lst][:].bitcast(U16).rearrange("p (n d) -> p d n", d=2)
                 )
-                v_w[lst, chunk] = parted
+                for n in range(count):
+                    v_w[lst, chunk + n] = parted[:, :, 2 * CHUNK * n : 2 * CHUNK * (n + 1)]
 
         wt_w = {}
         wt_s = {}
@@ -171,15 +172,12 @@ def tile_list_msg_tanh_res_bias_kernel(
 
         def quantize_wt(a, half):
             name = "wt_bf16_%d%d" % (a, half)
-            if (a, half) == (1, 0):
-                rounded = placed.tile([P, PACK, P, PACK], BF16, name=name, align_bytes=64, offset=AT_ROUNDED)
-            else:
-                rounded = keep.tile([P, PACK, P, PACK], BF16, name=name, align_bytes=64)
+            rounded = keep.tile([P, PACK, P, PACK], BF16, name=name, align_bytes=64)
             for lo, hi, loaded in wt_loaded[a, half]:
-                round_copy = nc.vector.tensor_copy if (a, half) == (1, 1) else nc.scalar.copy
+                round_copy, walk = (nc.vector.tensor_copy, "p m t i") if (a, half) == (1, 1) else (nc.scalar.copy, "p m i t")
                 round_copy(
-                    out=rounded[:, :, lo // PACK : hi // PACK, :].rearrange("p t m i -> p m t i"),
-                    in_=loaded[:].rearrange("p i (m t) -> p m t i", t=PACK),
+                    out=rounded[:, :, lo // PACK : hi // PACK, :].rearrange("p t m i -> " + walk),
+                    in_=loaded[:].rearrange("p i (m t) -> " + walk, t=PACK),
                 )
             words = keep.tile([P, PASS], U32, name="wt_w%d%d" % (a, half), align_bytes=64)
             plane = keep.tile([P, PASS], U8, name="wt_s%d%d" % (a, half), align_bytes=64)
@@ -224,10 +222,7 @@ def tile_list_msg_tanh_res_bias_kernel(
                     )
 
         def make_tanh(unit):
-            if unit in ON_VECTOR:
-                values = placed.tile([P, 2, PASS], F32, name="tanh%d%d" % unit, align_bytes=64, offset=SLOT * UNITS.index(unit))
-            else:
-                values = ring.tile([P, 2, PASS], F32, name="tanh", tag="tanh")
+            values = placed.tile([P, 2, PASS], F32, name="tanh%d%d" % unit, align_bytes=64, offset=SLOT * UNITS.index(unit))
             for part in range(2):
                 bank = sums[unit, part]
                 if unit in ON_VECTOR:
@@ -242,8 +237,8 @@ def tile_list_msg_tanh_res_bias_kernel(
 
         def make_h(unit):
             chunk, half = unit
-            if unit == (0, 1):
-                h = placed.tile([P, CHUNK, PACK], BF16, name="h01", align_bytes=64, offset=AT_FIRST_H)
+            if unit == (1, 0):
+                h = placed.tile([P, CHUNK, PACK], BF16, name="h10", align_bytes=64, offset=SLOT * UNITS.index((0, 1)))
             else:
                 h = ring.tile([P, CHUNK, PACK], BF16, name="h", tag="h", align_bytes=64)
             if unit in ON_VECTOR:
@@ -255,7 +250,7 @@ def tile_list_msg_tanh_res_bias_kernel(
                         op=MULT,
                     )
             else:
-                scaled = placed.tile([P, PACK, CHUNK], BF16, name="scaled%d%d" % unit, align_bytes=64, offset=SLOT * UNITS.index(unit))
+                scaled = ring.tile([P, PACK, CHUNK], BF16, name="scaled", tag="scaled", align_bytes=64)
                 for t in range(PACK):
                     nc.scalar.activation(
                         out=scaled[:, t, :],
@@ -310,9 +305,8 @@ def tile_list_msg_tanh_res_bias_kernel(
                 at_y = None if behind is None else SLOT * UNITS.index(behind) + KB * n
                 send(bank[:, CHUNK * n : CHUNK * (n + 1)], chunk, c, at_y)
 
-        fetch_words(0)
+        fetch_words(0, 2)
         quantize_wt(0, 0)
-        fetch_words(1)
         reorder_ws_scales()
         reorder_ws_words(0)
         quantize_wt(1, 0)
@@ -334,7 +328,11 @@ def tile_list_msg_tanh_res_bias_kernel(
         last = CHUNKS - 1
         for chunk in range(last):
             first_product((chunk + 1, 1))
-            send_tiles(chunk, (0, 1), bank_of((chunk + 1, 0), 1), (chunk + 1, 0))
+            if chunk == 0:
+                for c in range(2):
+                    send_tiles(chunk, (c,), bank_of((1, 0), c))
+            else:
+                send_tiles(chunk, (0, 1), bank_of((chunk + 1, 0), 1), (chunk + 1, 0))
             make_tanh((chunk + 1, 1))
             make_h((chunk + 1, 1))
             if chunk + 1 < last:

@@ -28,10 +28,10 @@ SOURCE, TARGET = 0, 1
 
 UNITS = [(0, 0), (1, 0), (0, 1), (1, 1), (2, 0), (2, 1), (3, 0), (3, 1)]
 ON_VECTOR = {(1, 0), (0, 1)}
-PASSES = (((TARGET, 0), (TARGET, 1), (SOURCE, 0), (SOURCE, 1)), ((TARGET, 0), (SOURCE, 0), (SOURCE, 1), (TARGET, 1)))
+PASSES = (((TARGET, 0), (SOURCE, 0), (TARGET, 1), (SOURCE, 1)), ((TARGET, 0), (SOURCE, 0), (SOURCE, 1), (TARGET, 1)))
 PAD = 4
 BANK = 2048
-BANKS = 8
+BANK_PAIRS = {(0, 0): 0, (1, 0): 1, (0, 1): 2, (1, 1): 3, (2, 1): 0, (3, 0): 1, (2, 0): 2, (3, 1): 3}
 
 KB = 1024
 SLOT = 4 * KB
@@ -191,7 +191,7 @@ def tile_list_msg_tanh_res_bias_kernel(
         h_s = {}
 
         def bank_of(unit, part):
-            return BANK * ((2 * UNITS.index(unit) + part) % BANKS)
+            return BANK * (2 * BANK_PAIRS[unit] + part)
 
         def first_product(unit):
             chunk, half = unit
@@ -269,7 +269,8 @@ def tile_list_msg_tanh_res_bias_kernel(
 
         def second_product(bank, chunk, c):
             rows = slice(P * c, P * (c + 1))
-            for half in (1, 0):
+            halves = (0, 1) if chunk in (0, CHUNKS - 1) else (1, 0)
+            for half in halves:
                 for words, plane, fmt in (
                     (wd8_w[:, half, PACK * P * c : PACK * P * (c + 1)], wd8_s, FP8X4),
                     (wd4_w[:, half, 2 * P * c : 2 * P * (c + 1)], wd4_s, FP4X4),
@@ -280,8 +281,8 @@ def tile_list_msg_tanh_res_bias_kernel(
                         lhsT_scale=plane[:, half, rows],
                         rhs=h_w[chunk, half][:].bitcast(FP8X4),
                         rhs_scale=h_s[chunk, half][:],
-                        start=(half == 1 and fmt is FP8X4),
-                        stop=(half == 0 and fmt is FP4X4),
+                        start=(half == halves[0] and fmt is FP8X4),
+                        stop=(half == halves[1] and fmt is FP4X4),
                     )
 
         def send(result, chunk, c, at_y):

@@ -117,8 +117,7 @@ def tile_list_msg_tanh_res_bias_kernel(
                 out=lowered_s[row:P:32, :, :].bitcast(I32), in_=picked_s[8 * row + 4 : P : 32, :, :].bitcast(I32)
             )
         nc.sync.dma_start(out=sm_t[:], in_=sm.rearrange("(g p t) -> p g t", g=2, t=PACK))
-        load_wt(1, 1, 0, PASS // 2)
-        load_wt(1, 1, PASS // 2, PASS)
+        load_wt(1, 1)
         load_ws(1)
         nc.sync.dma_start(out=wd8_w[:].bitcast(I32), in_=wd8_words.rearrange("a p n i -> p a (n i)").bitcast(I32))
         load_planes(wd8_s, wd8_scales)
@@ -242,11 +241,13 @@ def tile_list_msg_tanh_res_bias_kernel(
             else:
                 h = ring.tile([P, CHUNK, PACK], BF16, name="h", tag="h", align_bytes=64)
             if unit in ON_VECTOR:
-                for part in range(2):
+                values = tanh[unit][:].rearrange("p g (n t) -> p (g n) t", t=PACK)
+                width = CHUNK if True else P
+                for first in range(0, CHUNK, width):
                     nc.vector.tensor_tensor(
-                        out=h[:, P * part : P * (part + 1), :],
-                        in0=tanh[unit][:, part, :].rearrange("p (n t) -> p n t", t=PACK),
-                        in1=sm_t[:, half, :].unsqueeze(1).to_broadcast([P, P, PACK]),
+                        out=h[:, first : first + width, :],
+                        in0=values[:, first : first + width, :],
+                        in1=sm_t[:, half, :].unsqueeze(1).to_broadcast([P, width, PACK]),
                         op=MULT,
                     )
             else:

@@ -22,7 +22,6 @@ PASS = P * PACK
 QUADS = 4
 CHUNK = 256
 CHUNKS = J // CHUNK
-GROUPS = CHUNK // P
 TILES = N // P
 SOURCE, TARGET = 0, 1
 
@@ -78,11 +77,11 @@ def tile_list_msg_tanh_res_bias_kernel(
         wt_loaded = {}
         ws_loaded = {}
 
-        def load_wt(a, half, lo=0, hi=PASS):
-            loaded = keep.tile([P, PACK, hi - lo], F32, name="wt_loaded%d%d_%d" % (a, half, lo), align_bytes=64)
-            rows = wt[PASS * a : PASS * (a + 1), PASS * half + lo : PASS * half + hi]
+        def load_wt(a, half):
+            loaded = keep.tile([P, PACK, PASS], F32, name="wt_loaded%d%d" % (a, half), align_bytes=64)
+            rows = wt[PASS * a : PASS * (a + 1), PASS * half : PASS * (half + 1)]
             nc.sync.dma_start(out=loaded[:], in_=rows.rearrange("(p i) r -> p i r", i=PACK))
-            wt_loaded.setdefault((a, half), []).append((lo, hi, loaded))
+            wt_loaded[a, half] = loaded
 
         def load_ws(half):
             loaded = placed.tile([P, 2, PASS], I32, name="ws_loaded%d" % half, align_bytes=64, offset=AT_WS + 4 * KB * half)
@@ -170,14 +169,12 @@ def tile_list_msg_tanh_res_bias_kernel(
             ws_w[half] = words
 
         def quantize_wt(a, half):
-            name = "wt_bf16_%d%d" % (a, half)
-            rounded = keep.tile([P, PACK, P, PACK], BF16, name=name, align_bytes=64)
-            for lo, hi, loaded in wt_loaded[a, half]:
-                round_copy, walk = (nc.vector.tensor_copy, "p m t i") if (a, half) == (1, 1) else (nc.scalar.copy, "p m i t")
-                round_copy(
-                    out=rounded[:, :, lo // PACK : hi // PACK, :].rearrange("p t m i -> " + walk),
-                    in_=loaded[:].rearrange("p i (m t) -> " + walk, t=PACK),
-                )
+            rounded = keep.tile([P, PACK, P, PACK], BF16, name="wt_bf16_%d%d" % (a, half), align_bytes=64)
+            round_copy, walk = (nc.vector.tensor_copy, "p m t i") if (a, half) == (1, 1) else (nc.scalar.copy, "p m i t")
+            round_copy(
+                out=rounded[:].rearrange("p t m i -> " + walk),
+                in_=wt_loaded[a, half][:].rearrange("p i (m t) -> " + walk, t=PACK),
+            )
             words = keep.tile([P, PASS], U32, name="wt_w%d%d" % (a, half), align_bytes=64)
             plane = keep.tile([P, PASS], U8, name="wt_s%d%d" % (a, half), align_bytes=64)
             nc.vector.quantize_mx(out=words[:].bitcast(FP8X4), scales=plane[:], in_=rounded[:].rearrange("p t m i -> p (t m i)"))
@@ -235,21 +232,18 @@ def tile_list_msg_tanh_res_bias_kernel(
             tanh[unit] = values
 
         def make_h(unit):
-            chunk, half = unit
+            half = unit[1]
             if unit == (1, 0):
                 h = placed.tile([P, CHUNK, PACK], BF16, name="h10", align_bytes=64, offset=SLOT * UNITS.index((0, 1)))
             else:
                 h = ring.tile([P, CHUNK, PACK], BF16, name="h", tag="h", align_bytes=64)
             if unit in ON_VECTOR:
-                values = tanh[unit][:].rearrange("p g (n t) -> p (g n) t", t=PACK)
-                width = CHUNK if True else P
-                for first in range(0, CHUNK, width):
-                    nc.vector.tensor_tensor(
-                        out=h[:, first : first + width, :],
-                        in0=values[:, first : first + width, :],
-                        in1=sm_t[:, half, :].unsqueeze(1).to_broadcast([P, width, PACK]),
-                        op=MULT,
-                    )
+                nc.vector.tensor_tensor(
+                    out=h[:],
+                    in0=tanh[unit][:].rearrange("p part (n t) -> p (part n) t", t=PACK),
+                    in1=sm_t[:, half, :].unsqueeze(1).to_broadcast([P, CHUNK, PACK]),
+                    op=MULT,
+                )
             else:
                 scaled = ring.tile([P, PACK, CHUNK], BF16, name="scaled", tag="scaled", align_bytes=64)
                 for t in range(PACK):
@@ -297,7 +291,11 @@ def tile_list_msg_tanh_res_bias_kernel(
             weight = wgo_first[:] if chunk == 0 else wgo_rest[:, CHUNK * (chunk - 1) : CHUNK * (chunk - 1) + width]
             nc.vector.tensor_tensor(windows[c][:].indirect(entries(TARGET, chunk, width // CHUNK)), y[:], weight, MULT)
             if CHUNK * chunk + width == J:
-                nc.sync.dma_start(out=out[P * c : P * (c + 1), :], in_=windows[c][:])
+                queues = (nc.sync, nc.scalar) if c == TILES - 1 else (nc.sync,)
+                share = T // len(queues)
+                for n, queue in enumerate(queues):
+                    cols = slice(share * n, share * (n + 1))
+                    queue.dma_start(out=out[P * c : P * (c + 1), cols], in_=windows[c][:, cols])
 
         def send_tiles(chunk, tiles, at_bank, behind=None):
             bank = psum.tile([P, CHUNK * len(tiles)], F32, name="b%d%d" % (chunk, tiles[0]), offset=at_bank)
@@ -316,15 +314,10 @@ def tile_list_msg_tanh_res_bias_kernel(
         quantize_wt(0, 1)
         quantize_wt(1, 1)
         reorder_ws_words(1)
-        first_product((0, 0))
-        make_tanh((0, 0))
-        make_h((0, 0))
-        first_product((0, 1))
-        make_tanh((0, 1))
-        make_h((0, 1))
-        first_product((1, 0))
-        make_tanh((1, 0))
-        make_h((1, 0))
+        for unit in ((0, 0), (0, 1), (1, 0)):
+            first_product(unit)
+            make_tanh(unit)
+            make_h(unit)
         fetch_words(3)
 
         last = CHUNKS - 1

@@ -144,7 +144,8 @@ def tile_list_msg_tanh_res_bias_kernel(
             for lst in (TARGET, SOURCE):
                 parted = keep.tile([P, 2, 2 * count * CHUNK], U8, name="v_w%d%d" % (chunk, lst), align_bytes=64)
                 nc.vector.tensor_copy(
-                    out=parted[:].bitcast(U16), in_=picked[lst][:].bitcast(U16).rearrange("p (n d) -> p d n", d=2)
+                    out=parted[:].bitcast(U16).rearrange("p d (e n) -> p e d n", e=2),
+                    in_=picked[lst][:].bitcast(U16).rearrange("p (e n d) -> p e d n", e=2, d=2),
                 )
                 for n in range(count):
                     v_w[lst, chunk + n] = parted[:, :, 2 * CHUNK * n : 2 * CHUNK * (n + 1)]
@@ -163,17 +164,17 @@ def tile_list_msg_tanh_res_bias_kernel(
         def reorder_ws_words(half):
             words = keep.tile([P, 2, PASS], I32, name="ws_w%d" % half, align_bytes=64)
             nc.vector.tensor_copy(
-                out=words[:].rearrange("p a (t mq mm) -> p a mq t mm", t=PACK, mm=4),
-                in_=ws_loaded[half][:].rearrange("p a (mq mm t) -> p a mq t mm", t=PACK, mm=4),
+                out=words[:].rearrange("p a (t m) -> p a m t", t=PACK),
+                in_=ws_loaded[half][:].rearrange("p a (m t) -> p a m t", t=PACK),
             )
             ws_w[half] = words
 
         def quantize_wt(a, half):
             rounded = keep.tile([P, PACK, P, PACK], BF16, name="wt_bf16_%d%d" % (a, half), align_bytes=64)
-            round_copy, walk = (nc.vector.tensor_copy, "p m t i") if (a, half) == (1, 1) else (nc.scalar.copy, "p m i t")
+            round_copy = nc.vector.tensor_copy if (a, half) == (1, 1) else nc.scalar.copy
             round_copy(
-                out=rounded[:].rearrange("p t m i -> " + walk),
-                in_=wt_loaded[a, half][:].rearrange("p i (m t) -> " + walk, t=PACK),
+                out=rounded[:].rearrange("p t m i -> p m i t"),
+                in_=wt_loaded[a, half][:].rearrange("p i (m t) -> p m i t", t=PACK),
             )
             words = keep.tile([P, PASS], U32, name="wt_w%d%d" % (a, half), align_bytes=64)
             plane = keep.tile([P, PASS], U8, name="wt_s%d%d" % (a, half), align_bytes=64)

@@ -26,16 +26,28 @@ TILES = N // P
 SOURCE, TARGET = 0, 1
 
 UNITS = [(0, 0), (1, 0), (0, 1), (1, 1), (2, 0), (2, 1), (3, 0), (3, 1)]
-ON_VECTOR = {(1, 0), (0, 1)}
-PASSES = (((TARGET, 0), (SOURCE, 0), (TARGET, 1), (SOURCE, 1)), ((TARGET, 0), (SOURCE, 0), (SOURCE, 1), (TARGET, 1)))
+ON_VECTOR = {(0, 1), (1, 1)}
+PASSES = (((TARGET, 0), (TARGET, 1), (SOURCE, 0), (SOURCE, 1)), ((TARGET, 0), (SOURCE, 0), (SOURCE, 1), (TARGET, 1)))
+ROUNDING = {(0, 0): ("scalar",), (1, 0): ("scalar",), (0, 1): ("scalar", "vector"), (1, 1): ("vector", "vector")}
+BY_EDGES = (0, 1)
 PAD = 4
+ROWS_AT = 96
 BANK = 2048
-BANK_PAIRS = {(0, 0): 0, (1, 0): 1, (0, 1): 2, (1, 1): 3, (2, 1): 0, (3, 0): 1, (2, 0): 2, (3, 1): 3}
+BANKS = {(0, 0): (0, 1), (1, 0): (2, 3), (0, 1): (4, 5), (1, 1): (6, 4), (2, 0): (5, 6), (2, 1): (4, 0), (3, 0): (1, 2), (3, 1): (5, 4)}
 
 KB = 1024
 SLOT = 4 * KB
-AT_WS = SLOT * len(UNITS)
-LATE_GATHERS = {2: AT_WS, 3: AT_WS + 4 * KB}
+AT_WT = SLOT * len(UNITS)
+AT_TAB_S = AT_WT + 32 * KB
+AT_WS_S = AT_TAB_S + 2 * KB + 64
+AT_FIRST = AT_WS_S + 2 * KB + 64
+
+
+def at_wt(a, half):
+    return AT_WT + 8 * KB * (2 * half + a)
+
+
+LATE_GATHERS = {2: at_wt(1, 0), 3: at_wt(1, 1) + 4 * KB}
 
 
 def tile_list_msg_tanh_res_bias_kernel(
@@ -50,16 +62,18 @@ def tile_list_msg_tanh_res_bias_kernel(
 
         lists = [keep.tile([P, J // 16], U16, name="list_source"), keep.tile([P, J // 16], U16, name="list_target")]
         tab_w = keep.tile([P, T], I32, name="tab_w", align_bytes=64)
-        tab_s = keep.tile([P, T + PAD], U8, name="tab_s", align_bytes=64)
-        ws_s_tile = keep.tile([P, 2 * R + PAD], U8, name="ws_s_tile", align_bytes=64)
+        tab_s = placed.tile([P, T + PAD], U8, name="tab_s", align_bytes=64, offset=AT_TAB_S)
+        ws_s_tile = placed.tile([P, 2 * R + PAD], U8, name="ws_s_tile", align_bytes=64, offset=AT_WS_S)
         ws_s_loaded = ws_s_tile[:, 0 : 2 * R].rearrange("p (a r) -> p a r", a=2)
-        wd_s_tile = keep.tile([P, 4 * N + PAD], U8, name="wd_s_tile", align_bytes=64)
+        wd_s_tile = placed.tile([P, 4 * N], U8, name="wd_s_tile", align_bytes=64, offset=AT_WS_S)
         wd8_s = wd_s_tile[:, 0 : 2 * N].rearrange("p (a n) -> p a n", a=2)
         wd4_s = wd_s_tile[:, 2 * N : 4 * N].rearrange("p (a n) -> p a n", a=2)
         picked_s = keep.tile([P, 2, J], U8, name="picked_s", align_bytes=64)
-        lowered_tile = keep.tile([P, 2 * J + PAD], U8, name="lowered_tile", align_bytes=64)
-        lowered_s = lowered_tile[:, 0 : 2 * J].rearrange("p (l j) -> p l j", l=2)
-        v_s = [picked_s, lowered_s]
+        lowered = [
+            placed.tile([P, 2 * J], U8, name="lowered0", align_bytes=64, offset=AT_TAB_S),
+            keep.tile([P, 2 * J + PAD], U8, name="lowered1", align_bytes=64),
+        ]
+        v_s = [tile[:, 0 : 2 * J].rearrange("p (l j) -> p l j", l=2) for tile in lowered]
         windows = [keep.tile([P, T], F32, name="window%d" % c, align_bytes=64) for c in range(TILES)]
         sm_t = keep.tile([P, 2, PACK], F32, name="sm_t")
         b_t = keep.tile([P, TILES], F32, name="b_t")
@@ -68,8 +82,7 @@ def tile_list_msg_tanh_res_bias_kernel(
         wgo_first = keep.tile([P, CHUNK], F32, name="wgo_first")
         wgo_rest = keep.tile([P, J - CHUNK], F32, name="wgo_rest")
 
-        nc.gpsimd.memset(tab_s[:, 0 : T // 2].bitcast(I32), 0)
-        for planes in (tab_s[:, T // 2 :], ws_s_tile[:], lowered_tile[:], wd_s_tile[:]):
+        for planes in (tab_s[0:ROWS_AT, :], ws_s_tile[:], lowered[1][:]):
             nc.vector.memset(planes.bitcast(I32), 0)
         for window in windows:
             nc.gpsimd.memset(window[:].bitcast(I32), 0)
@@ -77,14 +90,19 @@ def tile_list_msg_tanh_res_bias_kernel(
         wt_loaded = {}
         ws_loaded = {}
 
-        def load_wt(a, half):
-            loaded = keep.tile([P, PACK, PASS], F32, name="wt_loaded%d%d" % (a, half), align_bytes=64)
-            rows = wt[PASS * a : PASS * (a + 1), PASS * half : PASS * (half + 1)]
-            nc.sync.dma_start(out=loaded[:], in_=rows.rearrange("(p i) r -> p i r", i=PACK))
-            wt_loaded[a, half] = loaded
+        def load_wt(a, half, pieces=1, between=None):
+            width = PASS // pieces
+            for n in range(pieces):
+                at = at_wt(a, half) + 4 * PACK * width * n
+                loaded = placed.tile([P, PACK, width], F32, name="wt_loaded%d%d%d" % (a, half, n), align_bytes=64, offset=at)
+                rows = wt[PASS * a : PASS * (a + 1), PASS * half + width * n : PASS * half + width * (n + 1)]
+                nc.sync.dma_start(out=loaded[:], in_=rows.rearrange("(p i) r -> p i r", i=PACK))
+                wt_loaded.setdefault((a, half), []).append(loaded)
+                if between and n == 0:
+                    between()
 
         def load_ws(half):
-            loaded = placed.tile([P, 2, PASS], I32, name="ws_loaded%d" % half, align_bytes=64, offset=AT_WS + 4 * KB * half)
+            loaded = keep.tile([P, 2, PASS], I32, name="ws_loaded%d" % half, align_bytes=64)
             words = ws_words.rearrange("a p r i -> p a (r i)")[:, :, PACK * PASS * half : PACK * PASS * (half + 1)]
             nc.sync.dma_start(out=loaded[:], in_=words.bitcast(I32))
             ws_loaded[half] = loaded
@@ -96,28 +114,27 @@ def tile_list_msg_tanh_res_bias_kernel(
                     in_=scales[:, 4 * quad : 4 * quad + 4, :].rearrange("a q n -> q a n").bitcast(I32),
                 )
 
+        def lower_planes(a):
+            for row in range(4):
+                first = ROWS_AT + 16 * a + row
+                rows = picked_s[first : first + 13 : 4, :, :]
+                nc.sync.dma_start(out=v_s[a][row:P:32, :, :].bitcast(I32), in_=rows.bitcast(I32))
+
         nc.sync.dma_start(lists[TARGET][:], offs2)
         nc.sync.dma_start(lists[SOURCE][:], offs)
-        for quad in range(QUADS):
-            nc.sync.dma_start(
-                out=tab_s[32 * quad : 32 * quad + 4, 0:T].bitcast(I32), in_=tab_scales[0, 4 * quad : 4 * quad + 4, :].bitcast(I32)
-            )
-        nc.sync.dma_start(out=tab_s[4:P:8, 0:T].bitcast(I32), in_=tab_scales[1].bitcast(I32))
-        load_wt(0, 0)
+        nc.sync.dma_start(out=tab_s[ROWS_AT:P, 0:T].bitcast(I32), in_=tab_scales.rearrange("a q t -> (a q) t").bitcast(I32))
+        nc.sync.dma_start(out=tab_w[:], in_=tab_words[0].rearrange("p t d -> p (t d)").bitcast(I32))
         for lst in (TARGET, SOURCE):
             nc.vector.tensor_copy(picked_s[:, lst, :], tab_s[:, 0:T].indirect(lists[lst][:]))
-        nc.sync.dma_start(out=tab_w[:], in_=tab_words[0].rearrange("p t d -> p (t d)").bitcast(I32))
-        load_wt(1, 0)
+        load_wt(0, 0)
         load_planes(ws_s_loaded, ws_scales)
+        load_wt(1, 0)
         load_ws(0)
-        load_wt(0, 1)
-        for row in range(4):
-            nc.sync.dma_start(
-                out=lowered_s[row:P:32, :, :].bitcast(I32), in_=picked_s[8 * row + 4 : P : 32, :, :].bitcast(I32)
-            )
-        nc.sync.dma_start(out=sm_t[:], in_=sm.rearrange("(g p t) -> p g t", g=2, t=PACK))
-        load_wt(1, 1)
+        lower_planes(0)
+        load_wt(0, 1, 2, lambda: lower_planes(1))
         load_ws(1)
+        nc.sync.dma_start(out=sm_t[:], in_=sm.rearrange("(g p t) -> p g t", g=2, t=PACK))
+        load_wt(1, 1, 2)
         nc.sync.dma_start(out=wd8_w[:].bitcast(I32), in_=wd8_words.rearrange("a p n i -> p a (n i)").bitcast(I32))
         load_planes(wd8_s, wd8_scales)
         nc.sync.dma_start(out=wd4_w[:].bitcast(I32), in_=wd4_words.rearrange("a p n -> p a n").bitcast(I32))
@@ -153,7 +170,7 @@ def tile_list_msg_tanh_res_bias_kernel(
         wt_w = {}
         wt_s = {}
         ws_w = {}
-        ws_s = keep.tile([P, 2, R], U8, name="ws_s", align_bytes=64)
+        ws_s = placed.tile([P, 2, R], U8, name="ws_s", align_bytes=64, offset=at_wt(0, 0))
 
         def reorder_ws_scales():
             nc.vector.tensor_copy(
@@ -163,19 +180,25 @@ def tile_list_msg_tanh_res_bias_kernel(
 
         def reorder_ws_words(half):
             words = keep.tile([P, 2, PASS], I32, name="ws_w%d" % half, align_bytes=64)
-            nc.vector.tensor_copy(
-                out=words[:].rearrange("p a (t m) -> p a m t", t=PACK),
-                in_=ws_loaded[half][:].rearrange("p a (m t) -> p a m t", t=PACK),
+            move = nc.scalar.copy if half == 0 else nc.vector.tensor_copy
+            move(
+                out=words[:].bitcast(U32).rearrange("p a (t m) -> p a m t", t=PACK),
+                in_=ws_loaded[half][:].bitcast(U32).rearrange("p a (m t) -> p a m t", t=PACK),
             )
             ws_w[half] = words
 
         def quantize_wt(a, half):
             rounded = keep.tile([P, PACK, P, PACK], BF16, name="wt_bf16_%d%d" % (a, half), align_bytes=64)
-            round_copy = nc.vector.tensor_copy if (a, half) == (1, 1) else nc.scalar.copy
-            round_copy(
-                out=rounded[:].rearrange("p t m i -> p m i t"),
-                in_=wt_loaded[a, half][:].rearrange("p i (m t) -> p m i t", t=PACK),
-            )
+            copies = ROUNDING[a, half]
+            pieces = wt_loaded[a, half]
+            share = P // len(copies)
+            for n, engine in enumerate(copies):
+                piece = pieces[n][:] if len(pieces) > 1 else pieces[0][:, :, PACK * share * n : PACK * share * (n + 1)]
+                round_copy = nc.vector.tensor_copy if engine == "vector" else nc.scalar.copy
+                round_copy(
+                    out=rounded[:, :, share * n : share * (n + 1), :].rearrange("p t m i -> p m i t"),
+                    in_=piece.rearrange("p i (m t) -> p m i t", t=PACK),
+                )
             words = keep.tile([P, PASS], U32, name="wt_w%d%d" % (a, half), align_bytes=64)
             plane = keep.tile([P, PASS], U8, name="wt_s%d%d" % (a, half), align_bytes=64)
             nc.vector.quantize_mx(out=words[:].bitcast(FP8X4), scales=plane[:], in_=rounded[:].rearrange("p t m i -> p (t m i)"))
@@ -188,14 +211,14 @@ def tile_list_msg_tanh_res_bias_kernel(
         h_s = {}
 
         def bank_of(unit, part):
-            return BANK * (2 * BANK_PAIRS[unit] + part)
+            return BANK * BANKS[unit][part]
 
         def first_product(unit):
             chunk, half = unit
             for part in range(2):
                 bank = psum.tile([P, PASS], F32, name="a%d%d%d" % (chunk, half, part), offset=bank_of(unit, part))
                 sums[unit, part] = bank
-                if unit in ON_VECTOR:
+                if unit == BY_EDGES:
                     first, width, outputs = part * P, P, range(PACK)
                 else:
                     first, width, outputs = 0, CHUNK, range(2 * part, 2 * part + 2)
@@ -219,34 +242,54 @@ def tile_list_msg_tanh_res_bias_kernel(
                     )
 
         def make_tanh(unit):
-            values = placed.tile([P, 2, PASS], F32, name="tanh%d%d" % unit, align_bytes=64, offset=SLOT * UNITS.index(unit))
+            at = SLOT * UNITS.index(unit)
+            if unit == BY_EDGES:
+                tanh[unit] = [
+                    placed.tile([P, PASS], F32, name="tanh01%d" % part, align_bytes=64, offset=AT_FIRST + 2 * KB * (part + 1))[:]
+                    for part in range(2)
+                ]
+            else:
+                tanh[unit] = placed.tile([P, 2, PASS], F32, name="tanh%d%d" % unit, align_bytes=64, offset=at)
             for part in range(2):
                 bank = sums[unit, part]
+                values = tanh[unit][part] if unit == BY_EDGES else tanh[unit][:, part, :]
                 if unit in ON_VECTOR:
+                    side = PACK if unit == BY_EDGES else 2
                     nc.scalar.activation(
-                        out=values[:, part, :].rearrange("p (n t) -> p n t", t=PACK),
-                        in_=bank[:].rearrange("p (t n) -> p n t", t=PACK),
+                        out=values.rearrange("p (n t) -> p n t", t=side),
+                        in_=bank[:].rearrange("p (t n) -> p n t", t=side),
                         func=ACT.Tanh,
                     )
                 else:
-                    nc.scalar.activation(out=values[:, part, :], in_=bank[:], func=ACT.Tanh)
-            tanh[unit] = values
+                    nc.scalar.activation(out=values, in_=bank[:], func=ACT.Tanh)
 
-        def make_h(unit):
+        def make_h(*units):
+            for unit, h in [(unit, scale_tanh(unit)) for unit in units]:
+                quantize_h(unit, h)
+
+        def scale_tanh(unit):
             half = unit[1]
-            if unit == (1, 0):
-                h = placed.tile([P, CHUNK, PACK], BF16, name="h10", align_bytes=64, offset=SLOT * UNITS.index((0, 1)))
-            else:
-                h = ring.tile([P, CHUNK, PACK], BF16, name="h", tag="h", align_bytes=64)
-            if unit in ON_VECTOR:
+            h = ring.tile([P, CHUNK, PACK], BF16, name="h", tag="h", align_bytes=64)
+            if unit == BY_EDGES:
+                for part in range(2):
+                    nc.vector.tensor_tensor(
+                        out=h[:, P * part : P * (part + 1), :],
+                        in0=tanh[unit][part].rearrange("p (n t) -> p n t", t=PACK),
+                        in1=sm_t[:, half, :].unsqueeze(1).to_broadcast([P, P, PACK]),
+                        op=MULT,
+                    )
+            elif unit in ON_VECTOR:
                 nc.vector.tensor_tensor(
-                    out=h[:],
-                    in0=tanh[unit][:].rearrange("p part (n t) -> p (part n) t", t=PACK),
-                    in1=sm_t[:, half, :].unsqueeze(1).to_broadcast([P, CHUNK, PACK]),
+                    out=h[:].rearrange("p n (part t) -> p n part t", t=2),
+                    in0=tanh[unit][:].rearrange("p part (n t) -> p n part t", t=2),
+                    in1=sm_t[:, half, :].rearrange("p (part t) -> p part t", t=2).unsqueeze(1).to_broadcast([P, CHUNK, 2, 2]),
                     op=MULT,
                 )
             else:
-                scaled = ring.tile([P, PACK, CHUNK], BF16, name="scaled", tag="scaled", align_bytes=64)
+                if unit == (1, 0):
+                    scaled = placed.tile([P, PACK, CHUNK], BF16, name="scaled10", align_bytes=64, offset=AT_FIRST + KB)
+                else:
+                    scaled = ring.tile([P, PACK, CHUNK], BF16, name="scaled", tag="scaled", align_bytes=64)
                 for t in range(PACK):
                     nc.scalar.activation(
                         out=scaled[:, t, :],
@@ -257,7 +300,13 @@ def tile_list_msg_tanh_res_bias_kernel(
                 nc.scalar.copy(
                     out=h[:].rearrange("p (c i) t -> p c t i", i=4), in_=scaled[:].rearrange("p t (c i) -> p c t i", i=4)
                 )
-            words = keep.tile([P, CHUNK], U32, name="h_w%d%d" % unit, align_bytes=64)
+            return h
+
+        def quantize_h(unit, h):
+            if unit == (0, 0):
+                words = placed.tile([P, CHUNK], U32, name="h_w00", align_bytes=64, offset=AT_FIRST + 3 * KB)
+            else:
+                words = keep.tile([P, CHUNK], U32, name="h_w%d%d" % unit, align_bytes=64)
             plane = keep.tile([P, CHUNK], U8, name="h_s%d%d" % unit, align_bytes=64)
             nc.vector.quantize_mx(out=words[:].bitcast(FP8X4), scales=plane[:], in_=h[:].rearrange("p n t -> p (n t)"))
             h_w[unit] = words
@@ -313,33 +362,35 @@ def tile_list_msg_tanh_res_bias_kernel(
         quantize_wt(1, 0)
         fetch_words(2)
         quantize_wt(0, 1)
-        quantize_wt(1, 1)
         reorder_ws_words(1)
+        quantize_wt(1, 1)
         for unit in ((0, 0), (0, 1), (1, 0)):
             first_product(unit)
             make_tanh(unit)
-            make_h(unit)
         fetch_words(3)
+        make_h((0, 0), (0, 1))
 
         last = CHUNKS - 1
         for chunk in range(last):
             first_product((chunk + 1, 1))
             if chunk == 0:
                 for c in range(2):
-                    send_tiles(chunk, (c,), bank_of((1, 0), c))
+                    send_tiles(chunk, (c,), BANK * c)
             else:
-                send_tiles(chunk, (0, 1), bank_of((chunk + 1, 0), 1), (chunk + 1, 0))
+                send_tiles(chunk, (0, 1), BANK * 3, (chunk + 1, 0))
             make_tanh((chunk + 1, 1))
             make_h((chunk + 1, 1))
+            if chunk == 0:
+                make_h((1, 0))
             if chunk + 1 < last:
                 first_product((chunk + 2, 0))
-                send_tiles(chunk, (2, 3), bank_of((chunk + 1, 1), 1), (chunk + 1, 1))
+                send_tiles(chunk, (2, 3), BANK * (2 if chunk == 0 else 7), (chunk + 1, 1))
                 make_tanh((chunk + 2, 0))
                 make_h((chunk + 2, 0))
-        send_tiles(last - 1, (2,), bank_of((last, 1), 1), (last, 1))
+        send_tiles(last - 1, (2,), BANK * 7, (last, 1))
         for c in range(TILES - 1):
             send_tiles(last, (c,), BANK * c)
-        bank = psum.tile([P, 2 * CHUNK], F32, name="b_last", offset=bank_of((last, 1), 0))
+        bank = psum.tile([P, 2 * CHUNK], F32, name="b_last", offset=BANK * 6)
         for n, chunk in enumerate((last - 1, last)):
             second_product(bank[:, CHUNK * n : CHUNK * (n + 1)], chunk, TILES - 1)
         send(bank[:], last - 1, TILES - 1, None)

@@ -47,6 +47,7 @@ def at_wt(a, half):
     return AT_WT + 8 * KB * (2 * half + a)
 
 
+LATE_PARTINGS = {(0, SOURCE): at_wt(0, 0) + 4 * KB, (3, SOURCE): AT_FIRST + 4 * KB}
 LATE_GATHERS = {2: at_wt(1, 0), 3: at_wt(1, 1) + 4 * KB}
 
 
@@ -82,7 +83,7 @@ def tile_list_msg_tanh_res_bias_kernel(
         wgo_first = keep.tile([P, CHUNK], F32, name="wgo_first")
         wgo_rest = keep.tile([P, J - CHUNK], F32, name="wgo_rest")
 
-        for planes in (tab_s[0:ROWS_AT, :], ws_s_tile[:], lowered[1][:]):
+        for planes in (ws_s_tile[:], tab_s[0:ROWS_AT, :], lowered[1][:]):
             nc.vector.memset(planes.bitcast(I32), 0)
         for window in windows:
             nc.gpsimd.memset(window[:].bitcast(I32), 0)
@@ -101,17 +102,18 @@ def tile_list_msg_tanh_res_bias_kernel(
                 if between and n == 0:
                     between()
 
-        def load_ws(half):
-            loaded = keep.tile([P, 2, PASS], I32, name="ws_loaded%d" % half, align_bytes=64)
+        def load_ws(half, pieces=1):
             words = ws_words.rearrange("a p r i -> p a (r i)")[:, :, PACK * PASS * half : PACK * PASS * (half + 1)]
-            nc.sync.dma_start(out=loaded[:], in_=words.bitcast(I32))
-            ws_loaded[half] = loaded
+            count = 2 // pieces
+            for n in range(pieces):
+                loaded = keep.tile([P, count, PASS], I32, name="ws_loaded%d%d" % (half, n), align_bytes=64)
+                nc.sync.dma_start(out=loaded[:], in_=words[:, count * n : count * (n + 1), :].bitcast(I32))
+                ws_loaded.setdefault(half, []).append(loaded)
 
         def load_planes(planes, scales):
-            for quad in range(QUADS):
+            for row in range(4):
                 nc.sync.dma_start(
-                    out=planes[32 * quad : 32 * quad + 4, :, :].bitcast(I32),
-                    in_=scales[:, 4 * quad : 4 * quad + 4, :].rearrange("a q n -> q a n").bitcast(I32),
+                    out=planes[row:P:32, :, :].bitcast(I32), in_=scales[:, row:16:4, :].rearrange("a q n -> q a n").bitcast(I32)
                 )
 
         def lower_planes(a):
@@ -120,25 +122,25 @@ def tile_list_msg_tanh_res_bias_kernel(
                 rows = picked_s[first : first + 13 : 4, :, :]
                 nc.sync.dma_start(out=v_s[a][row:P:32, :, :].bitcast(I32), in_=rows.bitcast(I32))
 
+        nc.sync.dma_start(out=tab_s[ROWS_AT:P, 0:T].bitcast(I32), in_=tab_scales.rearrange("a q t -> (a q) t").bitcast(I32))
         nc.sync.dma_start(lists[TARGET][:], offs2)
         nc.sync.dma_start(lists[SOURCE][:], offs)
-        nc.sync.dma_start(out=tab_s[ROWS_AT:P, 0:T].bitcast(I32), in_=tab_scales.rearrange("a q t -> (a q) t").bitcast(I32))
         nc.sync.dma_start(out=tab_w[:], in_=tab_words[0].rearrange("p t d -> p (t d)").bitcast(I32))
         for lst in (TARGET, SOURCE):
             nc.vector.tensor_copy(picked_s[:, lst, :], tab_s[:, 0:T].indirect(lists[lst][:]))
         load_wt(0, 0)
         load_planes(ws_s_loaded, ws_scales)
         load_wt(1, 0)
-        load_ws(0)
+        nc.sync.dma_start(out=sm_t[:], in_=sm.rearrange("(g p t) -> p g t", g=2, t=PACK))
         lower_planes(0)
+        load_ws(0)
         load_wt(0, 1, 2, lambda: lower_planes(1))
         load_ws(1)
-        nc.sync.dma_start(out=sm_t[:], in_=sm.rearrange("(g p t) -> p g t", g=2, t=PACK))
+        load_planes(wd4_s, wd4_scales)
         load_wt(1, 1, 2)
         nc.sync.dma_start(out=wd8_w[:].bitcast(I32), in_=wd8_words.rearrange("a p n i -> p a (n i)").bitcast(I32))
-        load_planes(wd8_s, wd8_scales)
         nc.sync.dma_start(out=wd4_w[:].bitcast(I32), in_=wd4_words.rearrange("a p n -> p a n").bitcast(I32))
-        load_planes(wd4_s, wd4_scales)
+        load_planes(wd8_s, wd8_scales)
         with nc.allow_non_contiguous_dma(reason="one bias value to a partition"):
             nc.sync.dma_start(out=b_t[:], in_=b.rearrange("(c p) -> p c", p=P))
         nc.sync.dma_start(out=wgo_first[:], in_=wgo[:, 0:CHUNK])
@@ -149,23 +151,31 @@ def tile_list_msg_tanh_res_bias_kernel(
         def entries(lst, first, count=1):
             return lists[lst][:, first * CHUNK // 16 : (first + count) * CHUNK // 16]
 
-        def fetch_words(chunk, count=1):
-            picked = {}
+        picked = {}
+
+        def gather_words(chunk, count=1):
             for lst in (TARGET, SOURCE):
                 name = "picked_w%d%d" % (chunk, lst)
                 if chunk in LATE_GATHERS:
-                    picked[lst] = placed.tile([P, CHUNK], U32, name=name, align_bytes=64, offset=LATE_GATHERS[chunk] + KB * lst)
+                    words = placed.tile([P, CHUNK], U32, name=name, align_bytes=64, offset=LATE_GATHERS[chunk] + KB * lst)
                 else:
-                    picked[lst] = keep.tile([P, count * CHUNK], U32, name=name)
-                nc.vector.tensor_copy(picked[lst][:], tab_w[:].bitcast(U32).indirect(entries(lst, chunk, count)))
-            for lst in (TARGET, SOURCE):
-                parted = keep.tile([P, 2, 2 * count * CHUNK], U8, name="v_w%d%d" % (chunk, lst), align_bytes=64)
-                nc.vector.tensor_copy(
-                    out=parted[:].bitcast(U16).rearrange("p d (e n) -> p e d n", e=2),
-                    in_=picked[lst][:].bitcast(U16).rearrange("p (e n d) -> p e d n", e=2, d=2),
-                )
-                for n in range(count):
-                    v_w[lst, chunk + n] = parted[:, :, 2 * CHUNK * n : 2 * CHUNK * (n + 1)]
+                    words = keep.tile([P, count * CHUNK], U32, name=name)
+                nc.vector.tensor_copy(words[:], tab_w[:].bitcast(U32).indirect(entries(lst, chunk, count)))
+                picked[chunk, lst] = words
+
+        def part_words(chunk, lst):
+            width = picked[chunk, lst].shape[1]
+            name = "v_w%d%d" % (chunk, lst)
+            if (chunk, lst) in LATE_PARTINGS:
+                parted = placed.tile([P, 2, 2 * width], U8, name=name, align_bytes=64, offset=LATE_PARTINGS[chunk, lst])
+            else:
+                parted = keep.tile([P, 2, 2 * width], U8, name=name, align_bytes=64)
+            nc.vector.tensor_copy(
+                out=parted[:].bitcast(U16).rearrange("p d (e n) -> p e d n", e=2),
+                in_=picked[chunk, lst][:].bitcast(U16).rearrange("p (e n d) -> p e d n", e=2, d=2),
+            )
+            for n in range(width // CHUNK):
+                v_w[lst, chunk + n] = parted[:, :, 2 * CHUNK * n : 2 * CHUNK * (n + 1)]
 
         wt_w = {}
         wt_s = {}
@@ -179,13 +189,16 @@ def tile_list_msg_tanh_res_bias_kernel(
             )
 
         def reorder_ws_words(half):
-            words = keep.tile([P, 2, PASS], I32, name="ws_w%d" % half, align_bytes=64)
             move = nc.scalar.copy if half == 0 else nc.vector.tensor_copy
-            move(
-                out=words[:].bitcast(U32).rearrange("p a (t m) -> p a m t", t=PACK),
-                in_=ws_loaded[half][:].bitcast(U32).rearrange("p a (m t) -> p a m t", t=PACK),
-            )
-            ws_w[half] = words
+            for n, loaded in enumerate(ws_loaded[half]):
+                count = loaded.shape[1]
+                words = keep.tile([P, count, PASS], U32, name="ws_w%d%d" % (half, n), align_bytes=64)
+                move(
+                    out=words[:].rearrange("p a (t m) -> p a m t", t=PACK),
+                    in_=loaded[:].bitcast(U32).rearrange("p a (m t) -> p a m t", t=PACK),
+                )
+                for a in range(count):
+                    ws_w[half, count * n + a] = words[:, a, :]
 
         def quantize_wt(a, half):
             rounded = keep.tile([P, PACK, P, PACK], BF16, name="wt_bf16_%d%d" % (a, half), align_bytes=64)
@@ -229,7 +242,7 @@ def tile_list_msg_tanh_res_bias_kernel(
                     if lst == TARGET:
                         words, plane = wt_w[a, half][:, cols], wt_s[a, half][:, cols]
                     else:
-                        words, plane = ws_w[half][:, a, cols], ws_s[:, a, PASS * half + P * t : PASS * half + P * (t + 1)]
+                        words, plane = ws_w[half, a][:, cols], ws_s[:, a, PASS * half + P * t : PASS * half + P * (t + 1)]
                     at = width * (t - outputs[0])
                     nc.tensor.matmul_mx(
                         out=bank[:, at : at + width],
@@ -269,7 +282,10 @@ def tile_list_msg_tanh_res_bias_kernel(
 
         def scale_tanh(unit):
             half = unit[1]
-            h = ring.tile([P, CHUNK, PACK], BF16, name="h", tag="h", align_bytes=64)
+            if unit == (1, 0):
+                h = placed.tile([P, CHUNK, PACK], BF16, name="h10", align_bytes=64, offset=AT_FIRST + KB)
+            else:
+                h = ring.tile([P, CHUNK, PACK], BF16, name="h", tag="h", align_bytes=64)
             if unit == BY_EDGES:
                 for part in range(2):
                     nc.vector.tensor_tensor(
@@ -286,10 +302,7 @@ def tile_list_msg_tanh_res_bias_kernel(
                     op=MULT,
                 )
             else:
-                if unit == (1, 0):
-                    scaled = placed.tile([P, PACK, CHUNK], BF16, name="scaled10", align_bytes=64, offset=AT_FIRST + KB)
-                else:
-                    scaled = ring.tile([P, PACK, CHUNK], BF16, name="scaled", tag="scaled", align_bytes=64)
+                scaled = ring.tile([P, PACK, CHUNK], BF16, name="scaled", tag="scaled", align_bytes=64)
                 for t in range(PACK):
                     nc.scalar.activation(
                         out=scaled[:, t, :],
@@ -297,9 +310,12 @@ def tile_list_msg_tanh_res_bias_kernel(
                         func=ACT.Copy,
                         scale=sm_t[:, half, t : t + 1],
                     )
-                nc.scalar.copy(
-                    out=h[:].rearrange("p (c i) t -> p c t i", i=4), in_=scaled[:].rearrange("p t (c i) -> p c t i", i=4)
-                )
+                share = CHUNK // (2 if unit == (1, 0) else 1)
+                for first in range(0, CHUNK, share):
+                    nc.scalar.copy(
+                        out=h[:, first : first + share, :].rearrange("p (c i) t -> p c t i", i=4),
+                        in_=scaled[:, :, first : first + share].rearrange("p t (c i) -> p c t i", i=4),
+                    )
             return h
 
         def quantize_h(unit, h):
@@ -355,20 +371,26 @@ def tile_list_msg_tanh_res_bias_kernel(
                 at_y = None if behind is None else SLOT * UNITS.index(behind) + KB * n
                 send(bank[:, CHUNK * n : CHUNK * (n + 1)], chunk, c, at_y)
 
-        fetch_words(0, 2)
+        gather_words(0, 2)
+        part_words(0, TARGET)
         quantize_wt(0, 0)
+        part_words(0, SOURCE)
         reorder_ws_scales()
         reorder_ws_words(0)
         quantize_wt(1, 0)
-        fetch_words(2)
+        gather_words(2)
+        part_words(2, TARGET)
+        part_words(2, SOURCE)
         quantize_wt(0, 1)
         reorder_ws_words(1)
         quantize_wt(1, 1)
         for unit in ((0, 0), (0, 1), (1, 0)):
             first_product(unit)
             make_tanh(unit)
-        fetch_words(3)
+        gather_words(3)
+        part_words(3, TARGET)
         make_h((0, 0), (0, 1))
+        part_words(3, SOURCE)
 
         last = CHUNKS - 1
         for chunk in range(last):

@@ -28,12 +28,17 @@ SOURCE, TARGET = 0, 1
 UNITS = [(0, 0), (1, 0), (0, 1), (1, 1), (2, 0), (2, 1), (3, 0), (3, 1)]
 ON_VECTOR = {(0, 1), (1, 1)}
 PASSES = (((TARGET, 0), (TARGET, 1), (SOURCE, 0), (SOURCE, 1)), ((TARGET, 0), (SOURCE, 0), (SOURCE, 1), (TARGET, 1)))
-ROUNDING = {(0, 0): ("scalar",), (1, 0): ("scalar",), (0, 1): ("scalar", "vector"), (1, 1): ("vector", "vector")}
+PIECES = {
+    (0, 0): ((512, "scalar"),),
+    (1, 0): ((512, "scalar"),),
+    (0, 1): ((256, "scalar"), (256, "vector")),
+    (1, 1): ((256, "vector"), (256, "vector")),
+}
 BY_EDGES = (0, 1)
 PAD = 4
 ROWS_AT = 96
 BANK = 2048
-BANKS = {(0, 0): (0, 1), (1, 0): (2, 3), (0, 1): (4, 5), (1, 1): (6, 4), (2, 0): (5, 6), (2, 1): (4, 0), (3, 0): (1, 2), (3, 1): (5, 4)}
+BANKS = {(0, 0): (0, 1), (1, 0): (2, 3), (0, 1): (4, 5), (1, 1): (6, 7), (2, 0): (4, 5), (2, 1): (0, 1), (3, 0): (4, 2), (3, 1): (5, 0)}
 
 KB = 1024
 SLOT = 4 * KB
@@ -91,16 +96,17 @@ def tile_list_msg_tanh_res_bias_kernel(
         wt_loaded = {}
         ws_loaded = {}
 
-        def load_wt(a, half, pieces=1, between=None):
-            width = PASS // pieces
-            for n in range(pieces):
-                at = at_wt(a, half) + 4 * PACK * width * n
-                loaded = placed.tile([P, PACK, width], F32, name="wt_loaded%d%d%d" % (a, half, n), align_bytes=64, offset=at)
-                rows = wt[PASS * a : PASS * (a + 1), PASS * half + width * n : PASS * half + width * (n + 1)]
+        def load_wt(a, half, between=None):
+            first = 0
+            for width, engine in PIECES[a, half]:
+                at = at_wt(a, half) + 4 * PACK * first
+                loaded = placed.tile([P, PACK, width], F32, name="wt_loaded%d%d_%d" % (a, half, first), align_bytes=64, offset=at)
+                rows = wt[PASS * a : PASS * (a + 1), PASS * half + first : PASS * half + first + width]
                 nc.sync.dma_start(out=loaded[:], in_=rows.rearrange("(p i) r -> p i r", i=PACK))
-                wt_loaded.setdefault((a, half), []).append(loaded)
-                if between and n == 0:
+                wt_loaded.setdefault((a, half), []).append((first, width, engine, loaded))
+                if between and first == 0:
                     between()
+                first = first + width
 
         def load_ws(half, pieces=1):
             words = ws_words.rearrange("a p r i -> p a (r i)")[:, :, PACK * PASS * half : PACK * PASS * (half + 1)]
@@ -134,10 +140,10 @@ def tile_list_msg_tanh_res_bias_kernel(
         nc.sync.dma_start(out=sm_t[:], in_=sm.rearrange("(g p t) -> p g t", g=2, t=PACK))
         lower_planes(0)
         load_ws(0)
-        load_wt(0, 1, 2, lambda: lower_planes(1))
+        load_wt(0, 1, lambda: lower_planes(1))
         load_ws(1)
         load_planes(wd4_s, wd4_scales)
-        load_wt(1, 1, 2)
+        load_wt(1, 1)
         nc.sync.dma_start(out=wd8_w[:].bitcast(I32), in_=wd8_words.rearrange("a p n i -> p a (n i)").bitcast(I32))
         nc.sync.dma_start(out=wd4_w[:].bitcast(I32), in_=wd4_words.rearrange("a p n -> p a n").bitcast(I32))
         load_planes(wd8_s, wd8_scales)
@@ -202,15 +208,11 @@ def tile_list_msg_tanh_res_bias_kernel(
 
         def quantize_wt(a, half):
             rounded = keep.tile([P, PACK, P, PACK], BF16, name="wt_bf16_%d%d" % (a, half), align_bytes=64)
-            copies = ROUNDING[a, half]
-            pieces = wt_loaded[a, half]
-            share = P // len(copies)
-            for n, engine in enumerate(copies):
-                piece = pieces[n][:] if len(pieces) > 1 else pieces[0][:, :, PACK * share * n : PACK * share * (n + 1)]
+            for first, width, engine, loaded in wt_loaded[a, half]:
                 round_copy = nc.vector.tensor_copy if engine == "vector" else nc.scalar.copy
                 round_copy(
-                    out=rounded[:, :, share * n : share * (n + 1), :].rearrange("p t m i -> p m i t"),
-                    in_=piece.rearrange("p i (m t) -> p m i t", t=PACK),
+                    out=rounded[:, :, first // PACK : (first + width) // PACK, :].rearrange("p t m i -> p m i t"),
+                    in_=loaded[:].rearrange("p i (m t) -> p m i t", t=PACK),
                 )
             words = keep.tile([P, PASS], U32, name="wt_w%d%d" % (a, half), align_bytes=64)
             plane = keep.tile([P, PASS], U8, name="wt_s%d%d" % (a, half), align_bytes=64)
@@ -236,7 +238,8 @@ def tile_list_msg_tanh_res_bias_kernel(
                 else:
                     first, width, outputs = 0, CHUNK, range(2 * part, 2 * part + 2)
                 edge = chunk * CHUNK + first
-                passes = [(lst, a, t) for lst, a in PASSES[half] for t in outputs]
+                order = PASSES[0] if (unit, part) == ((1, 1), 1) else PASSES[half]
+                passes = [(lst, a, t) for lst, a in order for t in outputs]
                 for n, (lst, a, t) in enumerate(passes):
                     cols = slice(P * t, P * (t + 1))
                     if lst == TARGET:
@@ -411,7 +414,7 @@ def tile_list_msg_tanh_res_bias_kernel(
                 make_h((chunk + 2, 0))
         send_tiles(last - 1, (2,), BANK * 7, (last, 1))
         for c in range(TILES - 1):
-            send_tiles(last, (c,), BANK * c)
+            send_tiles(last, (c,), BANK * (1, 2, 4)[c])
         bank = psum.tile([P, 2 * CHUNK], F32, name="b_last", offset=BANK * 6)
         for n, chunk in enumerate((last - 1, last)):
             second_product(bank[:, CHUNK * n : CHUNK * (n + 1)], chunk, TILES - 1)

@@ -22,6 +22,7 @@ PASS = P * PACK
 QUADS = 4
 CHUNK = 256
 CHUNKS = J // CHUNK
+EARLY = 3 * CHUNK
 TILES = N // P
 SOURCE, TARGET = 0, 1
 
@@ -75,11 +76,10 @@ def tile_list_msg_tanh_res_bias_kernel(
         wd8_s = wd_s_tile[:, 0 : 2 * N].rearrange("p (a n) -> p a n", a=2)
         wd4_s = wd_s_tile[:, 2 * N : 4 * N].rearrange("p (a n) -> p a n", a=2)
         picked_s = keep.tile([P, 2, J], U8, name="picked_s", align_bytes=64)
-        lowered = [
-            placed.tile([P, 2 * J], U8, name="lowered0", align_bytes=64, offset=AT_TAB_S),
-            keep.tile([P, 2 * J + PAD], U8, name="lowered1", align_bytes=64),
-        ]
-        v_s = [tile[:, 0 : 2 * J].rearrange("p (l j) -> p l j", l=2) for tile in lowered]
+        lowered = {
+            (0, 0): placed.tile([P, 2 * EARLY], U8, name="lowered00", align_bytes=64, offset=AT_TAB_S),
+            (1, 0): keep.tile([P, 2 * EARLY + PAD], U8, name="lowered10", align_bytes=64),
+        }
         windows = [keep.tile([P, T], F32, name="window%d" % c, align_bytes=64) for c in range(TILES)]
         sm_t = keep.tile([P, 2, PACK], F32, name="sm_t")
         b_t = keep.tile([P, TILES], F32, name="b_t")
@@ -88,12 +88,13 @@ def tile_list_msg_tanh_res_bias_kernel(
         wgo_first = keep.tile([P, CHUNK], F32, name="wgo_first")
         wgo_rest = keep.tile([P, J - CHUNK], F32, name="wgo_rest")
 
-        for planes in (ws_s_tile[:], tab_s[0:ROWS_AT, :], lowered[1][:]):
+        for planes in (ws_s_tile[:], tab_s[0:ROWS_AT, :], lowered[1, 0][:]):
             nc.vector.memset(planes.bitcast(I32), 0)
         for window in windows:
             nc.gpsimd.memset(window[:].bitcast(I32), 0)
 
         wt_loaded = {}
+        v_s = {}
         ws_loaded = {}
 
         def load_wt(a, half, between=None):
@@ -122,25 +123,31 @@ def tile_list_msg_tanh_res_bias_kernel(
                     out=planes[row:P:32, :, :].bitcast(I32), in_=scales[:, row:16:4, :].rearrange("a q n -> q a n").bitcast(I32)
                 )
 
-        def lower_planes(a):
+        def lower_planes(a, late):
+            first, width = (EARLY, J - EARLY) if late else (0, EARLY)
+            if late:
+                at = at_wt(0, 0) + 6 * KB + KB * a
+                lowered[a, late] = placed.tile([P, 2 * width], U8, name="lowered%d1" % a, align_bytes=64, offset=at)
+            planes = lowered[a, late][:, 0 : 2 * width].rearrange("p (l j) -> p l j", l=2)
+            v_s[a, late] = planes
             for row in range(4):
-                first = ROWS_AT + 16 * a + row
-                rows = picked_s[first : first + 13 : 4, :, :]
-                nc.sync.dma_start(out=v_s[a][row:P:32, :, :].bitcast(I32), in_=rows.bitcast(I32))
+                start = ROWS_AT + 16 * a + row
+                rows = picked_s[start : start + 13 : 4, :, first : first + width]
+                nc.sync.dma_start(out=planes[row:P:32, :, :].bitcast(I32), in_=rows.bitcast(I32))
 
         nc.sync.dma_start(out=tab_s[ROWS_AT:P, 0:T].bitcast(I32), in_=tab_scales.rearrange("a q t -> (a q) t").bitcast(I32))
         nc.sync.dma_start(lists[TARGET][:], offs2)
         nc.sync.dma_start(lists[SOURCE][:], offs)
-        nc.sync.dma_start(out=tab_w[:], in_=tab_words[0].rearrange("p t d -> p (t d)").bitcast(I32))
         for lst in (TARGET, SOURCE):
             nc.vector.tensor_copy(picked_s[:, lst, :], tab_s[:, 0:T].indirect(lists[lst][:]))
         load_wt(0, 0)
+        nc.sync.dma_start(out=tab_w[:], in_=tab_words[0].rearrange("p t d -> p (t d)").bitcast(I32))
         load_planes(ws_s_loaded, ws_scales)
         load_wt(1, 0)
         nc.sync.dma_start(out=sm_t[:], in_=sm.rearrange("(g p t) -> p g t", g=2, t=PACK))
-        lower_planes(0)
+        lower_planes(0, 0)
         load_ws(0)
-        load_wt(0, 1, lambda: lower_planes(1))
+        load_wt(0, 1, lambda: lower_planes(1, 0))
         load_ws(1)
         load_planes(wd4_s, wd4_scales)
         load_wt(1, 1)
@@ -150,7 +157,6 @@ def tile_list_msg_tanh_res_bias_kernel(
         with nc.allow_non_contiguous_dma(reason="one bias value to a partition"):
             nc.sync.dma_start(out=b_t[:], in_=b.rearrange("(c p) -> p c", p=P))
         nc.sync.dma_start(out=wgo_first[:], in_=wgo[:, 0:CHUNK])
-        nc.sync.dma_start(out=wgo_rest[:], in_=wgo[:, CHUNK:J])
 
         v_w = {}
 
@@ -237,7 +243,8 @@ def tile_list_msg_tanh_res_bias_kernel(
                     first, width, outputs = part * P, P, range(PACK)
                 else:
                     first, width, outputs = 0, CHUNK, range(2 * part, 2 * part + 2)
-                edge = chunk * CHUNK + first
+                late = chunk * CHUNK // EARLY
+                edge = chunk * CHUNK - late * EARLY + first
                 order = PASSES[0] if (unit, part) == ((1, 1), 1) else PASSES[half]
                 passes = [(lst, a, t) for lst, a in order for t in outputs]
                 for n, (lst, a, t) in enumerate(passes):
@@ -252,7 +259,7 @@ def tile_list_msg_tanh_res_bias_kernel(
                         lhsT=words.bitcast(FP8X4),
                         lhsT_scale=plane,
                         rhs=v_w[lst, chunk][:, a, 2 * first : 2 * (first + width)].bitcast(FP4X4),
-                        rhs_scale=v_s[a][:, lst, edge : edge + width],
+                        rhs_scale=v_s[a, late][:, lst, edge : edge + width],
                         start=(n == 0),
                         stop=(n == len(passes) - 1),
                     )
@@ -379,6 +386,9 @@ def tile_list_msg_tanh_res_bias_kernel(
         quantize_wt(0, 0)
         part_words(0, SOURCE)
         reorder_ws_scales()
+        nc.sync.dma_start(out=wgo_rest[:], in_=wgo[:, CHUNK:J])
+        for a in range(2):
+            lower_planes(a, 1)
         reorder_ws_words(0)
         quantize_wt(1, 0)
         gather_words(2)

from contextlib import ExitStack

import concourse.mybir as mybir

K, R, N, T, J = 1024, 1024, 512, 2048, 1024
FLOPS = 2 * (2 * K * R * J + 2 * R * N * J)

F32 = mybir.dt.float32
BF16 = mybir.dt.bfloat16
I32 = mybir.dt.int32
U32 = mybir.dt.uint32
U16 = mybir.dt.uint16
U8 = mybir.dt.uint8
FP8X4 = mybir.dt.float8_e4m3fn_x4
FP4X4 = mybir.dt.float4_e2m1fn_x4
ACT = mybir.ActivationFunctionType
MULT = mybir.AluOpType.mult

P = 128
PACK = 4
PASS = P * PACK
QUADS = 4
CHUNK = 256
CHUNKS = J // CHUNK
EARLY = 3 * CHUNK
TILES = N // P
SOURCE, TARGET = 0, 1

UNITS = [(0, 0), (1, 0), (0, 1), (1, 1), (2, 0), (2, 1), (3, 0), (3, 1)]
ON_VECTOR = {(0, 1), (1, 1)}
PASSES = (((TARGET, 0), (TARGET, 1), (SOURCE, 0), (SOURCE, 1)), ((TARGET, 0), (SOURCE, 0), (SOURCE, 1), (TARGET, 1)))
PIECES = {
    (0, 0): ((512, "scalar"),),
    (1, 0): ((512, "scalar"),),
    (0, 1): ((256, "scalar"), (256, "vector")),
    (1, 1): ((256, "vector"), (256, "vector")),
}
BY_EDGES = (0, 1)
PAD = 4
ROWS_AT = 96
BANK = 2048
BANKS = {(0, 0): (0, 1), (1, 0): (2, 3), (0, 1): (4, 5), (1, 1): (6, 7), (2, 0): (4, 5), (2, 1): (0, 1), (3, 0): (4, 2), (3, 1): (5, 0)}

KB = 1024
SLOT = 4 * KB
AT_WT = SLOT * len(UNITS)
AT_TAB_S = AT_WT + 32 * KB
AT_WS_S = AT_TAB_S + 2 * KB + 64
AT_FIRST = AT_WS_S + 2 * KB + 64


def at_wt(a, half):
    return AT_WT + 8 * KB * (2 * half + a)


LATE_PARTINGS = {(0, SOURCE): at_wt(0, 0) + 4 * KB, (3, SOURCE): AT_FIRST + 4 * KB}
LATE_GATHERS = {2: at_wt(1, 0), 3: at_wt(1, 1) + 4 * KB}


def tile_list_msg_tanh_res_bias_kernel(
    tc, tab_words, tab_scales, ws_words, ws_scales, wt, sm, wd4_words, wd4_scales, wd8_words, wd8_scales, b, wgo, offs, offs2, out
):
    nc = tc.nc
    with ExitStack() as ctx:
        keep = ctx.enter_context(tc.tile_pool(name="keep", bufs=1))
        ring = ctx.enter_context(tc.tile_pool(name="ring", bufs=3))
        placed = ctx.enter_context(tc.tile_pool(name="placed", bufs=1))
        psum = ctx.enter_context(tc.psum_pool(name="psum", bufs=1))

        lists = [keep.tile([P, J // 16], U16, name="list_source"), keep.tile([P, J // 16], U16, name="list_target")]
        tab_w = keep.tile([P, T], I32, name="tab_w", align_bytes=64)
        tab_s = placed.tile([P, T + PAD], U8, name="tab_s", align_bytes=64, offset=AT_TAB_S)
        ws_s_tile = placed.tile([P, 2 * R + PAD], U8, name="ws_s_tile", align_bytes=64, offset=AT_WS_S)
        ws_s_loaded = ws_s_tile[:, 0 : 2 * R].rearrange("p (a r) -> p a r", a=2)
        wd_s_tile = placed.tile([P, 4 * N], U8, name="wd_s_tile", align_bytes=64, offset=AT_WS_S)
        wd8_s = wd_s_tile[:, 0 : 2 * N].rearrange("p (a n) -> p a n", a=2)
        wd4_s = wd_s_tile[:, 2 * N : 4 * N].rearrange("p (a n) -> p a n", a=2)
        picked_s = keep.tile([P, 2, J], U8, name="picked_s", align_bytes=64)
        lowered = {
            (0, 0): placed.tile([P, 2 * EARLY], U8, name="lowered00", align_bytes=64, offset=AT_TAB_S),
            (1, 0): keep.tile([P, 2 * EARLY + PAD], U8, name="lowered10", align_bytes=64),
        }
        windows = [keep.tile([P, T], F32, name="window%d" % c, align_bytes=64) for c in range(TILES)]
        sm_t = keep.tile([P, 2, PACK], F32, name="sm_t")
        b_t = keep.tile([P, TILES], F32, name="b_t")
        wd8_w = keep.tile([P, 2, PACK * N], U8, name="wd8_w", align_bytes=64)
        wd4_w = keep.tile([P, 2, 2 * N], U8, name="wd4_w", align_bytes=64)
        wgo_first = keep.tile([P, CHUNK], F32, name="wgo_first")
        wgo_rest = keep.tile([P, J - CHUNK], F32, name="wgo_rest")

        for planes in (ws_s_tile[:], tab_s[0:ROWS_AT, :], lowered[1, 0][:]):
            nc.vector.memset(planes.bitcast(I32), 0)
        for window in windows:
            nc.gpsimd.memset(window[:].bitcast(I32), 0)

        wt_loaded = {}
        v_s = {}
        ws_loaded = {}

        def load_wt(a, half, between=None):
            first = 0
            for width, engine in PIECES[a, half]:
                at = at_wt(a, half) + 4 * PACK * first
                loaded = placed.tile([P, PACK, width], F32, name="wt_loaded%d%d_%d" % (a, half, first), align_bytes=64, offset=at)
                rows = wt[PASS * a : PASS * (a + 1), PASS * half + first : PASS * half + first + width]
                nc.sync.dma_start(out=loaded[:], in_=rows.rearrange("(p i) r -> p i r", i=PACK))
                wt_loaded.setdefault((a, half), []).append((first, width, engine, loaded))
                if between and first == 0:
                    between()
                first = first + width

        def load_ws(half, pieces=1):
            words = ws_words.rearrange("a p r i -> p a (r i)")[:, :, PACK * PASS * half : PACK * PASS * (half + 1)]
            count = 2 // pieces
            for n in range(pieces):
                loaded = keep.tile([P, count, PASS], I32, name="ws_loaded%d%d" % (half, n), align_bytes=64)
                nc.sync.dma_start(out=loaded[:], in_=words[:, count * n : count * (n + 1), :].bitcast(I32))
                ws_loaded.setdefault(half, []).append(loaded)

        def load_planes(planes, scales):
            for row in range(4):
                nc.sync.dma_start(
                    out=planes[row:P:32, :, :].bitcast(I32), in_=scales[:, row:16:4, :].rearrange("a q n -> q a n").bitcast(I32)
                )

        def lower_planes(a, late):
            first, width = (EARLY, J - EARLY) if late else (0, EARLY)
            if late:
                at = at_wt(0, 0) + 6 * KB + KB * a
                lowered[a, late] = placed.tile([P, 2 * width], U8, name="lowered%d1" % a, align_bytes=64, offset=at)
            planes = lowered[a, late][:, 0 : 2 * width].rearrange("p (l j) -> p l j", l=2)
            v_s[a, late] = planes
            for row in range(4):
                start = ROWS_AT + 16 * a + row
                rows = picked_s[start : start + 13 : 4, :, first : first + width]
                nc.sync.dma_start(out=planes[row:P:32, :, :].bitcast(I32), in_=rows.bitcast(I32))

        nc.sync.dma_start(out=tab_s[ROWS_AT:P, 0:T].bitcast(I32), in_=tab_scales.rearrange("a q t -> (a q) t").bitcast(I32))
        nc.sync.dma_start(lists[TARGET][:], offs2)
        nc.sync.dma_start(lists[SOURCE][:], offs)
        for lst in (TARGET, SOURCE):
            nc.vector.tensor_copy(picked_s[:, lst, :], tab_s[:, 0:T].indirect(lists[lst][:]))
        load_wt(0, 0)
        nc.sync.dma_start(out=tab_w[:], in_=tab_words[0].rearrange("p t d -> p (t d)").bitcast(I32))
        load_planes(ws_s_loaded, ws_scales)
        load_wt(1, 0)
        nc.sync.dma_start(out=sm_t[:], in_=sm.rearrange("(g p t) -> p g t", g=2, t=PACK))
        lower_planes(0, 0)
        load_ws(0)
        load_wt(0, 1, lambda: lower_planes(1, 0))
        load_ws(1)
        load_planes(wd4_s, wd4_scales)
        load_wt(1, 1)
        nc.sync.dma_start(out=wd8_w[:].bitcast(I32), in_=wd8_words.rearrange("a p n i -> p a (n i)").bitcast(I32))
        nc.sync.dma_start(out=wd4_w[:].bitcast(I32), in_=wd4_words.rearrange("a p n -> p a n").bitcast(I32))
        load_planes(wd8_s, wd8_scales)
        with nc.allow_non_contiguous_dma(reason="one bias value to a partition"):
            nc.sync.dma_start(out=b_t[:], in_=b.rearrange("(c p) -> p c", p=P))
        nc.sync.dma_start(out=wgo_first[:], in_=wgo[:, 0:CHUNK])

        v_w = {}

        def entries(lst, first, count=1):
            return lists[lst][:, first * CHUNK // 16 : (first + count) * CHUNK // 16]

        picked = {}

        def gather_words(chunk, count=1):
            for lst in (TARGET, SOURCE):
                name = "picked_w%d%d" % (chunk, lst)
                if chunk in LATE_GATHERS:
                    words = placed.tile([P, CHUNK], U32, name=name, align_bytes=64, offset=LATE_GATHERS[chunk] + KB * lst)
                else:
                    words = keep.tile([P, count * CHUNK], U32, name=name)
                nc.vector.tensor_copy(words[:], tab_w[:].bitcast(U32).indirect(entries(lst, chunk, count)))
                picked[chunk, lst] = words

        def part_words(chunk, lst):
            width = picked[chunk, lst].shape[1]
            name = "v_w%d%d" % (chunk, lst)
            if (chunk, lst) in LATE_PARTINGS:
                parted = placed.tile([P, 2, 2 * width], U8, name=name, align_bytes=64, offset=LATE_PARTINGS[chunk, lst])
            else:
                parted = keep.tile([P, 2, 2 * width], U8, name=name, align_bytes=64)
            nc.vector.tensor_copy(
                out=parted[:].bitcast(U16).rearrange("p d (e n) -> p e d n", e=2),
                in_=picked[chunk, lst][:].bitcast(U16).rearrange("p (e n d) -> p e d n", e=2, d=2),
            )
            for n in range(width // CHUNK):
                v_w[lst, chunk + n] = parted[:, :, 2 * CHUNK * n : 2 * CHUNK * (n + 1)]

        wt_w = {}
        wt_s = {}
        ws_w = {}
        ws_s = placed.tile([P, 2, R], U8, name="ws_s", align_bytes=64, offset=at_wt(0, 0))

        def reorder_ws_scales():
            nc.vector.tensor_copy(
                out=ws_s[:].rearrange("p a (g t mq mm) -> p (a g) mq t mm", g=2, t=PACK, mm=16),
                in_=ws_s_loaded.rearrange("p a (g mq mm t) -> p (a g) mq t mm", g=2, t=PACK, mm=16),
            )

        def reorder_ws_words(half):
            move = nc.scalar.copy if half == 0 else nc.vector.tensor_copy
            for n, loaded in enumerate(ws_loaded[half]):
                count = loaded.shape[1]
                words = keep.tile([P, count, PASS], U32, name="ws_w%d%d" % (half, n), align_bytes=64)
                move(
                    out=words[:].rearrange("p a (t m) -> p a m t", t=PACK),
                    in_=loaded[:].bitcast(U32).rearrange("p a (m t) -> p a m t", t=PACK),
                )
                for a in range(count):
                    ws_w[half, count * n + a] = words[:, a, :]

        def quantize_wt(a, half):
            rounded = keep.tile([P, PACK, P, PACK], BF16, name="wt_bf16_%d%d" % (a, half), align_bytes=64)
            for first, width, engine, loaded in wt_loaded[a, half]:
                round_copy = nc.vector.tensor_copy if engine == "vector" else nc.scalar.copy
                round_copy(
                    out=rounded[:, :, first // PACK : (first + width) // PACK, :].rearrange("p t m i -> p m i t"),
                    in_=loaded[:].rearrange("p i (m t) -> p m i t", t=PACK),
                )
            words = keep.tile([P, PASS], U32, name="wt_w%d%d" % (a, half), align_bytes=64)
            plane = keep.tile([P, PASS], U8, name="wt_s%d%d" % (a, half), align_bytes=64)
            nc.vector.quantize_mx(out=words[:].bitcast(FP8X4), scales=plane[:], in_=rounded[:].rearrange("p t m i -> p (t m i)"))
            wt_w[a, half] = words
            wt_s[a, half] = plane

        sums = {}
        tanh = {}
        h_w = {}
        h_s = {}

        def bank_of(unit, part):
            return BANK * BANKS[unit][part]

        def first_product(unit):
            chunk, half = unit
            for part in range(2):
                bank = psum.tile([P, PASS], F32, name="a%d%d%d" % (chunk, half, part), offset=bank_of(unit, part))
                sums[unit, part] = bank
                if unit == BY_EDGES:
                    first, width, outputs = part * P, P, range(PACK)
                else:
                    first, width, outputs = 0, CHUNK, range(2 * part, 2 * part + 2)
                late = chunk * CHUNK // EARLY
                edge = chunk * CHUNK - late * EARLY + first
                order = PASSES[0] if (unit, part) == ((1, 1), 1) else PASSES[half]
                passes = [(lst, a, t) for lst, a in order for t in outputs]
                for n, (lst, a, t) in enumerate(passes):
                    cols = slice(P * t, P * (t + 1))
                    if lst == TARGET:
                        words, plane = wt_w[a, half][:, cols], wt_s[a, half][:, cols]
                    else:
                        words, plane = ws_w[half, a][:, cols], ws_s[:, a, PASS * half + P * t : PASS * half + P * (t + 1)]
                    at = width * (t - outputs[0])
                    nc.tensor.matmul_mx(
                        out=bank[:, at : at + width],
                        lhsT=words.bitcast(FP8X4),
                        lhsT_scale=plane,
                        rhs=v_w[lst, chunk][:, a, 2 * first : 2 * (first + width)].bitcast(FP4X4),
                        rhs_scale=v_s[a, late][:, lst, edge : edge + width],
                        start=(n == 0),
                        stop=(n == len(passes) - 1),
                    )

        def make_tanh(unit):
            at = SLOT * UNITS.index(unit)
            if unit == BY_EDGES:
                tanh[unit] = [
                    placed.tile([P, PASS], F32, name="tanh01%d" % part, align_bytes=64, offset=AT_FIRST + 2 * KB * (part + 1))[:]
                    for part in range(2)
                ]
            else:
                tanh[unit] = placed.tile([P, 2, PASS], F32, name="tanh%d%d" % unit, align_bytes=64, offset=at)
            for part in range(2):
                bank = sums[unit, part]
                values = tanh[unit][part] if unit == BY_EDGES else tanh[unit][:, part, :]
                if unit in ON_VECTOR:
                    side = PACK if unit == BY_EDGES else 2
                    nc.scalar.activation(
                        out=values.rearrange("p (n t) -> p n t", t=side),
                        in_=bank[:].rearrange("p (t n) -> p n t", t=side),
                        func=ACT.Tanh,
                    )
                else:
                    nc.scalar.activation(out=values, in_=bank[:], func=ACT.Tanh)

        def make_h(*units):
            for unit, h in [(unit, scale_tanh(unit)) for unit in units]:
                quantize_h(unit, h)

        def scale_tanh(unit):
            half = unit[1]
            if unit == (1, 0):
                h = placed.tile([P, CHUNK, PACK], BF16, name="h10", align_bytes=64, offset=AT_FIRST + KB)
            else:
                h = ring.tile([P, CHUNK, PACK], BF16, name="h", tag="h", align_bytes=64)
            if unit == BY_EDGES:
                for part in range(2):
                    nc.vector.tensor_tensor(
                        out=h[:, P * part : P * (part + 1), :],
                        in0=tanh[unit][part].rearrange("p (n t) -> p n t", t=PACK),
                        in1=sm_t[:, half, :].unsqueeze(1).to_broadcast([P, P, PACK]),
                        op=MULT,
                    )
            elif unit in ON_VECTOR:
                nc.vector.tensor_tensor(
                    out=h[:].rearrange("p n (part t) -> p n part t", t=2),
                    in0=tanh[unit][:].rearrange("p part (n t) -> p n part t", t=2),
                    in1=sm_t[:, half, :].rearrange("p (part t) -> p part t", t=2).unsqueeze(1).to_broadcast([P, CHUNK, 2, 2]),
                    op=MULT,
                )
            else:
                scaled = ring.tile([P, PACK, CHUNK], BF16, name="scaled", tag="scaled", align_bytes=64)
                for t in range(PACK):
                    nc.scalar.activation(
                        out=scaled[:, t, :],
                        in_=tanh[unit][:, t // 2, CHUNK * (t % 2) : CHUNK * (t % 2 + 1)],
                        func=ACT.Copy,
                        scale=sm_t[:, half, t : t + 1],
                    )
                share = CHUNK // (2 if unit == (1, 0) else 1)
                for first in range(0, CHUNK, share):
                    nc.scalar.copy(
                        out=h[:, first : first + share, :].rearrange("p (c i) t -> p c t i", i=4),
                        in_=scaled[:, :, first : first + share].rearrange("p t (c i) -> p c t i", i=4),
                    )
            return h

        def quantize_h(unit, h):
            if unit == (0, 0):
                words = placed.tile([P, CHUNK], U32, name="h_w00", align_bytes=64, offset=AT_FIRST + 3 * KB)
            else:
                words = keep.tile([P, CHUNK], U32, name="h_w%d%d" % unit, align_bytes=64)
            plane = keep.tile([P, CHUNK], U8, name="h_s%d%d" % unit, align_bytes=64)
            nc.vector.quantize_mx(out=words[:].bitcast(FP8X4), scales=plane[:], in_=h[:].rearrange("p n t -> p (n t)"))
            h_w[unit] = words
            h_s[unit] = plane

        def second_product(bank, chunk, c):
            rows = slice(P * c, P * (c + 1))
            halves = (0, 1) if chunk in (0, CHUNKS - 1) else (1, 0)
            for half in halves:
                for words, plane, fmt in (
                    (wd8_w[:, half, PACK * P * c : PACK * P * (c + 1)], wd8_s, FP8X4),
                    (wd4_w[:, half, 2 * P * c : 2 * P * (c + 1)], wd4_s, FP4X4),
                ):
                    nc.tensor.matmul_mx(
                        out=bank,
                        lhsT=words.bitcast(fmt),
                        lhsT_scale=plane[:, half, rows],
                        rhs=h_w[chunk, half][:].bitcast(FP8X4),
                        rhs_scale=h_s[chunk, half][:],
                        start=(half == halves[0] and fmt is FP8X4),
                        stop=(half == halves[1] and fmt is FP4X4),
                    )

        def send(result, chunk, c, at_y):
            width = result.shape[1]
            name = "y%d%d" % (chunk, c)
            if at_y is None:
                y = keep.tile([P, width], F32, name=name)
            else:
                y = placed.tile([P, width], F32, name=name, align_bytes=64, offset=at_y)
            nc.scalar.activation(out=y[:], in_=result, func=ACT.Identity, bias=b_t[:, c : c + 1])
            weight = wgo_first[:] if chunk == 0 else wgo_rest[:, CHUNK * (chunk - 1) : CHUNK * (chunk - 1) + width]
            nc.vector.tensor_tensor(windows[c][:].indirect(entries(TARGET, chunk, width // CHUNK)), y[:], weight, MULT)
            if CHUNK * chunk + width == J:
                queues = (nc.sync, nc.scalar) if c == TILES - 1 else (nc.sync,)
                share = T // len(queues)
                for n, queue in enumerate(queues):
                    cols = slice(share * n, share * (n + 1))
                    queue.dma_start(out=out[P * c : P * (c + 1), cols], in_=windows[c][:, cols])

        def send_tiles(chunk, tiles, at_bank, behind=None):
            bank = psum.tile([P, CHUNK * len(tiles)], F32, name="b%d%d" % (chunk, tiles[0]), offset=at_bank)
            for n, c in enumerate(tiles):
                second_product(bank[:, CHUNK * n : CHUNK * (n + 1)], chunk, c)
            for n, c in enumerate(tiles):
                at_y = None if behind is None else SLOT * UNITS.index(behind) + KB * n
                send(bank[:, CHUNK * n : CHUNK * (n + 1)], chunk, c, at_y)

        gather_words(0, 2)
        part_words(0, TARGET)
        quantize_wt(0, 0)
        part_words(0, SOURCE)
        reorder_ws_scales()
        nc.sync.dma_start(out=wgo_rest[:], in_=wgo[:, CHUNK:J])
        for a in range(2):
            lower_planes(a, 1)
        reorder_ws_words(0)
        quantize_wt(1, 0)
        gather_words(2)
        part_words(2, TARGET)
        part_words(2, SOURCE)
        quantize_wt(0, 1)
        reorder_ws_words(1)
        quantize_wt(1, 1)
        for unit in ((0, 0), (0, 1), (1, 0)):
            first_product(unit)
            make_tanh(unit)
        gather_words(3)
        part_words(3, TARGET)
        make_h((0, 0), (0, 1))
        part_words(3, SOURCE)

        last = CHUNKS - 1
        for chunk in range(last):
            first_product((chunk + 1, 1))
            if chunk == 0:
                for c in range(2):
                    send_tiles(chunk, (c,), BANK * c)
            else:
                send_tiles(chunk, (0, 1), BANK * 3, (chunk + 1, 0))
            make_tanh((chunk + 1, 1))
            make_h((chunk + 1, 1))
            if chunk == 0:
                make_h((1, 0))
            if chunk + 1 < last:
                first_product((chunk + 2, 0))
                send_tiles(chunk, (2, 3), BANK * (2 if chunk == 0 else 7), (chunk + 1, 1))
                make_tanh((chunk + 2, 0))
                make_h((chunk + 2, 0))
        send_tiles(last - 1, (2,), BANK * 7, (last, 1))
        for c in range(TILES - 1):
            send_tiles(last, (c,), BANK * (1, 2, 4)[c])
        bank = psum.tile([P, 2 * CHUNK], F32, name="b_last", offset=BANK * 6)
        for n, chunk in enumerate((last - 1, last)):
            second_product(bank[:, CHUNK * n : CHUNK * (n + 1)], chunk, TILES - 1)
        send(bank[:], last - 1, TILES - 1, None)
